import numpy as np
import ml_dtypes


def mxq(x, axis, fmt="e4m3"):
    dtype, down = {"e4m3": (ml_dtypes.float8_e4m3fn, 7), "e5m2": (ml_dtypes.float8_e5m2, 14)}[fmt]
    v = np.moveaxis(np.asarray(x, np.float32).astype(ml_dtypes.bfloat16).astype(np.float64), axis, -1)
    blocks = v.reshape(v.shape[:-1] + (-1, 32))
    amax = np.abs(blocks).max(-1, keepdims=True)
    byte = np.maximum(np.where(amax > 0, np.frexp(amax)[1] - 1 + 127, 0) - down, 1)
    scale = np.exp2(byte - 127.0)
    codes = (blocks / scale).astype(np.float32).astype(dtype).astype(np.float64)
    return np.moveaxis((codes * scale).reshape(v.shape), -1, axis)


WIDE = False


def mx_kscale(k):
    if not WIDE:
        return np.ones(k)
    levels = np.array([10, -10, 5, -5, 0])
    if k % 512:
        return np.exp2(np.random.permutation(np.resize(levels, k // 32))).repeat(32)
    a = np.empty((k // 512, 16))
    for p in range(k // 512):
        a[p, :8] = np.random.permutation(np.resize(levels, 8))
        for g in range(8):
            far = levels[np.abs(levels - a[p, g]) >= 10]
            a[p, g + 8] = far[np.random.randint(len(far))]
    return np.exp2(a.ravel()).repeat(32)


def f64(x):
    return np.asarray(x).astype(np.float64)


def striped(idx):
    return np.tile(idx.reshape(-1, 16).T, (8, 1)).astype(np.uint16)


def unstriped(offs):
    return offs[:16].T.reshape(-1).astype(np.int64)


E2M1 = np.array([0.0, 0.5, 1.0, 1.5, 2.0, 3.0, 4.0, 6.0, -0.0, -0.5, -1.0, -1.5, -2.0, -3.0, -4.0, -6.0])


def pack_weight(w, fmt):
    k, n = w.shape
    w = f64(np.asarray(w, np.float32).astype(ml_dtypes.bfloat16)).reshape(k // 32, 32, n)
    amax = np.abs(w).max(1)
    if fmt == "e4m3":
        byte = np.frexp(amax)[1] - 1 + 127 - 7
    else:
        mant, ex = np.frexp(amax / 6.0)
        byte = np.where(mant > 0.5, ex, ex - 1) + 127
    byte = np.clip(np.where(amax > 0, byte, 1), 1, 254)
    scaled = (w * np.exp2(127.0 - byte)[:, None, :]).reshape(k, n).astype(np.float32)
    by_word = np.ascontiguousarray(scaled.reshape(k // 512, 128, 4, n).transpose(0, 1, 3, 2))
    if fmt == "e4m3":
        words = by_word.astype(ml_dtypes.float8_e4m3fn).view(np.uint8)
    else:
        c = by_word.astype(ml_dtypes.float4_e2m1fn).view(np.uint8) & 0xF
        words = (c[..., 0::2] | (c[..., 1::2] << 4)).reshape(k // 512, 128, 2 * n)
    return np.ascontiguousarray(words), np.ascontiguousarray(byte.astype(np.uint8).reshape(k // 512, 16, n))


def unpack_weight(words, scales, fmt):
    g, _, n = scales.shape
    words = np.ascontiguousarray(words).reshape(g, 128, n, -1)
    if fmt == "e4m3":
        vals = words.view(ml_dtypes.float8_e4m3fn).astype(np.float64)
    else:
        nib = np.empty((g, 128, n, 4), np.uint8)
        nib[..., 0::2] = words & 0xF
        nib[..., 1::2] = words >> 4
        vals = E2M1[nib]
    vals = vals * np.repeat(np.exp2(scales.astype(np.float64) - 127.0), 8, axis=1)[..., None]
    return vals.transpose(0, 1, 3, 2).reshape(g * 512, n)


def relu(v):
    return np.maximum(v, 0.0)


K, T, E, C, H, N = 1536, 640, 5, 256, 512, 256


def by_expert(wq, xq):
    return np.concatenate([wq[e].T @ xq[:, e * C:(e + 1) * C] for e in range(E)], axis=1)


def setup_inputs():
    n = np.random.standard_normal
    s = mx_kscale(K)[:, None]
    u = mx_kscale(H)
    first = np.random.permutation(np.repeat(np.arange(E), T // E))
    second = (first + 1 + np.random.permutation(np.repeat(np.arange(E - 1), -(-T // (E - 1)))[:T])) % E
    while np.bincount(second, minlength=E).max() != T // E:
        load = np.bincount(second, minlength=E); hi, lo = int(load.argmax()), int(load.argmin())
        t = np.flatnonzero((second == hi) & (first != lo))[0]; second[t] = lo
    slot_token = np.empty(E * C, np.int64); pos = np.empty((2, T), np.int64); fill = np.zeros(E, np.int64)
    place = np.stack([np.random.permutation(C) for _ in range(E)])
    for r, deal in enumerate((first, second)):
        for t in np.random.permutation(T):
            e = deal[t]; j = e * C + place[e, fill[e]]; fill[e] += 1; slot_token[j] = t; pos[r, t] = j
    g = np.random.uniform(0.2, 0.8, T)
    w1 = [pack_weight(m, "e2m1") for m in n((E, K, H)) / np.sqrt(K) / s[None] * u[None, None, :]]
    w2 = [pack_weight(m, "e2m1") for m in n((E, H, N)) / np.sqrt(H) / u[None, :, None]]
    w_slot = np.empty(E * C); w_slot[pos[0]] = g; w_slot[pos[1]] = 1.0 - g
    return {
        "xT": (n((K, T)) * s).astype(np.float32),
        "w1_words": np.stack([m[0] for m in w1]),
        "w1_scales": np.stack([m[1] for m in w1]),
        "w2_words": np.stack([m[0] for m in w2]),
        "w2_scales": np.stack([m[1] for m in w2]),
        "gate": np.tile(w_slot, (K, 1)).astype(np.float32),
        "offs": striped(slot_token),
        "pos1": striped(pos[0]),
        "pos2": striped(pos[1]),
    }


def reference(xT, w1_words, w1_scales, w2_words, w2_scales, gate, offs, pos1, pos2):
    idx = unstriped(offs)
    w1 = np.stack([unpack_weight(w1_words[e], w1_scales[e], "e2m1") for e in range(E)])
    w2 = np.stack([unpack_weight(w2_words[e], w2_scales[e], "e2m1") for e in range(E)])
    xq = mxq(f64(gate) * f64(xT)[:, idx], 0, "e4m3")
    h = relu(by_expert(w1, xq))
    y = by_expert(w2, mxq(h, 0, "e4m3"))
    return y[:, unstriped(pos1)] + y[:, unstriped(pos2)]

@@ -1,0 +1,253 @@
+from contextlib import ExitStack
+
+import concourse.mybir as mybir
+from concourse.masks import make_identity
+
+K, T, E, C, H, N = 1536, 640, 5, 256, 512, 256
+S = E * C
+P = 128
+PACK = 4
+K_PASS = P * PACK
+PASSES = K // K_PASS
+OFFS_COL = 16
+
+FLOPS = 2 * S * (K * H + H * N)
+BYTES = 4 * K * T + E * (K * H + H * N) // 2 + E * (K * H + H * N) // 32 + 4 * S + 2 * P * (S + 2 * T) // 16 + 4 * N * T
+
+F32 = mybir.dt.float32
+BF16 = mybir.dt.bfloat16
+I32 = mybir.dt.int32
+U32 = mybir.dt.uint32
+U16 = mybir.dt.uint16
+U8 = mybir.dt.uint8
+FP8X4 = mybir.dt.float8_e4m3fn_x4
+FP4X4 = mybir.dt.float4_e2m1fn_x4
+MULT = mybir.AluOpType.mult
+ADD = mybir.AluOpType.add
+COPY = mybir.ActivationFunctionType.Copy
+RELU = mybir.ActivationFunctionType.Relu
+
+WINDOW = 800
+GATE_PIECES = [(0, 256), (256, 512), (768, 512)]
+PROGRAM = [
+    ("G", 0, 768, 0, 256),
+    ("Q", 0, 768, 0),
+    ("G", 0, 768, 1),
+    ("G", 0, 768, 2),
+    ("Q", 0, 768, 1),
+    ("Q", 0, 768, 2),
+    ("M", 0, 256, 0, 3),
+    ("M", 256, 256, 0, 3),
+    ("M", 512, 256, 0, 3),
+    ("R", 0, False),
+    ("R", 128, False),
+    ("R", 512, False),
+    ("R", 384, False),
+    ("G", 768, 512, 0),
+    ("R", 256, False),
+    ("G", 768, 512, 1),
+    ("R", 640, False),
+    ("T", 256, 256, False),
+    ("H", 256, 256),
+    ("T", 0, 256, False),
+    ("Q", 768, 512, 0),
+    ("Q", 768, 512, 1),
+    ("G", 768, 256, 2),
+    ("G", 1024, 128, 2),
+    ("H", 0, 256),
+    ("Q", 768, 256, 2),
+    ("G", 1152, 128, 2),
+    ("M", 768, 256, 0, 3),
+    ("M", 1152, 128, 0, 2),
+    ("M", 1024, 128, 0, 2),
+    ("Q", 1024, 128, 2),
+    ("T", 512, 256, False),
+    ("Q", 1152, 128, 2),
+    ("R", 768, True),
+    ("R", 896, True),
+    ("Y", 0, 256, False),
+    ("M", 1024, 128, 2, 3),
+    ("M", 1152, 128, 2, 3),
+    ("R", 1024, False),
+    ("R", 1152, False),
+    ("T", 768, 256, True),
+    ("T", 1024, 128, True),
+    ("Y", 256, 256, False),
+    ("H", 512, 256),
+    ("T", 1152, 128, True),
+    ("H", 1024, 128),
+    ("H", 768, 256),
+    ("Y", 1024, 128, False),
+    ("H", 1152, 128),
+    ("Y", 512, 256, False),
+    ("Y", 768, 256, False),
+    ("Y", 1152, 128, True),
+]
+
+
+def tile_moe_pre_mlp_relu_kernel(
+    tc, xT, w1_words, w1_scales, w2_words, w2_scales, gate, offs, pos1, pos2, out
+):
+    nc = tc.nc
+    with ExitStack() as ctx:
+        keep = ctx.enter_context(tc.tile_pool(name="keep", bufs=1))
+        stage = ctx.enter_context(tc.tile_pool(name="stage", bufs=2))
+        gpool = ctx.enter_context(tc.tile_pool(name="gpool", bufs=8))
+        hpool = ctx.enter_context(tc.tile_pool(name="hpool", bufs=10))
+        psum_a = ctx.enter_context(tc.psum_pool(name="psum_a", bufs=4))
+        psum_b = ctx.enter_context(tc.psum_pool(name="psum_b", bufs=2))
+
+        slot_tokens = keep.tile([P, S // OFFS_COL], U16, name="slot_tokens")
+        first_slots = keep.tile([P, T // OFFS_COL], U16, name="first_slots")
+        second_slots = keep.tile([P, T // OFFS_COL], U16, name="second_slots")
+        planes = [[keep.tile([P, WINDOW], F32, name="plane_%d_%d" % (g, j), align_bytes=64) for j in range(PACK)] for g in range(PASSES)]
+        gates = keep.tile([P, S], F32, name="gates", align_bytes=64)
+        x_codes = [keep.tile([P, S], U32, name="x_codes_%d" % g, align_bytes=64) for g in range(PASSES)]
+        x_plane = [keep.tile([P, S], U8, name="x_plane_%d" % g, align_bytes=64) for g in range(PASSES)]
+        w1_codes = [keep.tile([P, PASSES, 2 * H], U8, name="w1_codes_%d" % e, align_bytes=64) for e in range(E)]
+        w1_plane = keep.tile([P, E * PASSES, H], U8, name="w1_plane", align_bytes=64)
+        w2_codes = keep.tile([P, E, 2 * N], U8, name="w2_codes", align_bytes=64)
+        w2_plane = keep.tile([P, E, N], U8, name="w2_plane", align_bytes=64)
+        identity = keep.tile([P, P], F32, name="identity", align_bytes=64)
+        y_all = keep.tile([P, N // P, S], F32, name="y_all", align_bytes=64)
+        y_rows = [y_all[:, b, :] for b in range(N // P)]
+
+        nc.vector.memset(w1_plane[:].rearrange("p a b -> p (a b)").bitcast(I32), 0)
+        nc.vector.memset(w2_plane[:].rearrange("p a b -> p (a b)").bitcast(I32), 0)
+        for g in range(PASSES):
+            for j in range(PACK):
+                nc.gpsimd.memset(planes[g][j][:, T:WINDOW], 0.0)
+        make_identity(nc, identity[:])
+
+        x_rows = xT.rearrange("(g p j) t -> g j p t", p=P, j=PACK)
+        nc.sync.dma_start(slot_tokens[:], offs)
+        nc.sync.dma_start(planes[0][0][:, 0:T], x_rows[0, 0])
+        for s0, width in GATE_PIECES[:-1]:
+            nc.sync.dma_start(gates[:, s0 : s0 + width], gate[0:P, s0 : s0 + width])
+        for g in range(PASSES):
+            for j in range(PACK):
+                if g + j > 0:
+                    nc.sync.dma_start(planes[g][j][:, 0:T], x_rows[g, j])
+        s0, width = GATE_PIECES[-1]
+        nc.sync.dma_start(gates[:, s0 : s0 + width], gate[0:P, s0 : s0 + width])
+        w1_rows = w1_scales.rearrange("e s q i -> q (e s) i").bitcast(I32)
+        w2_rows = w2_scales.rearrange("e s q i -> q (e s) i").bitcast(I32)
+        for quad in range(4):
+            nc.sync.dma_start(w1_plane[32 * quad : 32 * quad + 4].bitcast(I32), w1_rows[4 * quad : 4 * quad + 4])
+        for quad in range(4):
+            nc.sync.dma_start(w2_plane[32 * quad : 32 * quad + 4].bitcast(I32), w2_rows[4 * quad : 4 * quad + 4])
+        for e in range(E):
+            nc.sync.dma_start(w1_codes[e][:].bitcast(I32), w1_words[e].rearrange("s p b -> p s b").bitcast(I32))
+            if e == 1:
+                nc.sync.dma_start(w2_codes[:].bitcast(I32), w2_words.rearrange("e s p b -> p (e s) b").bitcast(I32))
+        nc.sync.dma_start(first_slots[:], pos1)
+        nc.sync.dma_start(second_slots[:], pos2)
+
+        def pieces(s0, width):
+            return [(s0, width)] if width in (128, 256, 512, 1024) else [(s0, 512 if width > 512 else 256), (s0 + (512 if width > 512 else 256), width - (512 if width > 512 else 256))]
+
+        x_grouped = {}
+        a_banks = {}
+        h_rows = {}
+        h_grouped = {}
+        y_banks = {}
+
+        def gather_x(s0, width, g, head=0):
+            gathered = stage.tile([P, PACK, width], F32, name="gathered", align_bytes=64)
+            for j in range(PACK):
+                cuts = [0, head, width] if head and j == 0 else [0, width]
+                for c0, c1 in zip(cuts, cuts[1:]):
+                    offsets = slot_tokens[:, (s0 + c0) // OFFS_COL : (s0 + c1) // OFFS_COL]
+                    nc.vector.tensor_tensor(gathered[:, j, c0:c1], planes[g][j][:].indirect(offsets), gates[:, s0 + c0 : s0 + c1], MULT)
+            for p0, w in pieces(s0, width):
+                grouped = gpool.tile([P, w, PACK], BF16, name="x_grouped", align_bytes=64)
+                nc.scalar.activation(
+                    grouped[:].rearrange("p (c i) j -> p c j i", i=4),
+                    gathered[:, :, p0 - s0 : p0 - s0 + w].rearrange("p j (c i) -> p c j i", i=4),
+                    COPY,
+                )
+                x_grouped[p0, g] = grouped
+
+        def quantize_x(s0, width, g):
+            for p0, w in pieces(s0, width):
+                nc.vector.quantize_mx(
+                    out=x_codes[g][:, p0 : p0 + w].bitcast(FP8X4),
+                    scales=x_plane[g][:, p0 : p0 + w],
+                    in_=x_grouped[p0, g][:].rearrange("p c j -> p (c j)"),
+                )
+
+        def first_layer(s0, width, g0, g1):
+            for b0 in range(s0, s0 + width, P):
+                e = b0 // C
+                if g0 == 0:
+                    a_banks[b0] = psum_a.tile([P, H], F32, name="a_bank")
+                for g in range(g0, g1):
+                    nc.tensor.matmul_mx(
+                        out=a_banks[b0][:],
+                        lhsT=x_codes[g][:, b0 : b0 + P].bitcast(FP8X4),
+                        lhsT_scale=x_plane[g][:, b0 : b0 + P],
+                        rhs=w1_codes[e][:, g, :].bitcast(FP4X4),
+                        rhs_scale=w1_plane[:, e * PASSES + g, :],
+                        start=(g == 0),
+                        stop=(g == PASSES - 1),
+                    )
+
+        def relu(b0, on_vector):
+            rows = hpool.tile([P, 2, P, 2], BF16, name="h_rows", align_bytes=64)
+            sums = a_banks[b0][:].rearrange("s (p u d) -> s u p d", u=2, d=2)
+            if on_vector:
+                nc.vector.tensor_scalar_max(rows[:], sums, 0.0)
+            else:
+                nc.scalar.activation(rows[:], sums, RELU)
+            h_rows[b0] = rows
+
+        def turn_h(s0, width, on_vector):
+            turned = psum_b.tile([P, 2, width], F32, name="turned")
+            for b0 in range(s0, s0 + width, P):
+                words = h_rows[b0][:].rearrange("s u p d -> s (u p d)").bitcast(F32)
+                for u in range(2):
+                    nc.tensor.transpose(turned[:, u, b0 - s0 : b0 - s0 + P], words[:, u * P : (u + 1) * P], identity[:])
+            grouped = hpool.tile([P, width * PACK], BF16, name="h_grouped", align_bytes=64)
+            move = nc.vector.tensor_copy if on_vector else nc.scalar.copy
+            move(grouped[:].bitcast(F32).rearrange("p (s u) -> p s u", u=2), turned[:].rearrange("p u s -> p s u"))
+            h_grouped[s0] = grouped
+
+        def second_layer(s0, width):
+            e = s0 // C
+            h_codes = hpool.tile([P, width], U32, name="h_codes", align_bytes=64)
+            h_plane = hpool.tile([P, width], U8, name="h_plane", align_bytes=64)
+            nc.vector.quantize_mx(out=h_codes[:].bitcast(FP8X4), scales=h_plane[:], in_=h_grouped[s0][:])
+            y_bank = psum_b.tile([P, N // P, width], F32, name="y_bank")
+            for b in range(N // P):
+                nc.tensor.matmul_mx(
+                    out=y_bank[:, b, :],
+                    lhsT=w2_codes[:, e, 2 * b * P : 2 * (b + 1) * P].bitcast(FP4X4),
+                    lhsT_scale=w2_plane[:, e, b * P : (b + 1) * P],
+                    rhs=h_codes[:].bitcast(FP8X4),
+                    rhs_scale=h_plane[:],
+                    start=True,
+                    stop=True,
+                )
+            y_banks[s0] = y_bank
+
+        def store_y(s0, width, on_vector):
+            move = nc.vector.tensor_copy if on_vector else nc.scalar.copy
+            move(y_all[:, :, s0 : s0 + width], y_banks[s0][:])
+
+        steps = {"G": gather_x, "Q": quantize_x, "M": first_layer, "R": relu, "T": turn_h, "H": second_layer, "Y": store_y}
+        for step in PROGRAM:
+            steps[step[0]](*step[1:])
+
+        first = [stage.tile([P, T], F32, name="first", align_bytes=64) for b in range(N // P)]
+        second = [stage.tile([P, T], F32, name="second", align_bytes=64) for b in range(N // P)]
+        total = [stage.tile([P, T], F32, name="total", align_bytes=64) for b in range(N // P)]
+        nc.vector.tensor_copy(first[0][:], y_rows[0].indirect(first_slots[:]))
+        nc.vector.tensor_copy(second[0][:], y_rows[0].indirect(second_slots[:]))
+        nc.vector.tensor_copy(first[1][:], y_rows[1].indirect(first_slots[:]))
+        nc.vector.tensor_tensor(total[0][:], first[0][:], second[0][:], ADD)
+        nc.sync.dma_start(out[0:P, :], total[0][:])
+        nc.vector.tensor_copy(second[1][:], y_rows[1].indirect(second_slots[:]))
+        for t0 in range(0, T, T // 2):
+            cols = slice(t0, t0 + T // 2)
+            nc.vector.tensor_tensor(total[1][:, cols], first[1][:, cols], second[1][:, cols], ADD)
+            nc.sync.dma_start(out[P : 2 * P, cols], total[1][:, cols])

@@ -27,61 +27,72 @@ ADD = mybir.AluOpType.add
 COPY = mybir.ActivationFunctionType.Copy
 RELU = mybir.ActivationFunctionType.Relu
 
-WINDOW = 800
-GATE_PIECES = [(0, 256), (256, 512), (768, 512)]
+WINDOW = 640
+GATE_PIECES = [(0, 256), (256, 256), (512, 768)]
 PROGRAM = [
-    ("G", 0, 768, 0, 256),
-    ("Q", 0, 768, 0),
-    ("G", 0, 768, 1),
-    ("G", 0, 768, 2),
-    ("Q", 0, 768, 1),
-    ("Q", 0, 768, 2),
-    ("M", 0, 256, 0, 3),
-    ("M", 256, 256, 0, 3),
-    ("M", 512, 256, 0, 3),
+    ("G", 0, 512, 0, 256),
+    ("G", 0, 512, 1),
+    ("Q", 0, 512, 0),
+    ("M", 0, 512, 0, 1),
+    ("G", 0, 512, 2),
+    ("Q", 0, 512, 1),
+    ("M", 0, 512, 1, 2),
+    ("G", 512, 512, 0),
+    ("Q", 0, 512, 2),
+    ("M", 0, 512, 2, 3),
     ("R", 0, False),
     ("R", 128, False),
-    ("R", 512, False),
-    ("R", 384, False),
-    ("G", 768, 512, 0),
     ("R", 256, False),
-    ("G", 768, 512, 1),
-    ("R", 640, False),
-    ("T", 256, 256, False),
-    ("H", 256, 256),
+    ("R", 384, False),
     ("T", 0, 256, False),
-    ("Q", 768, 512, 0),
-    ("Q", 768, 512, 1),
-    ("G", 768, 256, 2),
-    ("G", 1024, 128, 2),
+    ("G", 512, 512, 1),
+    ("T", 256, 256, False),
+    ("Q", 512, 512, 0),
+    ("M", 512, 512, 0, 1),
+    ("G", 512, 512, 2),
     ("H", 0, 256),
-    ("Q", 768, 256, 2),
-    ("G", 1152, 128, 2),
-    ("M", 768, 256, 0, 3),
-    ("M", 1152, 128, 0, 2),
-    ("M", 1024, 128, 0, 2),
-    ("Q", 1024, 128, 2),
-    ("T", 512, 256, False),
-    ("Q", 1152, 128, 2),
-    ("R", 768, True),
-    ("R", 896, True),
+    ("H", 256, 256),
     ("Y", 0, 256, False),
+    ("Q", 512, 512, 1),
+    ("M", 512, 512, 1, 2),
+    ("G", 1024, 256, 0),
+    ("Y", 256, 256, False),
+    ("Q", 512, 512, 2),
+    ("M", 512, 128, 2, 3),
+    ("M", 640, 128, 2, 3),
+    ("R", 512, False),
+    ("R", 640, False),
+    ("M", 768, 128, 2, 3),
+    ("M", 896, 128, 2, 3),
+    ("G", 1024, 256, 1),
+    ("R", 768, False),
+    ("R", 896, False),
+    ("Q", 1024, 256, 0),
+    ("G", 1024, 128, 2),
+    ("Q", 1024, 256, 1),
+    ("M", 1024, 128, 0, 1),
+    ("G", 1152, 128, 2),
+    ("M", 1024, 128, 1, 2),
+    ("M", 1152, 128, 0, 1),
+    ("T", 512, 256, False),
+    ("M", 1152, 128, 1, 2),
+    ("Q", 1024, 128, 2),
+    ("T", 768, 256, True),
     ("M", 1024, 128, 2, 3),
+    ("Q", 1152, 128, 2),
     ("M", 1152, 128, 2, 3),
     ("R", 1024, False),
-    ("R", 1152, False),
-    ("T", 768, 256, True),
-    ("T", 1024, 128, True),
-    ("Y", 256, 256, False),
-    ("H", 512, 256),
-    ("T", 1152, 128, True),
-    ("H", 1024, 128),
+    ("T", 1024, 128, False),
     ("H", 768, 256),
-    ("Y", 1024, 128, False),
-    ("H", 1152, 128),
-    ("Y", 512, 256, False),
+    ("H", 512, 256),
+    ("Y", 512, 256, True),
+    ("R", 1152, True),
+    ("T", 1152, 128, False),
     ("Y", 768, 256, False),
+    ("H", 1024, 128),
+    ("H", 1152, 128),
     ("Y", 1152, 128, True),
+    ("Y", 1024, 128, False),
 ]
 
 
@@ -91,9 +102,9 @@ def tile_moe_pre_mlp_relu_kernel(
     nc = tc.nc
     with ExitStack() as ctx:
         keep = ctx.enter_context(tc.tile_pool(name="keep", bufs=1))
-        stage = ctx.enter_context(tc.tile_pool(name="stage", bufs=2))
-        gpool = ctx.enter_context(tc.tile_pool(name="gpool", bufs=8))
-        hpool = ctx.enter_context(tc.tile_pool(name="hpool", bufs=10))
+        v_ring = ctx.enter_context(tc.tile_pool(name="v_ring", bufs=10))
+        s_ring = ctx.enter_context(tc.tile_pool(name="s_ring", bufs=8))
+        codes = ctx.enter_context(tc.tile_pool(name="codes", bufs=10))
         psum_a = ctx.enter_context(tc.psum_pool(name="psum_a", bufs=4))
         psum_b = ctx.enter_context(tc.psum_pool(name="psum_b", bufs=2))
 
@@ -102,8 +113,6 @@ def tile_moe_pre_mlp_relu_kernel(
         second_slots = keep.tile([P, T // OFFS_COL], U16, name="second_slots")
         planes = [[keep.tile([P, WINDOW], F32, name="plane_%d_%d" % (g, j), align_bytes=64) for j in range(PACK)] for g in range(PASSES)]
         gates = keep.tile([P, S], F32, name="gates", align_bytes=64)
-        x_codes = [keep.tile([P, S], U32, name="x_codes_%d" % g, align_bytes=64) for g in range(PASSES)]
-        x_plane = [keep.tile([P, S], U8, name="x_plane_%d" % g, align_bytes=64) for g in range(PASSES)]
         w1_codes = [keep.tile([P, PASSES, 2 * H], U8, name="w1_codes_%d" % e, align_bytes=64) for e in range(E)]
         w1_plane = keep.tile([P, E * PASSES, H], U8, name="w1_plane", align_bytes=64)
         w2_codes = keep.tile([P, E, 2 * N], U8, name="w2_codes", align_bytes=64)
@@ -114,9 +123,6 @@ def tile_moe_pre_mlp_relu_kernel(
 
         nc.vector.memset(w1_plane[:].rearrange("p a b -> p (a b)").bitcast(I32), 0)
         nc.vector.memset(w2_plane[:].rearrange("p a b -> p (a b)").bitcast(I32), 0)
-        for g in range(PASSES):
-            for j in range(PACK):
-                nc.gpsimd.memset(planes[g][j][:, T:WINDOW], 0.0)
         make_identity(nc, identity[:])
 
         x_rows = xT.rearrange("(g p j) t -> g j p t", p=P, j=PACK)
@@ -147,20 +153,21 @@ def tile_moe_pre_mlp_relu_kernel(
             return [(s0, width)] if width in (128, 256, 512, 1024) else [(s0, 512 if width > 512 else 256), (s0 + (512 if width > 512 else 256), width - (512 if width > 512 else 256))]
 
         x_grouped = {}
+        x_mx = {}
         a_banks = {}
         h_rows = {}
         h_grouped = {}
         y_banks = {}
 
         def gather_x(s0, width, g, head=0):
-            gathered = stage.tile([P, PACK, width], F32, name="gathered", align_bytes=64)
+            gathered = v_ring.tile([P, PACK, width], F32, name="gathered", tag="v", align_bytes=64)
             for j in range(PACK):
                 cuts = [0, head, width] if head and j == 0 else [0, width]
                 for c0, c1 in zip(cuts, cuts[1:]):
                     offsets = slot_tokens[:, (s0 + c0) // OFFS_COL : (s0 + c1) // OFFS_COL]
                     nc.vector.tensor_tensor(gathered[:, j, c0:c1], planes[g][j][:].indirect(offsets), gates[:, s0 + c0 : s0 + c1], MULT)
             for p0, w in pieces(s0, width):
-                grouped = gpool.tile([P, w, PACK], BF16, name="x_grouped", align_bytes=64)
+                grouped = s_ring.tile([P, w, PACK], BF16, name="x_grouped", tag="s", align_bytes=64)
                 nc.scalar.activation(
                     grouped[:].rearrange("p (c i) j -> p c j i", i=4),
                     gathered[:, :, p0 - s0 : p0 - s0 + w].rearrange("p j (c i) -> p c j i", i=4),
@@ -170,9 +177,13 @@ def tile_moe_pre_mlp_relu_kernel(
 
         def quantize_x(s0, width, g):
             for p0, w in pieces(s0, width):
+                x_codes = codes.tile([P, w], U32, name="x_codes", align_bytes=64)
+                x_plane = v_ring.tile([P, w], U8, name="x_plane", tag="v", align_bytes=64)
+                for b0 in range(p0, p0 + w, P):
+                    x_mx[b0, g] = (x_codes[:, b0 - p0 : b0 - p0 + P], x_plane[:, b0 - p0 : b0 - p0 + P])
                 nc.vector.quantize_mx(
-                    out=x_codes[g][:, p0 : p0 + w].bitcast(FP8X4),
-                    scales=x_plane[g][:, p0 : p0 + w],
+                    out=x_codes[:].bitcast(FP8X4),
+                    scales=x_plane[:],
                     in_=x_grouped[p0, g][:].rearrange("p c j -> p (c j)"),
                 )
 
@@ -184,8 +195,8 @@ def tile_moe_pre_mlp_relu_kernel(
                 for g in range(g0, g1):
                     nc.tensor.matmul_mx(
                         out=a_banks[b0][:],
-                        lhsT=x_codes[g][:, b0 : b0 + P].bitcast(FP8X4),
-                        lhsT_scale=x_plane[g][:, b0 : b0 + P],
+                        lhsT=x_mx[b0, g][0].bitcast(FP8X4),
+                        lhsT_scale=x_mx[b0, g][1],
                         rhs=w1_codes[e][:, g, :].bitcast(FP4X4),
                         rhs_scale=w1_plane[:, e * PASSES + g, :],
                         start=(g == 0),
@@ -193,7 +204,7 @@ def tile_moe_pre_mlp_relu_kernel(
                     )
 
         def relu(b0, on_vector):
-            rows = hpool.tile([P, 2, P, 2], BF16, name="h_rows", align_bytes=64)
+            rows = (v_ring if on_vector else s_ring).tile([P, 2, P, 2], BF16, name="h_rows", tag="v" if on_vector else "s", align_bytes=64)
             sums = a_banks[b0][:].rearrange("s (p u d) -> s u p d", u=2, d=2)
             if on_vector:
                 nc.vector.tensor_scalar_max(rows[:], sums, 0.0)
@@ -207,15 +218,15 @@ def tile_moe_pre_mlp_relu_kernel(
                 words = h_rows[b0][:].rearrange("s u p d -> s (u p d)").bitcast(F32)
                 for u in range(2):
                     nc.tensor.transpose(turned[:, u, b0 - s0 : b0 - s0 + P], words[:, u * P : (u + 1) * P], identity[:])
-            grouped = hpool.tile([P, width * PACK], BF16, name="h_grouped", align_bytes=64)
+            grouped = (v_ring if on_vector else s_ring).tile([P, width * PACK], BF16, name="h_grouped", tag="v" if on_vector else "s", align_bytes=64)
             move = nc.vector.tensor_copy if on_vector else nc.scalar.copy
             move(grouped[:].bitcast(F32).rearrange("p (s u) -> p s u", u=2), turned[:].rearrange("p u s -> p s u"))
             h_grouped[s0] = grouped
 
         def second_layer(s0, width):
             e = s0 // C
-            h_codes = hpool.tile([P, width], U32, name="h_codes", align_bytes=64)
-            h_plane = hpool.tile([P, width], U8, name="h_plane", align_bytes=64)
+            h_codes = codes.tile([P, width], U32, name="h_codes", align_bytes=64)
+            h_plane = v_ring.tile([P, width], U8, name="h_plane", tag="v", align_bytes=64)
             nc.vector.quantize_mx(out=h_codes[:].bitcast(FP8X4), scales=h_plane[:], in_=h_grouped[s0][:])
             y_bank = psum_b.tile([P, N // P, width], F32, name="y_bank")
             for b in range(N // P):
@@ -238,16 +249,20 @@ def tile_moe_pre_mlp_relu_kernel(
         for step in PROGRAM:
             steps[step[0]](*step[1:])
 
-        first = [stage.tile([P, T], F32, name="first", align_bytes=64) for b in range(N // P)]
-        second = [stage.tile([P, T], F32, name="second", align_bytes=64) for b in range(N // P)]
-        total = [stage.tile([P, T], F32, name="total", align_bytes=64) for b in range(N // P)]
-        nc.vector.tensor_copy(first[0][:], y_rows[0].indirect(first_slots[:]))
-        nc.vector.tensor_copy(second[0][:], y_rows[0].indirect(second_slots[:]))
-        nc.vector.tensor_copy(first[1][:], y_rows[1].indirect(first_slots[:]))
-        nc.vector.tensor_tensor(total[0][:], first[0][:], second[0][:], ADD)
-        nc.sync.dma_start(out[0:P, :], total[0][:])
-        nc.vector.tensor_copy(second[1][:], y_rows[1].indirect(second_slots[:]))
+        def fetch(b, slots):
+            fetched = v_ring.tile([P, T], F32, name="fetched", tag="v", align_bytes=64)
+            nc.vector.tensor_copy(fetched[:], y_rows[b].indirect(slots[:]))
+            return fetched
+
+        first_0 = fetch(0, first_slots)
+        second_0 = fetch(0, second_slots)
+        first_1 = fetch(1, first_slots)
+        total_0 = v_ring.tile([P, T], F32, name="total_0", tag="v", align_bytes=64)
+        nc.vector.tensor_tensor(total_0[:], first_0[:], second_0[:], ADD)
+        nc.sync.dma_start(out[0:P, :], total_0[:])
+        second_1 = fetch(1, second_slots)
+        total_1 = v_ring.tile([P, T], F32, name="total_1", tag="v", align_bytes=64)
         for t0 in range(0, T, T // 2):
             cols = slice(t0, t0 + T // 2)
-            nc.vector.tensor_tensor(total[1][:, cols], first[1][:, cols], second[1][:, cols], ADD)
-            nc.sync.dma_start(out[P : 2 * P, cols], total[1][:, cols])
+            nc.vector.tensor_tensor(total_1[:, cols], first_1[:, cols], second_1[:, cols], ADD)
+            nc.sync.dma_start(out[P : 2 * P, cols], total_1[:, cols])

@@ -31,13 +31,17 @@ WINDOW = 640
 GATE_PIECES = [(0, 256), (256, 256), (512, 768)]
 PROGRAM = [
     ("G", 0, 512, 0, 256),
+    ("I", 0, 512, 0, False),
     ("G", 0, 512, 1),
+    ("I", 0, 512, 1, False),
     ("Q", 0, 512, 0),
     ("M", 0, 512, 0, 1),
     ("G", 0, 512, 2),
+    ("I", 0, 512, 2, False),
     ("Q", 0, 512, 1),
     ("M", 0, 512, 1, 2),
     ("G", 512, 512, 0),
+    ("I", 512, 512, 0, False),
     ("Q", 0, 512, 2),
     ("M", 0, 512, 2, 3),
     ("R", 0, False),
@@ -46,53 +50,55 @@ PROGRAM = [
     ("R", 384, False),
     ("T", 0, 256, False),
     ("G", 512, 512, 1),
+    ("I", 512, 512, 1, False),
     ("T", 256, 256, False),
     ("Q", 512, 512, 0),
     ("M", 512, 512, 0, 1),
     ("G", 512, 512, 2),
-    ("H", 0, 256),
-    ("H", 256, 256),
-    ("Y", 0, 256, False),
+    ("I", 512, 512, 2, False),
     ("Q", 512, 512, 1),
-    ("M", 512, 512, 1, 2),
     ("G", 1024, 256, 0),
-    ("Y", 256, 256, False),
+    ("H", 0, 256),
+    ("I", 1024, 256, 0, False),
+    ("M", 512, 512, 1, 2),
     ("Q", 512, 512, 2),
-    ("M", 512, 128, 2, 3),
-    ("M", 640, 128, 2, 3),
-    ("R", 512, False),
-    ("R", 640, False),
-    ("M", 768, 128, 2, 3),
-    ("M", 896, 128, 2, 3),
+    ("M", 512, 512, 2, 3),
+    ("Y", 0, 256, False),
     ("G", 1024, 256, 1),
-    ("R", 768, False),
-    ("R", 896, False),
+    ("R", 512, False),
     ("Q", 1024, 256, 0),
+    ("R", 640, False),
+    ("R", 768, False),
+    ("I", 1024, 256, 1, False),
+    ("M", 1024, 256, 0, 1),
+    ("H", 256, 256),
+    ("R", 896, False),
     ("G", 1024, 128, 2),
     ("Q", 1024, 256, 1),
-    ("M", 1024, 128, 0, 1),
     ("G", 1152, 128, 2),
-    ("M", 1024, 128, 1, 2),
-    ("M", 1152, 128, 0, 1),
-    ("T", 512, 256, False),
-    ("M", 1152, 128, 1, 2),
+    ("I", 1024, 128, 2, False),
     ("Q", 1024, 128, 2),
-    ("T", 768, 256, True),
+    ("T", 512, 256, False),
+    ("I", 1152, 128, 2, True),
+    ("T", 768, 256, False),
+    ("M", 1024, 256, 1, 2),
     ("M", 1024, 128, 2, 3),
     ("Q", 1152, 128, 2),
-    ("M", 1152, 128, 2, 3),
+    ("H", 512, 256),
+    ("Y", 256, 256, False),
+    ("H", 768, 256),
     ("R", 1024, False),
     ("T", 1024, 128, False),
-    ("H", 768, 256),
-    ("H", 512, 256),
-    ("Y", 512, 256, True),
+    ("Y", 512, 256, False),
+    ("M", 1152, 128, 2, 3),
     ("R", 1152, True),
     ("T", 1152, 128, False),
-    ("Y", 768, 256, False),
     ("H", 1024, 128),
     ("H", 1152, 128),
-    ("Y", 1152, 128, True),
-    ("Y", 1024, 128, False),
+    ("Y", 768, 256, True),
+    ("Z", 1152, 128, 0, False),
+    ("Z", 1152, 128, 1, False),
+    ("Y", 1024, 128, True),
 ]
 
 
@@ -105,8 +111,7 @@ def tile_moe_pre_mlp_relu_kernel(
         v_ring = ctx.enter_context(tc.tile_pool(name="v_ring", bufs=10))
         s_ring = ctx.enter_context(tc.tile_pool(name="s_ring", bufs=8))
         codes = ctx.enter_context(tc.tile_pool(name="codes", bufs=10))
-        psum_a = ctx.enter_context(tc.psum_pool(name="psum_a", bufs=4))
-        psum_b = ctx.enter_context(tc.psum_pool(name="psum_b", bufs=2))
+        psum = ctx.enter_context(tc.psum_pool(name="psum", bufs=8))
 
         slot_tokens = keep.tile([P, S // OFFS_COL], U16, name="slot_tokens")
         first_slots = keep.tile([P, T // OFFS_COL], U16, name="first_slots")
@@ -154,6 +159,7 @@ def tile_moe_pre_mlp_relu_kernel(
 
         x_grouped = {}
         x_mx = {}
+        x_gathered = {}
         a_banks = {}
         h_rows = {}
         h_grouped = {}
@@ -166,14 +172,17 @@ def tile_moe_pre_mlp_relu_kernel(
                 for c0, c1 in zip(cuts, cuts[1:]):
                     offsets = slot_tokens[:, (s0 + c0) // OFFS_COL : (s0 + c1) // OFFS_COL]
                     nc.vector.tensor_tensor(gathered[:, j, c0:c1], planes[g][j][:].indirect(offsets), gates[:, s0 + c0 : s0 + c1], MULT)
-            for p0, w in pieces(s0, width):
-                grouped = s_ring.tile([P, w, PACK], BF16, name="x_grouped", tag="s", align_bytes=64)
-                nc.scalar.activation(
-                    grouped[:].rearrange("p (c i) j -> p c j i", i=4),
-                    gathered[:, :, p0 - s0 : p0 - s0 + w].rearrange("p j (c i) -> p c j i", i=4),
-                    COPY,
-                )
-                x_grouped[p0, g] = grouped
+            x_gathered[s0, g] = gathered
+
+        def group_x(s0, width, g, on_vector):
+            grouped = (v_ring if on_vector else s_ring).tile([P, width, PACK], BF16, name="x_grouped", tag="v" if on_vector else "s", align_bytes=64)
+            dst = grouped[:].rearrange("p (c i) j -> p c j i", i=4)
+            src = x_gathered[s0, g][:].rearrange("p j (c i) -> p c j i", i=4)
+            if on_vector:
+                nc.vector.tensor_copy(dst, src)
+            else:
+                nc.scalar.activation(dst, src, COPY)
+            x_grouped[s0, g] = grouped
 
         def quantize_x(s0, width, g):
             for p0, w in pieces(s0, width):
@@ -191,7 +200,7 @@ def tile_moe_pre_mlp_relu_kernel(
             for b0 in range(s0, s0 + width, P):
                 e = b0 // C
                 if g0 == 0:
-                    a_banks[b0] = psum_a.tile([P, H], F32, name="a_bank")
+                    a_banks[b0] = psum.tile([P, H], F32, name="a_bank", tag="bank")
                 for g in range(g0, g1):
                     nc.tensor.matmul_mx(
                         out=a_banks[b0][:],
@@ -213,7 +222,7 @@ def tile_moe_pre_mlp_relu_kernel(
             h_rows[b0] = rows
 
         def turn_h(s0, width, on_vector):
-            turned = psum_b.tile([P, 2, width], F32, name="turned")
+            turned = psum.tile([P, 2, width], F32, name="turned", tag="bank")
             for b0 in range(s0, s0 + width, P):
                 words = h_rows[b0][:].rearrange("s u p d -> s (u p d)").bitcast(F32)
                 for u in range(2):
@@ -228,7 +237,7 @@ def tile_moe_pre_mlp_relu_kernel(
             h_codes = codes.tile([P, width], U32, name="h_codes", align_bytes=64)
             h_plane = v_ring.tile([P, width], U8, name="h_plane", tag="v", align_bytes=64)
             nc.vector.quantize_mx(out=h_codes[:].bitcast(FP8X4), scales=h_plane[:], in_=h_grouped[s0][:])
-            y_bank = psum_b.tile([P, N // P, width], F32, name="y_bank")
+            y_bank = psum.tile([P, N // P, width], F32, name="y_bank", tag="bank")
             for b in range(N // P):
                 nc.tensor.matmul_mx(
                     out=y_bank[:, b, :],
@@ -245,24 +254,30 @@ def tile_moe_pre_mlp_relu_kernel(
             move = nc.vector.tensor_copy if on_vector else nc.scalar.copy
             move(y_all[:, :, s0 : s0 + width], y_banks[s0][:])
 
-        steps = {"G": gather_x, "Q": quantize_x, "M": first_layer, "R": relu, "T": turn_h, "H": second_layer, "Y": store_y}
+        def store_y_rows(s0, width, b, on_vector):
+            move = nc.vector.tensor_copy if on_vector else nc.scalar.copy
+            move(y_all[:, b, s0 : s0 + width], y_banks[s0][:, b, :])
+
+        steps = {"I": group_x, "Z": store_y_rows, "G": gather_x, "Q": quantize_x, "M": first_layer, "R": relu, "T": turn_h, "H": second_layer, "Y": store_y}
         for step in PROGRAM:
             steps[step[0]](*step[1:])
 
-        def fetch(b, slots):
-            fetched = v_ring.tile([P, T], F32, name="fetched", tag="v", align_bytes=64)
-            nc.vector.tensor_copy(fetched[:], y_rows[b].indirect(slots[:]))
+        def fetch(b, slots, t0, width):
+            fetched = v_ring.tile([P, width], F32, name="fetched", tag="v", align_bytes=64)
+            nc.vector.tensor_copy(fetched[:], y_rows[b].indirect(slots[:, t0 // OFFS_COL : (t0 + width) // OFFS_COL]))
             return fetched
 
-        first_0 = fetch(0, first_slots)
-        second_0 = fetch(0, second_slots)
-        first_1 = fetch(1, first_slots)
-        total_0 = v_ring.tile([P, T], F32, name="total_0", tag="v", align_bytes=64)
-        nc.vector.tensor_tensor(total_0[:], first_0[:], second_0[:], ADD)
-        nc.sync.dma_start(out[0:P, :], total_0[:])
-        second_1 = fetch(1, second_slots)
-        total_1 = v_ring.tile([P, T], F32, name="total_1", tag="v", align_bytes=64)
-        for t0 in range(0, T, T // 2):
-            cols = slice(t0, t0 + T // 2)
-            nc.vector.tensor_tensor(total_1[:, cols], first_1[:, cols], second_1[:, cols], ADD)
-            nc.sync.dma_start(out[P : 2 * P, cols], total_1[:, cols])
+        def combine(b, t0, width, first, second, engine):
+            total = v_ring.tile([P, width], F32, name="total", tag="v", align_bytes=64)
+            engine.tensor_tensor(total[:], first, second, ADD)
+            nc.sync.dma_start(out[b * P : (b + 1) * P, t0 : t0 + width], total[:])
+
+        half = T // 2
+        first_0 = fetch(0, first_slots, 0, T)
+        second_0 = fetch(0, second_slots, 0, T)
+        first_1 = fetch(1, first_slots, 0, T)
+        second_1a = fetch(1, second_slots, 0, half)
+        combine(0, 0, T, first_0[:], second_0[:], nc.vector)
+        second_1b = fetch(1, second_slots, half, half)
+        combine(1, 0, half, first_1[:, 0:half], second_1a[:], nc.vector)
+        combine(1, half, half, first_1[:, half:T], second_1b[:], nc.vector)

@@ -268,16 +268,11 @@ def tile_moe_pre_mlp_relu_kernel(
             return fetched
 
         def combine(b, t0, width, first, second, engine):
-            total = v_ring.tile([P, width], F32, name="total", tag="v", align_bytes=64)
+            total = codes.tile([P, width], F32, name="total", bufs=3, align_bytes=64)
             engine.tensor_tensor(total[:], first, second, ADD)
             nc.sync.dma_start(out[b * P : (b + 1) * P, t0 : t0 + width], total[:])
 
-        half = T // 2
-        first_0 = fetch(0, first_slots, 0, T)
-        second_0 = fetch(0, second_slots, 0, T)
-        first_1 = fetch(1, first_slots, 0, T)
-        second_1a = fetch(1, second_slots, 0, half)
-        combine(0, 0, T, first_0[:], second_0[:], nc.vector)
-        second_1b = fetch(1, second_slots, half, half)
-        combine(1, 0, half, first_1[:, 0:half], second_1a[:], nc.vector)
-        combine(1, half, half, first_1[:, half:T], second_1b[:], nc.vector)
+        for b, t0, width, engine in ((0, 0, T, nc.gpsimd), (1, 0, 416, nc.gpsimd), (1, 416, T - 416, nc.vector)):
+            first = fetch(b, first_slots, t0, width)
+            second = fetch(b, second_slots, t0, width)
+            combine(b, t0, width, first[:], second[:], engine)

@@ -7,9 +7,9 @@ K, T, E, C, H, N = 1536, 640, 5, 256, 512, 256
 S = E * C
 P = 128
 PACK = 4
-K_PASS = P * PACK
-PASSES = K // K_PASS
-OFFS_COL = 16
+PASSES = K // (P * PACK)
+LIST_COLUMN = 16
+QUADRANT = 32
 
 FLOPS = 2 * S * (K * H + H * N)
 BYTES = 4 * K * T + E * (K * H + H * N) // 2 + E * (K * H + H * N) // 32 + 4 * S + 2 * P * (S + 2 * T) // 16 + 4 * N * T
@@ -27,79 +27,12 @@ ADD = mybir.AluOpType.add
 COPY = mybir.ActivationFunctionType.Copy
 RELU = mybir.ActivationFunctionType.Relu
 
-WINDOW = 640
-GATE_PIECES = [(0, 256), (256, 256), (512, 768)]
-PROGRAM = [
-    ("G", 0, 512, 0, 256),
-    ("I", 0, 512, 0, False),
-    ("G", 0, 512, 1),
-    ("I", 0, 512, 1, False),
-    ("Q", 0, 512, 0),
-    ("M", 0, 512, 0, 1),
-    ("G", 0, 512, 2),
-    ("I", 0, 512, 2, False),
-    ("Q", 0, 512, 1),
-    ("M", 0, 512, 1, 2),
-    ("G", 512, 512, 0),
-    ("I", 512, 512, 0, False),
-    ("Q", 0, 512, 2),
-    ("M", 0, 512, 2, 3),
-    ("R", 0, False),
-    ("R", 128, False),
-    ("R", 256, False),
-    ("R", 384, False),
-    ("T", 0, 256, False),
-    ("G", 512, 512, 1),
-    ("I", 512, 512, 1, False),
-    ("T", 256, 256, False),
-    ("Q", 512, 512, 0),
-    ("M", 512, 512, 0, 1),
-    ("G", 512, 512, 2),
-    ("I", 512, 512, 2, False),
-    ("Q", 512, 512, 1),
-    ("G", 1024, 256, 0),
-    ("H", 0, 256),
-    ("I", 1024, 256, 0, False),
-    ("M", 512, 512, 1, 2),
-    ("Q", 512, 512, 2),
-    ("M", 512, 512, 2, 3),
-    ("Y", 0, 256, False),
-    ("G", 1024, 256, 1),
-    ("R", 512, False),
-    ("Q", 1024, 256, 0),
-    ("R", 640, False),
-    ("R", 768, False),
-    ("I", 1024, 256, 1, False),
-    ("M", 1024, 256, 0, 1),
-    ("H", 256, 256),
-    ("R", 896, False),
-    ("G", 1024, 128, 2),
-    ("Q", 1024, 256, 1),
-    ("G", 1152, 128, 2),
-    ("I", 1024, 128, 2, False),
-    ("Q", 1024, 128, 2),
-    ("T", 512, 256, False),
-    ("I", 1152, 128, 2, True),
-    ("T", 768, 256, False),
-    ("M", 1024, 256, 1, 2),
-    ("M", 1024, 128, 2, 3),
-    ("Q", 1152, 128, 2),
-    ("H", 512, 256),
-    ("Y", 256, 256, False),
-    ("H", 768, 256),
-    ("R", 1024, False),
-    ("T", 1024, 128, False),
-    ("Y", 512, 256, False),
-    ("M", 1152, 128, 2, 3),
-    ("R", 1152, True),
-    ("T", 1152, 128, False),
-    ("H", 1024, 128),
-    ("H", 1152, 128),
-    ("Y", 768, 256, True),
-    ("Z", 1152, 128, 0, False),
-    ("Z", 1152, 128, 1, False),
-    ("Y", 1024, 128, True),
-]
+CHUNK_A, CHUNK_B, CHUNK_C = (0, 512), (512, 512), (1024, 256)
+BLOCK_8, BLOCK_9 = (1024, P), (1152, P)
+EXPERT = [(e * C, C) for e in range(E)]
+FIRST_GATHER = 192
+GPSIMD_TOKENS = 384
+VECTOR_RING, SCALAR_RING, CODE_RING, PSUM_BANKS = 10, 8, 10, 8
 
 
 def tile_moe_pre_mlp_relu_kernel(
@@ -108,15 +41,26 @@ def tile_moe_pre_mlp_relu_kernel(
     nc = tc.nc
     with ExitStack() as ctx:
         keep = ctx.enter_context(tc.tile_pool(name="keep", bufs=1))
-        v_ring = ctx.enter_context(tc.tile_pool(name="v_ring", bufs=10))
-        s_ring = ctx.enter_context(tc.tile_pool(name="s_ring", bufs=8))
-        codes = ctx.enter_context(tc.tile_pool(name="codes", bufs=10))
-        psum = ctx.enter_context(tc.psum_pool(name="psum", bufs=8))
+        v_ring = ctx.enter_context(tc.tile_pool(name="v_ring", bufs=VECTOR_RING))
+        s_ring = ctx.enter_context(tc.tile_pool(name="s_ring", bufs=SCALAR_RING))
+        codes = ctx.enter_context(tc.tile_pool(name="codes", bufs=CODE_RING))
+        psum = ctx.enter_context(tc.psum_pool(name="psum", bufs=PSUM_BANKS))
 
-        slot_tokens = keep.tile([P, S // OFFS_COL], U16, name="slot_tokens")
-        first_slots = keep.tile([P, T // OFFS_COL], U16, name="first_slots")
-        second_slots = keep.tile([P, T // OFFS_COL], U16, name="second_slots")
-        planes = [[keep.tile([P, WINDOW], F32, name="plane_%d_%d" % (g, j), align_bytes=64) for j in range(PACK)] for g in range(PASSES)]
+        def ring_tile(engine, shape, dtype, name):
+            if engine is nc.vector:
+                return v_ring.tile(shape, dtype, name=name, tag="v", align_bytes=64)
+            return s_ring.tile(shape, dtype, name=name, tag="s", align_bytes=64)
+
+        def copy(engine, dst, src):
+            if engine is nc.vector:
+                nc.vector.tensor_copy(dst, src)
+            else:
+                nc.scalar.copy(dst, src)
+
+        slot_tokens = keep.tile([P, S // LIST_COLUMN], U16, name="slot_tokens")
+        first_slots = keep.tile([P, T // LIST_COLUMN], U16, name="first_slots")
+        second_slots = keep.tile([P, T // LIST_COLUMN], U16, name="second_slots")
+        tokens = [[keep.tile([P, T], F32, name="tokens_%d_%d" % (g, d), align_bytes=64) for d in range(PACK)] for g in range(PASSES)]
         gates = keep.tile([P, S], F32, name="gates", align_bytes=64)
         w1_codes = [keep.tile([P, PASSES, 2 * H], U8, name="w1_codes_%d" % e, align_bytes=64) for e in range(E)]
         w1_plane = keep.tile([P, E * PASSES, H], U8, name="w1_plane", align_bytes=64)
@@ -124,118 +68,104 @@ def tile_moe_pre_mlp_relu_kernel(
         w2_plane = keep.tile([P, E, N], U8, name="w2_plane", align_bytes=64)
         identity = keep.tile([P, P], F32, name="identity", align_bytes=64)
         y_all = keep.tile([P, N // P, S], F32, name="y_all", align_bytes=64)
-        y_rows = [y_all[:, b, :] for b in range(N // P)]
 
         nc.vector.memset(w1_plane[:].rearrange("p a b -> p (a b)").bitcast(I32), 0)
         nc.vector.memset(w2_plane[:].rearrange("p a b -> p (a b)").bitcast(I32), 0)
         make_identity(nc, identity[:])
 
-        x_rows = xT.rearrange("(g p j) t -> g j p t", p=P, j=PACK)
+        x_rows = xT.rearrange("(g p d) t -> g d p t", p=P, d=PACK)
+        end_a = CHUNK_A[1]
+        nc.sync.dma_start(tokens[0][0][:], x_rows[0, 0])
         nc.sync.dma_start(slot_tokens[:], offs)
-        nc.sync.dma_start(planes[0][0][:, 0:T], x_rows[0, 0])
-        for s0, width in GATE_PIECES[:-1]:
-            nc.sync.dma_start(gates[:, s0 : s0 + width], gate[0:P, s0 : s0 + width])
-        for g in range(PASSES):
-            for j in range(PACK):
-                if g + j > 0:
-                    nc.sync.dma_start(planes[g][j][:, 0:T], x_rows[g, j])
-        s0, width = GATE_PIECES[-1]
-        nc.sync.dma_start(gates[:, s0 : s0 + width], gate[0:P, s0 : s0 + width])
-        w1_rows = w1_scales.rearrange("e s q i -> q (e s) i").bitcast(I32)
-        w2_rows = w2_scales.rearrange("e s q i -> q (e s) i").bitcast(I32)
-        for quad in range(4):
-            nc.sync.dma_start(w1_plane[32 * quad : 32 * quad + 4].bitcast(I32), w1_rows[4 * quad : 4 * quad + 4])
-        for quad in range(4):
-            nc.sync.dma_start(w2_plane[32 * quad : 32 * quad + 4].bitcast(I32), w2_rows[4 * quad : 4 * quad + 4])
+        nc.sync.dma_start(gates[:, 0:FIRST_GATHER], gate[0:P, 0:FIRST_GATHER])
+        nc.sync.dma_start(gates[:, FIRST_GATHER:end_a], gate[0:P, FIRST_GATHER:end_a])
+        for row in range(1, PASSES * PACK):
+            g, d = divmod(row, PACK)
+            nc.sync.dma_start(tokens[g][d][:], x_rows[g, d])
+        nc.sync.dma_start(gates[:, end_a:S], gate[0:P, end_a:S])
+        for plane, scales in ((w1_plane, w1_scales), (w2_plane, w2_scales)):
+            rows = scales.rearrange("e s q i -> q (e s) i").bitcast(I32)
+            for quad in range(P // QUADRANT):
+                nc.sync.dma_start(plane[QUADRANT * quad : QUADRANT * quad + 4].bitcast(I32), rows[4 * quad : 4 * quad + 4])
         for e in range(E):
             nc.sync.dma_start(w1_codes[e][:].bitcast(I32), w1_words[e].rearrange("s p b -> p s b").bitcast(I32))
-            if e == 1:
+            if (e + 1) * C == end_a:
                 nc.sync.dma_start(w2_codes[:].bitcast(I32), w2_words.rearrange("e s p b -> p (e s) b").bitcast(I32))
         nc.sync.dma_start(first_slots[:], pos1)
         nc.sync.dma_start(second_slots[:], pos2)
 
-        def pieces(s0, width):
-            return [(s0, width)] if width in (128, 256, 512, 1024) else [(s0, 512 if width > 512 else 256), (s0 + (512 if width > 512 else 256), width - (512 if width > 512 else 256))]
+        x_gathered, x_grouped, x_operand, a_banks, h_rows, h_grouped, y_banks = {}, {}, {}, {}, {}, {}, {}
 
-        x_grouped = {}
-        x_mx = {}
-        x_gathered = {}
-        a_banks = {}
-        h_rows = {}
-        h_grouped = {}
-        y_banks = {}
-
-        def gather_x(s0, width, g, head=0):
-            gathered = v_ring.tile([P, PACK, width], F32, name="gathered", tag="v", align_bytes=64)
-            for j in range(PACK):
-                cuts = [0, head, width] if head and j == 0 else [0, width]
+        def gather_x(slots, g, first_cut=None):
+            s0, width = slots
+            gathered = ring_tile(nc.vector, [P, PACK, width], F32, "gathered")
+            for d in range(PACK):
+                cuts = [0, first_cut, width] if first_cut and d == 0 else [0, width]
                 for c0, c1 in zip(cuts, cuts[1:]):
-                    offsets = slot_tokens[:, (s0 + c0) // OFFS_COL : (s0 + c1) // OFFS_COL]
-                    nc.vector.tensor_tensor(gathered[:, j, c0:c1], planes[g][j][:].indirect(offsets), gates[:, s0 + c0 : s0 + c1], MULT)
+                    offsets = slot_tokens[:, (s0 + c0) // LIST_COLUMN : (s0 + c1) // LIST_COLUMN]
+                    nc.vector.tensor_tensor(gathered[:, d, c0:c1], tokens[g][d][:].indirect(offsets), gates[:, s0 + c0 : s0 + c1], MULT)
             x_gathered[s0, g] = gathered
 
-        def group_x(s0, width, g, on_vector):
-            grouped = (v_ring if on_vector else s_ring).tile([P, width, PACK], BF16, name="x_grouped", tag="v" if on_vector else "s", align_bytes=64)
-            dst = grouped[:].rearrange("p (c i) j -> p c j i", i=4)
-            src = x_gathered[s0, g][:].rearrange("p j (c i) -> p c j i", i=4)
-            if on_vector:
+        def group_x(slots, g, engine):
+            s0, width = slots
+            grouped = ring_tile(engine, [P, width, PACK], BF16, "x_grouped")
+            dst = grouped[:].rearrange("p (c i) d -> p c d i", i=4)
+            src = x_gathered[s0, g][:].rearrange("p d (c i) -> p c d i", i=4)
+            if engine is nc.vector:
                 nc.vector.tensor_copy(dst, src)
             else:
                 nc.scalar.activation(dst, src, COPY)
             x_grouped[s0, g] = grouped
 
-        def quantize_x(s0, width, g):
-            for p0, w in pieces(s0, width):
-                x_codes = codes.tile([P, w], U32, name="x_codes", align_bytes=64)
-                x_plane = v_ring.tile([P, w], U8, name="x_plane", tag="v", align_bytes=64)
-                for b0 in range(p0, p0 + w, P):
-                    x_mx[b0, g] = (x_codes[:, b0 - p0 : b0 - p0 + P], x_plane[:, b0 - p0 : b0 - p0 + P])
-                nc.vector.quantize_mx(
-                    out=x_codes[:].bitcast(FP8X4),
-                    scales=x_plane[:],
-                    in_=x_grouped[p0, g][:].rearrange("p c j -> p (c j)"),
-                )
+        def quantize_x(slots, g):
+            s0, width = slots
+            x_codes = codes.tile([P, width], U32, name="x_codes", align_bytes=64)
+            x_plane = ring_tile(nc.vector, [P, width], U8, "x_plane")
+            for c0 in range(0, width, P):
+                x_operand[s0 + c0, g] = (x_codes[:, c0 : c0 + P], x_plane[:, c0 : c0 + P])
+            nc.vector.quantize_mx(out=x_codes[:].bitcast(FP8X4), scales=x_plane[:], in_=x_grouped[s0, g][:].rearrange("p c d -> p (c d)"))
 
-        def first_layer(s0, width, g0, g1):
+        def first_layer(slots, g):
+            s0, width = slots
             for b0 in range(s0, s0 + width, P):
                 e = b0 // C
-                if g0 == 0:
+                if g == 0:
                     a_banks[b0] = psum.tile([P, H], F32, name="a_bank", tag="bank")
-                for g in range(g0, g1):
-                    nc.tensor.matmul_mx(
-                        out=a_banks[b0][:],
-                        lhsT=x_mx[b0, g][0].bitcast(FP8X4),
-                        lhsT_scale=x_mx[b0, g][1],
-                        rhs=w1_codes[e][:, g, :].bitcast(FP4X4),
-                        rhs_scale=w1_plane[:, e * PASSES + g, :],
-                        start=(g == 0),
-                        stop=(g == PASSES - 1),
-                    )
+                nc.tensor.matmul_mx(
+                    out=a_banks[b0][:],
+                    lhsT=x_operand[b0, g][0].bitcast(FP8X4),
+                    lhsT_scale=x_operand[b0, g][1],
+                    rhs=w1_codes[e][:, g, :].bitcast(FP4X4),
+                    rhs_scale=w1_plane[:, e * PASSES + g, :],
+                    start=(g == 0),
+                    stop=(g == PASSES - 1),
+                )
 
-        def relu(b0, on_vector):
-            rows = (v_ring if on_vector else s_ring).tile([P, 2, P, 2], BF16, name="h_rows", tag="v" if on_vector else "s", align_bytes=64)
-            sums = a_banks[b0][:].rearrange("s (p u d) -> s u p d", u=2, d=2)
-            if on_vector:
+        def relu(b0, engine):
+            rows = ring_tile(engine, [P, 2, P, 2], BF16, "h_rows")
+            sums = a_banks[b0][:].rearrange("s (p u v) -> s u p v", u=2, v=2)
+            if engine is nc.vector:
                 nc.vector.tensor_scalar_max(rows[:], sums, 0.0)
             else:
                 nc.scalar.activation(rows[:], sums, RELU)
             h_rows[b0] = rows
 
-        def turn_h(s0, width, on_vector):
+        def turn_h(slots):
+            s0, width = slots
             turned = psum.tile([P, 2, width], F32, name="turned", tag="bank")
-            for b0 in range(s0, s0 + width, P):
-                words = h_rows[b0][:].rearrange("s u p d -> s (u p d)").bitcast(F32)
+            for c0 in range(0, width, P):
+                pairs = h_rows[s0 + c0][:].rearrange("s u p v -> s (u p v)").bitcast(F32)
                 for u in range(2):
-                    nc.tensor.transpose(turned[:, u, b0 - s0 : b0 - s0 + P], words[:, u * P : (u + 1) * P], identity[:])
-            grouped = (v_ring if on_vector else s_ring).tile([P, width * PACK], BF16, name="h_grouped", tag="v" if on_vector else "s", align_bytes=64)
-            move = nc.vector.tensor_copy if on_vector else nc.scalar.copy
-            move(grouped[:].bitcast(F32).rearrange("p (s u) -> p s u", u=2), turned[:].rearrange("p u s -> p s u"))
+                    nc.tensor.transpose(turned[:, u, c0 : c0 + P], pairs[:, u * P : (u + 1) * P], identity[:])
+            grouped = ring_tile(nc.scalar, [P, width * PACK], BF16, "h_grouped")
+            nc.scalar.copy(grouped[:].bitcast(F32).rearrange("p (s u) -> p s u", u=2), turned[:].rearrange("p u s -> p s u"))
             h_grouped[s0] = grouped
 
-        def second_layer(s0, width):
+        def second_layer(slots):
+            s0, width = slots
             e = s0 // C
             h_codes = codes.tile([P, width], U32, name="h_codes", align_bytes=64)
-            h_plane = v_ring.tile([P, width], U8, name="h_plane", tag="v", align_bytes=64)
+            h_plane = ring_tile(nc.vector, [P, width], U8, "h_plane")
             nc.vector.quantize_mx(out=h_codes[:].bitcast(FP8X4), scales=h_plane[:], in_=h_grouped[s0][:])
             y_bank = psum.tile([P, N // P, width], F32, name="y_bank", tag="bank")
             for b in range(N // P):
@@ -250,29 +180,86 @@ def tile_moe_pre_mlp_relu_kernel(
                 )
             y_banks[s0] = y_bank
 
-        def store_y(s0, width, on_vector):
-            move = nc.vector.tensor_copy if on_vector else nc.scalar.copy
-            move(y_all[:, :, s0 : s0 + width], y_banks[s0][:])
+        def keep_y(slots, engine):
+            s0, width = slots
+            copy(engine, y_all[:, :, s0 : s0 + width], y_banks[s0][:])
 
-        def store_y_rows(s0, width, b, on_vector):
-            move = nc.vector.tensor_copy if on_vector else nc.scalar.copy
-            move(y_all[:, b, s0 : s0 + width], y_banks[s0][:, b, :])
-
-        steps = {"I": group_x, "Z": store_y_rows, "G": gather_x, "Q": quantize_x, "M": first_layer, "R": relu, "T": turn_h, "H": second_layer, "Y": store_y}
-        for step in PROGRAM:
-            steps[step[0]](*step[1:])
-
-        def fetch(b, slots, t0, width):
-            fetched = v_ring.tile([P, width], F32, name="fetched", tag="v", align_bytes=64)
-            nc.vector.tensor_copy(fetched[:], y_rows[b].indirect(slots[:, t0 // OFFS_COL : (t0 + width) // OFFS_COL]))
+        def fetch_y(b, slot_list, t0, width):
+            fetched = ring_tile(nc.vector, [P, width], F32, "fetched")
+            offsets = slot_list[:, t0 // LIST_COLUMN : (t0 + width) // LIST_COLUMN]
+            nc.vector.tensor_copy(fetched[:], y_all[:, b, :].indirect(offsets))
             return fetched
 
-        def combine(b, t0, width, first, second, engine):
-            total = codes.tile([P, width], F32, name="total", bufs=3, align_bytes=64)
-            engine.tensor_tensor(total[:], first, second, ADD)
-            nc.sync.dma_start(out[b * P : (b + 1) * P, t0 : t0 + width], total[:])
+        vector, scalar = nc.vector, nc.scalar
 
-        for b, t0, width, engine in ((0, 0, T, nc.gpsimd), (1, 0, 416, nc.gpsimd), (1, 416, T - 416, nc.vector)):
-            first = fetch(b, first_slots, t0, width)
-            second = fetch(b, second_slots, t0, width)
-            combine(b, t0, width, first[:], second[:], engine)
+        gather_x(CHUNK_A, 0, FIRST_GATHER)
+        group_x(CHUNK_A, 0, scalar)
+        for (ahead, g_ahead), g in zip(((CHUNK_A, 1), (CHUNK_A, 2), (CHUNK_B, 0)), range(PASSES)):
+            gather_x(ahead, g_ahead)
+            group_x(ahead, g_ahead, scalar)
+            quantize_x(CHUNK_A, g)
+            first_layer(CHUNK_A, g)
+
+        for b0 in range(0, end_a, P):
+            relu(b0, scalar)
+        turn_h(EXPERT[0])
+        gather_x(CHUNK_B, 1)
+        group_x(CHUNK_B, 1, scalar)
+        turn_h(EXPERT[1])
+        quantize_x(CHUNK_B, 0)
+        first_layer(CHUNK_B, 0)
+        gather_x(CHUNK_B, 2)
+        group_x(CHUNK_B, 2, scalar)
+        quantize_x(CHUNK_B, 1)
+
+        gather_x(CHUNK_C, 0)
+        second_layer(EXPERT[0])
+        group_x(CHUNK_C, 0, scalar)
+        first_layer(CHUNK_B, 1)
+        quantize_x(CHUNK_B, 2)
+        first_layer(CHUNK_B, 2)
+        keep_y(EXPERT[0], scalar)
+        gather_x(CHUNK_C, 1)
+        relu(4 * P, scalar)
+        quantize_x(CHUNK_C, 0)
+        relu(5 * P, scalar)
+        relu(6 * P, scalar)
+        group_x(CHUNK_C, 1, scalar)
+        first_layer(CHUNK_C, 0)
+        second_layer(EXPERT[1])
+        relu(7 * P, scalar)
+        gather_x(BLOCK_8, 2)
+        quantize_x(CHUNK_C, 1)
+        gather_x(BLOCK_9, 2)
+
+        group_x(BLOCK_8, 2, scalar)
+        quantize_x(BLOCK_8, 2)
+        turn_h(EXPERT[2])
+        group_x(BLOCK_9, 2, vector)
+        turn_h(EXPERT[3])
+        first_layer(CHUNK_C, 1)
+        first_layer(BLOCK_8, 2)
+        quantize_x(BLOCK_9, 2)
+        second_layer(EXPERT[2])
+        keep_y(EXPERT[1], scalar)
+        second_layer(EXPERT[3])
+        relu(BLOCK_8[0], scalar)
+        turn_h(BLOCK_8)
+        keep_y(EXPERT[2], scalar)
+        first_layer(BLOCK_9, 2)
+        relu(BLOCK_9[0], vector)
+        turn_h(BLOCK_9)
+        second_layer(BLOCK_8)
+        second_layer(BLOCK_9)
+        keep_y(EXPERT[3], vector)
+        for b in range(N // P):
+            nc.scalar.copy(y_all[:, b, BLOCK_9[0] : S], y_banks[BLOCK_9[0]][:, b, :])
+        keep_y(BLOCK_8, vector)
+
+        pieces = ((0, 0, T, nc.gpsimd), (1, 0, GPSIMD_TOKENS, nc.gpsimd), (1, GPSIMD_TOKENS, T - GPSIMD_TOKENS, vector))
+        for b, t0, width, adder in pieces:
+            first = fetch_y(b, first_slots, t0, width)
+            second = fetch_y(b, second_slots, t0, width)
+            total = codes.tile([P, width], F32, name="total", bufs=len(pieces), align_bytes=64)
+            adder.tensor_tensor(total[:], first[:], second[:], ADD)
+            nc.sync.dma_start(out[b * P : (b + 1) * P, t0 : t0 + width], total[:])

@@ -31,8 +31,8 @@ CHUNK_A, CHUNK_B, CHUNK_C = (0, 512), (512, 512), (1024, 256)
 BLOCK_8, BLOCK_9 = (1024, P), (1152, P)
 EXPERT = [(e * C, C) for e in range(E)]
 FIRST_GATHER = 192
-GPSIMD_TOKENS = 384
-VECTOR_RING, SCALAR_RING, CODE_RING, PSUM_BANKS = 10, 8, 10, 8
+LAST_STORE = 256
+VECTOR_RING, SCALAR_RING, CODE_RING, PSUM_BANKS = 10, 12, 10, 8
 
 
 def tile_moe_pre_mlp_relu_kernel(
@@ -67,7 +67,7 @@ def tile_moe_pre_mlp_relu_kernel(
         w2_codes = keep.tile([P, E, 2 * N], U8, name="w2_codes", align_bytes=64)
         w2_plane = keep.tile([P, E, N], U8, name="w2_plane", align_bytes=64)
         identity = keep.tile([P, P], F32, name="identity", align_bytes=64)
-        y_all = keep.tile([P, N // P, S], F32, name="y_all", align_bytes=64)
+        y_half = [keep.tile([P, S], F32, name="y_half_%d" % b, align_bytes=64) for b in range(N // P)]
 
         nc.vector.memset(w1_plane[:].rearrange("p a b -> p (a b)").bitcast(I32), 0)
         nc.vector.memset(w2_plane[:].rearrange("p a b -> p (a b)").bitcast(I32), 0)
@@ -94,7 +94,7 @@ def tile_moe_pre_mlp_relu_kernel(
         nc.sync.dma_start(first_slots[:], pos1)
         nc.sync.dma_start(second_slots[:], pos2)
 
-        x_gathered, x_grouped, x_operand, a_banks, h_rows, h_grouped, y_banks = {}, {}, {}, {}, {}, {}, {}
+        x_gathered, x_grouped, x_operand, a_banks, h_rows, h_turned, h_grouped, h_operand, y_banks = {}, {}, {}, {}, {}, {}, {}, {}, {}
 
         def gather_x(slots, g, first_cut=None):
             s0, width = slots
@@ -129,25 +129,34 @@ def tile_moe_pre_mlp_relu_kernel(
             s0, width = slots
             for b0 in range(s0, s0 + width, P):
                 e = b0 // C
-                if g == 0:
-                    a_banks[b0] = psum.tile([P, H], F32, name="a_bank", tag="bank")
-                nc.tensor.matmul_mx(
-                    out=a_banks[b0][:],
-                    lhsT=x_operand[b0, g][0].bitcast(FP8X4),
-                    lhsT_scale=x_operand[b0, g][1],
-                    rhs=w1_codes[e][:, g, :].bitcast(FP4X4),
-                    rhs_scale=w1_plane[:, e * PASSES + g, :],
-                    start=(g == 0),
-                    stop=(g == PASSES - 1),
-                )
+                columns = P if b0 == BLOCK_9[0] else H
+                for i0 in range(0, H, columns):
+                    if g == 0:
+                        a_banks[b0, i0] = psum.tile([P, columns], F32, name="a_bank", tag="bank")
+                    nc.tensor.matmul_mx(
+                        out=a_banks[b0, i0][:],
+                        lhsT=x_operand[b0, g][0].bitcast(FP8X4),
+                        lhsT_scale=x_operand[b0, g][1],
+                        rhs=w1_codes[e][:, g, 2 * i0 : 2 * (i0 + columns)].bitcast(FP4X4),
+                        rhs_scale=w1_plane[:, e * PASSES + g, i0 : i0 + columns],
+                        start=(g == 0),
+                        stop=(g == PASSES - 1),
+                    )
 
         def relu(b0, engine):
             rows = ring_tile(engine, [P, 2, P, 2], BF16, "h_rows")
-            sums = a_banks[b0][:].rearrange("s (p u v) -> s u p v", u=2, v=2)
-            if engine is nc.vector:
-                nc.vector.tensor_scalar_max(rows[:], sums, 0.0)
-            else:
-                nc.scalar.activation(rows[:], sums, RELU)
+            nc.scalar.activation(rows[:], a_banks[b0, 0][:].rearrange("s (p u v) -> s u p v", u=2, v=2), RELU)
+            h_rows[b0] = rows
+
+        def relu_by_quarters(b0):
+            rows = ring_tile(nc.vector, [P, 2, P, 2], BF16, "h_rows")
+            for i0 in range(0, H, P):
+                dst = rows[:, :, i0 // PACK : (i0 + P) // PACK, :]
+                sums = a_banks[b0, i0][:].rearrange("s (p u v) -> s u p v", u=2, v=2)
+                if i0 < H // 2:
+                    nc.vector.tensor_scalar_max(dst, sums, 0.0)
+                else:
+                    nc.scalar.activation(dst, sums, RELU)
             h_rows[b0] = rows
 
         def turn_h(slots):
@@ -157,109 +166,118 @@ def tile_moe_pre_mlp_relu_kernel(
                 pairs = h_rows[s0 + c0][:].rearrange("s u p v -> s (u p v)").bitcast(F32)
                 for u in range(2):
                     nc.tensor.transpose(turned[:, u, c0 : c0 + P], pairs[:, u * P : (u + 1) * P], identity[:])
-            grouped = ring_tile(nc.scalar, [P, width * PACK], BF16, "h_grouped")
-            nc.scalar.copy(grouped[:].bitcast(F32).rearrange("p (s u) -> p s u", u=2), turned[:].rearrange("p u s -> p s u"))
+            h_turned[s0] = turned
+
+        def group_h(slots, engine):
+            s0, width = slots
+            grouped = ring_tile(engine, [P, width * PACK], BF16, "h_grouped")
+            copy(engine, grouped[:].bitcast(F32).rearrange("p (s u) -> p s u", u=2), h_turned[s0][:].rearrange("p u s -> p s u"))
             h_grouped[s0] = grouped
 
-        def second_layer(slots):
+        def quantize_h(slots):
             s0, width = slots
-            e = s0 // C
             h_codes = codes.tile([P, width], U32, name="h_codes", align_bytes=64)
             h_plane = ring_tile(nc.vector, [P, width], U8, "h_plane")
             nc.vector.quantize_mx(out=h_codes[:].bitcast(FP8X4), scales=h_plane[:], in_=h_grouped[s0][:])
-            y_bank = psum.tile([P, N // P, width], F32, name="y_bank", tag="bank")
-            for b in range(N // P):
+            h_operand[s0] = (h_codes, h_plane)
+
+        def second_layer(parts, b):
+            s0 = parts[0][0]
+            y_bank = psum.tile([P, sum(width for first, width in parts)], F32, name="y_bank", tag="bank")
+            for first, width in parts:
+                e = first // C
                 nc.tensor.matmul_mx(
-                    out=y_bank[:, b, :],
+                    out=y_bank[:, first - s0 : first - s0 + width],
                     lhsT=w2_codes[:, e, 2 * b * P : 2 * (b + 1) * P].bitcast(FP4X4),
                     lhsT_scale=w2_plane[:, e, b * P : (b + 1) * P],
-                    rhs=h_codes[:].bitcast(FP8X4),
-                    rhs_scale=h_plane[:],
+                    rhs=h_operand[first][0][:].bitcast(FP8X4),
+                    rhs_scale=h_operand[first][1][:],
                     start=True,
                     stop=True,
                 )
-            y_banks[s0] = y_bank
+                y_banks[first, b] = (y_bank, first - s0)
 
-        def keep_y(slots, engine):
+        def keep_y(slots, b, engine):
             s0, width = slots
-            copy(engine, y_all[:, :, s0 : s0 + width], y_banks[s0][:])
-
-        def fetch_y(b, slot_list, t0, width):
-            fetched = ring_tile(nc.vector, [P, width], F32, "fetched")
-            offsets = slot_list[:, t0 // LIST_COLUMN : (t0 + width) // LIST_COLUMN]
-            nc.vector.tensor_copy(fetched[:], y_all[:, b, :].indirect(offsets))
-            return fetched
+            y_bank, c0 = y_banks[s0, b]
+            copy(engine, y_half[b][:, s0 : s0 + width], y_bank[:, c0 : c0 + width])
 
         vector, scalar = nc.vector, nc.scalar
 
-        gather_x(CHUNK_A, 0, FIRST_GATHER)
-        group_x(CHUNK_A, 0, scalar)
-        for (ahead, g_ahead), g in zip(((CHUNK_A, 1), (CHUNK_A, 2), (CHUNK_B, 0)), range(PASSES)):
-            gather_x(ahead, g_ahead)
-            group_x(ahead, g_ahead, scalar)
-            quantize_x(CHUNK_A, g)
-            first_layer(CHUNK_A, g)
+        def multiply(slots, g):
+            quantize_x(slots, g)
+            first_layer(slots, g)
 
+        def fetch(slots, g, first_cut=None):
+            gather_x(slots, g, first_cut)
+            group_x(slots, g, scalar)
+
+        fetch(CHUNK_A, 0, FIRST_GATHER)
+        fetch(CHUNK_A, 1)
+        multiply(CHUNK_A, 0)
+        fetch(CHUNK_A, 2)
+        multiply(CHUNK_A, 1)
+        fetch(CHUNK_B, 0)
+        multiply(CHUNK_A, 2)
         for b0 in range(0, end_a, P):
             relu(b0, scalar)
         turn_h(EXPERT[0])
-        gather_x(CHUNK_B, 1)
-        group_x(CHUNK_B, 1, scalar)
         turn_h(EXPERT[1])
-        quantize_x(CHUNK_B, 0)
-        first_layer(CHUNK_B, 0)
-        gather_x(CHUNK_B, 2)
-        group_x(CHUNK_B, 2, scalar)
-        quantize_x(CHUNK_B, 1)
-
-        gather_x(CHUNK_C, 0)
-        second_layer(EXPERT[0])
-        group_x(CHUNK_C, 0, scalar)
-        first_layer(CHUNK_B, 1)
-        quantize_x(CHUNK_B, 2)
-        first_layer(CHUNK_B, 2)
-        keep_y(EXPERT[0], scalar)
-        gather_x(CHUNK_C, 1)
+        fetch(CHUNK_B, 1)
+        multiply(CHUNK_B, 0)
+        group_h(EXPERT[0], scalar)
+        group_h(EXPERT[1], scalar)
+        fetch(CHUNK_B, 2)
+        multiply(CHUNK_B, 1)
+        fetch(CHUNK_C, 0)
+        multiply(CHUNK_B, 2)
         relu(4 * P, scalar)
-        quantize_x(CHUNK_C, 0)
         relu(5 * P, scalar)
         relu(6 * P, scalar)
-        group_x(CHUNK_C, 1, scalar)
-        first_layer(CHUNK_C, 0)
-        second_layer(EXPERT[1])
-        relu(7 * P, scalar)
-        gather_x(BLOCK_8, 2)
-        quantize_x(CHUNK_C, 1)
-        gather_x(BLOCK_9, 2)
-
-        group_x(BLOCK_8, 2, scalar)
-        quantize_x(BLOCK_8, 2)
         turn_h(EXPERT[2])
-        group_x(BLOCK_9, 2, vector)
+        fetch(CHUNK_C, 1)
+        multiply(CHUNK_C, 0)
+        relu(7 * P, scalar)
+        fetch(BLOCK_8, 2)
         turn_h(EXPERT[3])
-        first_layer(CHUNK_C, 1)
-        first_layer(BLOCK_8, 2)
-        quantize_x(BLOCK_9, 2)
-        second_layer(EXPERT[2])
-        keep_y(EXPERT[1], scalar)
-        second_layer(EXPERT[3])
+        multiply(CHUNK_C, 1)
+        group_h(EXPERT[2], scalar)
+        fetch(BLOCK_9, 2)
+        multiply(BLOCK_8, 2)
+        quantize_h(EXPERT[0])
+        quantize_h(EXPERT[1])
+        second_layer(EXPERT[0:2], 0)
+        multiply(BLOCK_9, 2)
         relu(BLOCK_8[0], scalar)
+        keep_y(EXPERT[0], 0, scalar)
+        group_h(EXPERT[3], vector)
+        relu_by_quarters(BLOCK_9[0])
+        quantize_h(EXPERT[2])
+        quantize_h(EXPERT[3])
+        keep_y(EXPERT[1], 0, vector)
         turn_h(BLOCK_8)
-        keep_y(EXPERT[2], scalar)
-        first_layer(BLOCK_9, 2)
-        relu(BLOCK_9[0], vector)
+        group_h(BLOCK_8, scalar)
         turn_h(BLOCK_9)
-        second_layer(BLOCK_8)
-        second_layer(BLOCK_9)
-        keep_y(EXPERT[3], vector)
-        for b in range(N // P):
-            nc.scalar.copy(y_all[:, b, BLOCK_9[0] : S], y_banks[BLOCK_9[0]][:, b, :])
-        keep_y(BLOCK_8, vector)
+        group_h(BLOCK_9, scalar)
+        second_layer(EXPERT[2:4], 0)
+        keep_y(CHUNK_B, 0, scalar)
+        quantize_h(BLOCK_8)
+        second_layer([BLOCK_8], 0)
+        keep_y(BLOCK_8, 0, scalar)
+        quantize_h(BLOCK_9)
+        second_layer([BLOCK_9], 0)
+        keep_y(BLOCK_9, 0, scalar)
+        for chunk, parts in ((CHUNK_A, EXPERT[0:2]), (CHUNK_B, EXPERT[2:4]), (CHUNK_C, [BLOCK_8, BLOCK_9])):
+            second_layer(parts, 1)
+            keep_y(chunk, 1, scalar)
 
-        pieces = ((0, 0, T, nc.gpsimd), (1, 0, GPSIMD_TOKENS, nc.gpsimd), (1, GPSIMD_TOKENS, T - GPSIMD_TOKENS, vector))
-        for b, t0, width, adder in pieces:
-            first = fetch_y(b, first_slots, t0, width)
-            second = fetch_y(b, second_slots, t0, width)
-            total = codes.tile([P, width], F32, name="total", bufs=len(pieces), align_bytes=64)
-            adder.tensor_tensor(total[:], first[:], second[:], ADD)
+        firsts = []
+        for b in range(N // P):
+            first = ring_tile(vector, [P, T], F32, "first")
+            nc.vector.tensor_copy(first[:], y_half[b][:].indirect(first_slots[:]))
+            firsts.append(first)
+        for b, t0, width in ((0, 0, T), (1, 0, T - LAST_STORE), (1, T - LAST_STORE, LAST_STORE)):
+            total = ring_tile(vector, [P, width], F32, "total")
+            offsets = second_slots[:, t0 // LIST_COLUMN : (t0 + width) // LIST_COLUMN]
+            nc.vector.tensor_tensor(total[:], y_half[b][:].indirect(offsets), firsts[b][:, t0 : t0 + width], ADD)
             nc.sync.dma_start(out[b * P : (b + 1) * P, t0 : t0 + width], total[:])

@@ -32,6 +32,7 @@ BLOCK_8, BLOCK_9 = (1024, P), (1152, P)
 EXPERT = [(e * C, C) for e in range(E)]
 FIRST_GATHER = 192
 LAST_STORE = 256
+LAST_GATHER = 96
 VECTOR_RING, SCALAR_RING, CODE_RING, PSUM_BANKS = 10, 12, 10, 8
 
 
@@ -106,24 +107,20 @@ def tile_moe_pre_mlp_relu_kernel(
                     nc.vector.tensor_tensor(gathered[:, d, c0:c1], tokens[g][d][:].indirect(offsets), gates[:, s0 + c0 : s0 + c1], MULT)
             x_gathered[s0, g] = gathered
 
-        def group_x(slots, g, engine):
+        def group_x(slots, g, chunk):
             s0, width = slots
-            grouped = ring_tile(engine, [P, width, PACK], BF16, "x_grouped")
-            dst = grouped[:].rearrange("p (c i) d -> p c d i", i=4)
-            src = x_gathered[s0, g][:].rearrange("p d (c i) -> p c d i", i=4)
-            if engine is nc.vector:
-                nc.vector.tensor_copy(dst, src)
-            else:
-                nc.scalar.activation(dst, src, COPY)
-            x_grouped[s0, g] = grouped
+            if s0 == chunk[0]:
+                x_grouped[chunk, g] = ring_tile(nc.scalar, [P, chunk[1], PACK], BF16, "x_grouped")
+            dst = x_grouped[chunk, g][:, s0 - chunk[0] : s0 - chunk[0] + width, :].rearrange("p (c i) d -> p c d i", i=4)
+            nc.scalar.activation(dst, x_gathered[s0, g][:].rearrange("p d (c i) -> p c d i", i=4), COPY)
 
-        def quantize_x(slots, g):
+        def quantize_x(slots, g, chunk):
             s0, width = slots
             x_codes = codes.tile([P, width], U32, name="x_codes", align_bytes=64)
             x_plane = ring_tile(nc.vector, [P, width], U8, "x_plane")
             for c0 in range(0, width, P):
                 x_operand[s0 + c0, g] = (x_codes[:, c0 : c0 + P], x_plane[:, c0 : c0 + P])
-            nc.vector.quantize_mx(out=x_codes[:].bitcast(FP8X4), scales=x_plane[:], in_=x_grouped[s0, g][:].rearrange("p c d -> p (c d)"))
+            nc.vector.quantize_mx(out=x_codes[:].bitcast(FP8X4), scales=x_plane[:], in_=x_grouped[chunk, g][:, s0 - chunk[0] : s0 - chunk[0] + width, :].rearrange("p c d -> p (c d)"))
 
         def first_layer(slots, g):
             s0, width = slots
@@ -204,13 +201,13 @@ def tile_moe_pre_mlp_relu_kernel(
 
         vector, scalar = nc.vector, nc.scalar
 
-        def multiply(slots, g):
-            quantize_x(slots, g)
+        def multiply(slots, g, chunk=None):
+            quantize_x(slots, g, chunk or slots)
             first_layer(slots, g)
 
-        def fetch(slots, g, first_cut=None):
+        def fetch(slots, g, first_cut=None, chunk=None):
             gather_x(slots, g, first_cut)
-            group_x(slots, g, scalar)
+            group_x(slots, g, chunk or slots)
 
         fetch(CHUNK_A, 0, FIRST_GATHER)
         fetch(CHUNK_A, 1)
@@ -238,20 +235,20 @@ def tile_moe_pre_mlp_relu_kernel(
         fetch(CHUNK_C, 1)
         multiply(CHUNK_C, 0)
         relu(7 * P, scalar)
-        fetch(BLOCK_8, 2)
+        group_h(EXPERT[2], scalar)
+        fetch((CHUNK_C[0], C - LAST_GATHER), 2, chunk=CHUNK_C)
         turn_h(EXPERT[3])
         multiply(CHUNK_C, 1)
-        group_h(EXPERT[2], scalar)
-        fetch(BLOCK_9, 2)
-        multiply(BLOCK_8, 2)
+        fetch((S - LAST_GATHER, LAST_GATHER), 2, chunk=CHUNK_C)
         quantize_h(EXPERT[0])
+        multiply(BLOCK_8, 2, CHUNK_C)
         quantize_h(EXPERT[1])
         second_layer(EXPERT[0:2], 0)
-        multiply(BLOCK_9, 2)
+        multiply(BLOCK_9, 2, CHUNK_C)
         relu(BLOCK_8[0], scalar)
-        keep_y(EXPERT[0], 0, scalar)
         group_h(EXPERT[3], vector)
         relu_by_quarters(BLOCK_9[0])
+        keep_y(EXPERT[0], 0, scalar)
         quantize_h(EXPERT[2])
         quantize_h(EXPERT[3])
         keep_y(EXPERT[1], 0, vector)
@@ -271,13 +268,24 @@ def tile_moe_pre_mlp_relu_kernel(
             second_layer(parts, 1)
             keep_y(chunk, 1, scalar)
 
-        firsts = []
-        for b in range(N // P):
-            first = ring_tile(vector, [P, T], F32, "first")
-            nc.vector.tensor_copy(first[:], y_half[b][:].indirect(first_slots[:]))
-            firsts.append(first)
-        for b, t0, width in ((0, 0, T), (1, 0, T - LAST_STORE), (1, T - LAST_STORE, LAST_STORE)):
-            total = ring_tile(vector, [P, width], F32, "total")
-            offsets = second_slots[:, t0 // LIST_COLUMN : (t0 + width) // LIST_COLUMN]
-            nc.vector.tensor_tensor(total[:], y_half[b][:].indirect(offsets), firsts[b][:, t0 : t0 + width], ADD)
-            nc.sync.dma_start(out[b * P : (b + 1) * P, t0 : t0 + width], total[:])
+        firsts = {}
+
+        def fetch_first(b, t0, t1):
+            if t0 == 0:
+                firsts[b] = ring_tile(vector, [P, T], F32, "first")
+            nc.vector.tensor_copy(firsts[b][:, t0:t1], y_half[b][:].indirect(first_slots[:, t0 // LIST_COLUMN : t1 // LIST_COLUMN]))
+
+        def add_second(b, t0, t1):
+            total = ring_tile(vector, [P, t1 - t0], F32, "total")
+            offsets = second_slots[:, t0 // LIST_COLUMN : t1 // LIST_COLUMN]
+            nc.vector.tensor_tensor(total[:], y_half[b][:].indirect(offsets), firsts[b][:, t0:t1], ADD)
+            nc.sync.dma_start(out[b * P : (b + 1) * P, t0:t1], total[:])
+
+        cut = T - LAST_STORE
+        fetch_first(0, 0, cut)
+        fetch_first(0, cut, T)
+        add_second(0, 0, cut)
+        fetch_first(1, 0, T)
+        add_second(0, cut, T)
+        add_second(1, 0, cut)
+        add_second(1, cut, T)

@@ -28,11 +28,12 @@ COPY = mybir.ActivationFunctionType.Copy
 RELU = mybir.ActivationFunctionType.Relu
 
 CHUNK_A, CHUNK_B, CHUNK_C = (0, 512), (512, 512), (1024, 256)
-BLOCK_8, BLOCK_9 = (1024, P), (1152, P)
 EXPERT = [(e * C, C) for e in range(E)]
+BLOCK_8, BLOCK_9 = (1024, P), (1152, P)
 FIRST_GATHER = 192
-LAST_STORE = 256
 LAST_GATHER = 96
+C_FRONT, C_BACK = (CHUNK_C[0], C - LAST_GATHER), (S - LAST_GATHER, LAST_GATHER)
+LAST_STORE = 256
 VECTOR_RING, SCALAR_RING, CODE_RING, PSUM_BANKS = 10, 12, 10, 8
 
 
@@ -95,36 +96,32 @@ def tile_moe_pre_mlp_relu_kernel(
         nc.sync.dma_start(first_slots[:], pos1)
         nc.sync.dma_start(second_slots[:], pos2)
 
-        x_gathered, x_grouped, x_operand, a_banks, h_rows, h_turned, h_grouped, h_operand, y_banks = {}, {}, {}, {}, {}, {}, {}, {}, {}
+        x_grouped, a_banks = {}, {}
+        h_rows, h_turned, h_grouped, h_operand = {}, {}, {}, {}
+        y_banks, first_results = {}, {}
+        vector, scalar = nc.vector, nc.scalar
 
-        def gather_x(slots, g, first_cut=None):
+        def fetch_x(slots, g, chunk, first_cut=None):
             s0, width = slots
-            gathered = ring_tile(nc.vector, [P, PACK, width], F32, "gathered")
+            gathered = ring_tile(vector, [P, PACK, width], F32, "gathered")
             for d in range(PACK):
                 cuts = [0, first_cut, width] if first_cut and d == 0 else [0, width]
                 for c0, c1 in zip(cuts, cuts[1:]):
                     offsets = slot_tokens[:, (s0 + c0) // LIST_COLUMN : (s0 + c1) // LIST_COLUMN]
                     nc.vector.tensor_tensor(gathered[:, d, c0:c1], tokens[g][d][:].indirect(offsets), gates[:, s0 + c0 : s0 + c1], MULT)
-            x_gathered[s0, g] = gathered
-
-        def group_x(slots, g, chunk):
-            s0, width = slots
             if s0 == chunk[0]:
-                x_grouped[chunk, g] = ring_tile(nc.scalar, [P, chunk[1], PACK], BF16, "x_grouped")
-            dst = x_grouped[chunk, g][:, s0 - chunk[0] : s0 - chunk[0] + width, :].rearrange("p (c i) d -> p c d i", i=4)
-            nc.scalar.activation(dst, x_gathered[s0, g][:].rearrange("p d (c i) -> p c d i", i=4), COPY)
+                x_grouped[chunk, g] = ring_tile(scalar, [P, chunk[1], PACK], BF16, "x_grouped")
+            grouped = x_grouped[chunk, g][:, s0 - chunk[0] : s0 - chunk[0] + width, :]
+            nc.scalar.activation(grouped.rearrange("p (c i) d -> p c d i", i=4), gathered[:].rearrange("p d (c i) -> p c d i", i=4), COPY)
 
-        def quantize_x(slots, g, chunk):
+        def first_layer(slots, g, chunk):
             s0, width = slots
             x_codes = codes.tile([P, width], U32, name="x_codes", align_bytes=64)
-            x_plane = ring_tile(nc.vector, [P, width], U8, "x_plane")
+            x_plane = ring_tile(vector, [P, width], U8, "x_plane")
+            grouped = x_grouped[chunk, g][:, s0 - chunk[0] : s0 - chunk[0] + width, :]
+            nc.vector.quantize_mx(out=x_codes[:].bitcast(FP8X4), scales=x_plane[:], in_=grouped.rearrange("p c d -> p (c d)"))
             for c0 in range(0, width, P):
-                x_operand[s0 + c0, g] = (x_codes[:, c0 : c0 + P], x_plane[:, c0 : c0 + P])
-            nc.vector.quantize_mx(out=x_codes[:].bitcast(FP8X4), scales=x_plane[:], in_=x_grouped[chunk, g][:, s0 - chunk[0] : s0 - chunk[0] + width, :].rearrange("p c d -> p (c d)"))
-
-        def first_layer(slots, g):
-            s0, width = slots
-            for b0 in range(s0, s0 + width, P):
+                b0 = s0 + c0
                 e = b0 // C
                 columns = P if b0 == BLOCK_9[0] else H
                 for i0 in range(0, H, columns):
@@ -132,28 +129,28 @@ def tile_moe_pre_mlp_relu_kernel(
                         a_banks[b0, i0] = psum.tile([P, columns], F32, name="a_bank", tag="bank")
                     nc.tensor.matmul_mx(
                         out=a_banks[b0, i0][:],
-                        lhsT=x_operand[b0, g][0].bitcast(FP8X4),
-                        lhsT_scale=x_operand[b0, g][1],
+                        lhsT=x_codes[:, c0 : c0 + P].bitcast(FP8X4),
+                        lhsT_scale=x_plane[:, c0 : c0 + P],
                         rhs=w1_codes[e][:, g, 2 * i0 : 2 * (i0 + columns)].bitcast(FP4X4),
                         rhs_scale=w1_plane[:, e * PASSES + g, i0 : i0 + columns],
                         start=(g == 0),
                         stop=(g == PASSES - 1),
                     )
 
-        def relu(b0, engine):
-            rows = ring_tile(engine, [P, 2, P, 2], BF16, "h_rows")
+        def relu(b0):
+            rows = ring_tile(scalar, [P, 2, P, 2], BF16, "h_rows")
             nc.scalar.activation(rows[:], a_banks[b0, 0][:].rearrange("s (p u v) -> s u p v", u=2, v=2), RELU)
             h_rows[b0] = rows
 
         def relu_by_quarters(b0):
-            rows = ring_tile(nc.vector, [P, 2, P, 2], BF16, "h_rows")
-            for i0 in range(0, H, P):
-                dst = rows[:, :, i0 // PACK : (i0 + P) // PACK, :]
+            rows = ring_tile(vector, [P, 2, P, 2], BF16, "h_rows")
+            for quarter, i0 in enumerate(range(0, H, P)):
+                part = rows[:, :, i0 // PACK : (i0 + P) // PACK, :]
                 sums = a_banks[b0, i0][:].rearrange("s (p u v) -> s u p v", u=2, v=2)
-                if i0 < H // 2:
-                    nc.vector.tensor_scalar_max(dst, sums, 0.0)
+                if quarter % 2 == 0:
+                    nc.vector.tensor_scalar_max(part, sums, 0.0)
                 else:
-                    nc.scalar.activation(dst, sums, RELU)
+                    nc.scalar.activation(part, sums, RELU)
             h_rows[b0] = rows
 
         def turn_h(slots):
@@ -174,7 +171,7 @@ def tile_moe_pre_mlp_relu_kernel(
         def quantize_h(slots):
             s0, width = slots
             h_codes = codes.tile([P, width], U32, name="h_codes", align_bytes=64)
-            h_plane = ring_tile(nc.vector, [P, width], U8, "h_plane")
+            h_plane = ring_tile(vector, [P, width], U8, "h_plane")
             nc.vector.quantize_mx(out=h_codes[:].bitcast(FP8X4), scales=h_plane[:], in_=h_grouped[s0][:])
             h_operand[s0] = (h_codes, h_plane)
 
@@ -199,87 +196,74 @@ def tile_moe_pre_mlp_relu_kernel(
             y_bank, c0 = y_banks[s0, b]
             copy(engine, y_half[b][:, s0 : s0 + width], y_bank[:, c0 : c0 + width])
 
-        vector, scalar = nc.vector, nc.scalar
-
-        def multiply(slots, g, chunk=None):
-            quantize_x(slots, g, chunk or slots)
-            first_layer(slots, g)
-
-        def fetch(slots, g, first_cut=None, chunk=None):
-            gather_x(slots, g, first_cut)
-            group_x(slots, g, chunk or slots)
-
-        fetch(CHUNK_A, 0, FIRST_GATHER)
-        fetch(CHUNK_A, 1)
-        multiply(CHUNK_A, 0)
-        fetch(CHUNK_A, 2)
-        multiply(CHUNK_A, 1)
-        fetch(CHUNK_B, 0)
-        multiply(CHUNK_A, 2)
-        for b0 in range(0, end_a, P):
-            relu(b0, scalar)
-        turn_h(EXPERT[0])
-        turn_h(EXPERT[1])
-        fetch(CHUNK_B, 1)
-        multiply(CHUNK_B, 0)
-        group_h(EXPERT[0], scalar)
-        group_h(EXPERT[1], scalar)
-        fetch(CHUNK_B, 2)
-        multiply(CHUNK_B, 1)
-        fetch(CHUNK_C, 0)
-        multiply(CHUNK_B, 2)
-        relu(4 * P, scalar)
-        relu(5 * P, scalar)
-        relu(6 * P, scalar)
-        turn_h(EXPERT[2])
-        fetch(CHUNK_C, 1)
-        multiply(CHUNK_C, 0)
-        relu(7 * P, scalar)
-        group_h(EXPERT[2], scalar)
-        fetch((CHUNK_C[0], C - LAST_GATHER), 2, chunk=CHUNK_C)
-        turn_h(EXPERT[3])
-        multiply(CHUNK_C, 1)
-        fetch((S - LAST_GATHER, LAST_GATHER), 2, chunk=CHUNK_C)
-        quantize_h(EXPERT[0])
-        multiply(BLOCK_8, 2, CHUNK_C)
-        quantize_h(EXPERT[1])
-        second_layer(EXPERT[0:2], 0)
-        multiply(BLOCK_9, 2, CHUNK_C)
-        relu(BLOCK_8[0], scalar)
-        group_h(EXPERT[3], vector)
-        relu_by_quarters(BLOCK_9[0])
-        keep_y(EXPERT[0], 0, scalar)
-        quantize_h(EXPERT[2])
-        quantize_h(EXPERT[3])
-        keep_y(EXPERT[1], 0, vector)
-        turn_h(BLOCK_8)
-        group_h(BLOCK_8, scalar)
-        turn_h(BLOCK_9)
-        group_h(BLOCK_9, scalar)
-        second_layer(EXPERT[2:4], 0)
-        keep_y(CHUNK_B, 0, scalar)
-        quantize_h(BLOCK_8)
-        second_layer([BLOCK_8], 0)
-        keep_y(BLOCK_8, 0, scalar)
-        quantize_h(BLOCK_9)
-        second_layer([BLOCK_9], 0)
-        keep_y(BLOCK_9, 0, scalar)
-        for chunk, parts in ((CHUNK_A, EXPERT[0:2]), (CHUNK_B, EXPERT[2:4]), (CHUNK_C, [BLOCK_8, BLOCK_9])):
-            second_layer(parts, 1)
-            keep_y(chunk, 1, scalar)
-
-        firsts = {}
-
         def fetch_first(b, t0, t1):
             if t0 == 0:
-                firsts[b] = ring_tile(vector, [P, T], F32, "first")
-            nc.vector.tensor_copy(firsts[b][:, t0:t1], y_half[b][:].indirect(first_slots[:, t0 // LIST_COLUMN : t1 // LIST_COLUMN]))
+                first_results[b] = ring_tile(vector, [P, T], F32, "first_result")
+            offsets = first_slots[:, t0 // LIST_COLUMN : t1 // LIST_COLUMN]
+            nc.vector.tensor_copy(first_results[b][:, t0:t1], y_half[b][:].indirect(offsets))
 
         def add_second(b, t0, t1):
             total = ring_tile(vector, [P, t1 - t0], F32, "total")
             offsets = second_slots[:, t0 // LIST_COLUMN : t1 // LIST_COLUMN]
-            nc.vector.tensor_tensor(total[:], y_half[b][:].indirect(offsets), firsts[b][:, t0:t1], ADD)
+            nc.vector.tensor_tensor(total[:], y_half[b][:].indirect(offsets), first_results[b][:, t0:t1], ADD)
             nc.sync.dma_start(out[b * P : (b + 1) * P, t0:t1], total[:])
+
+        fetch_x(CHUNK_A, 0, CHUNK_A, FIRST_GATHER)
+        for g in range(1, PASSES):
+            fetch_x(CHUNK_A, g, CHUNK_A)
+            first_layer(CHUNK_A, g - 1, CHUNK_A)
+        fetch_x(CHUNK_B, 0, CHUNK_B)
+        first_layer(CHUNK_A, PASSES - 1, CHUNK_A)
+        for b0 in range(0, end_a, P):
+            relu(b0)
+        for slots in EXPERT[0:2]:
+            turn_h(slots)
+        fetch_x(CHUNK_B, 1, CHUNK_B)
+        first_layer(CHUNK_B, 0, CHUNK_B)
+        for slots in EXPERT[0:2]:
+            group_h(slots, scalar)
+        fetch_x(CHUNK_B, 2, CHUNK_B)
+        first_layer(CHUNK_B, 1, CHUNK_B)
+        fetch_x(CHUNK_C, 0, CHUNK_C)
+        first_layer(CHUNK_B, 2, CHUNK_B)
+        last_of_b = CHUNK_C[0] - P
+        for b0 in range(end_a, last_of_b, P):
+            relu(b0)
+        turn_h(EXPERT[2])
+        fetch_x(CHUNK_C, 1, CHUNK_C)
+        first_layer(CHUNK_C, 0, CHUNK_C)
+        relu(last_of_b)
+        fetch_x(C_FRONT, 2, CHUNK_C)
+        turn_h(EXPERT[3])
+        first_layer(CHUNK_C, 1, CHUNK_C)
+        fetch_x(C_BACK, 2, CHUNK_C)
+
+        first_layer(BLOCK_8, 2, CHUNK_C)
+        for slots in EXPERT[0:2]:
+            quantize_h(slots)
+        second_layer(EXPERT[0:2], 0)
+        first_layer(BLOCK_9, 2, CHUNK_C)
+        group_h(EXPERT[2], scalar)
+        relu(BLOCK_8[0])
+        group_h(EXPERT[3], vector)
+        relu_by_quarters(BLOCK_9[0])
+        keep_y(EXPERT[0], 0, scalar)
+        for slots in EXPERT[2:4]:
+            quantize_h(slots)
+        keep_y(EXPERT[1], 0, vector)
+        for block in (BLOCK_8, BLOCK_9):
+            turn_h(block)
+            group_h(block, scalar)
+        second_layer(EXPERT[2:4], 0)
+        keep_y(CHUNK_B, 0, scalar)
+        for block in (BLOCK_8, BLOCK_9):
+            quantize_h(block)
+            second_layer([block], 0)
+            keep_y(block, 0, scalar)
+
+        for chunk, parts in ((CHUNK_A, EXPERT[0:2]), (CHUNK_B, EXPERT[2:4]), (CHUNK_C, [BLOCK_8, BLOCK_9])):
+            second_layer(parts, 1)
+            keep_y(chunk, 1, scalar)
 
         cut = T - LAST_STORE
         fetch_first(0, 0, cut)

@@ -86,13 +86,12 @@ def tile_moe_pre_mlp_relu_kernel(
             nc.sync.dma_start(tokens[g][d][:], x_rows[g, d])
         nc.sync.dma_start(gates[:, end_a:S], gate[0:P, end_a:S])
         for plane, scales in ((w1_plane, w1_scales), (w2_plane, w2_scales)):
-            rows = scales.rearrange("e s q i -> q (e s) i").bitcast(I32)
+            scale_rows = scales.rearrange("e s q i -> q (e s) i").bitcast(I32)
             for quad in range(P // QUADRANT):
-                nc.sync.dma_start(plane[QUADRANT * quad : QUADRANT * quad + 4].bitcast(I32), rows[4 * quad : 4 * quad + 4])
+                nc.sync.dma_start(plane[QUADRANT * quad : QUADRANT * quad + 4].bitcast(I32), scale_rows[4 * quad : 4 * quad + 4])
         for e in range(E):
             nc.sync.dma_start(w1_codes[e][:].bitcast(I32), w1_words[e].rearrange("s p b -> p s b").bitcast(I32))
-            if (e + 1) * C == end_a:
-                nc.sync.dma_start(w2_codes[:].bitcast(I32), w2_words.rearrange("e s p b -> p (e s) b").bitcast(I32))
+        nc.sync.dma_start(w2_codes[:].bitcast(I32), w2_words.rearrange("e s p b -> p (e s) b").bitcast(I32))
         nc.sync.dma_start(first_slots[:], pos1)
         nc.sync.dma_start(second_slots[:], pos2)
 
@@ -145,12 +144,12 @@ def tile_moe_pre_mlp_relu_kernel(
         def relu_by_quarters(b0):
             rows = ring_tile(vector, [P, 2, P, 2], BF16, "h_rows")
             for quarter, i0 in enumerate(range(0, H, P)):
-                part = rows[:, :, i0 // PACK : (i0 + P) // PACK, :]
+                quarter_rows = rows[:, :, i0 // PACK : (i0 + P) // PACK, :]
                 sums = a_banks[b0, i0][:].rearrange("s (p u v) -> s u p v", u=2, v=2)
                 if quarter % 2 == 0:
-                    nc.vector.tensor_scalar_max(part, sums, 0.0)
+                    nc.vector.tensor_scalar_max(quarter_rows, sums, 0.0)
                 else:
-                    nc.scalar.activation(part, sums, RELU)
+                    nc.scalar.activation(quarter_rows, sums, RELU)
             h_rows[b0] = rows
 
         def turn_h(slots):
@@ -177,19 +176,19 @@ def tile_moe_pre_mlp_relu_kernel(
 
         def second_layer(parts, b):
             s0 = parts[0][0]
-            y_bank = psum.tile([P, sum(width for first, width in parts)], F32, name="y_bank", tag="bank")
-            for first, width in parts:
-                e = first // C
+            y_bank = psum.tile([P, sum(width for r0, width in parts)], F32, name="y_bank", tag="bank")
+            for r0, width in parts:
+                e = r0 // C
                 nc.tensor.matmul_mx(
-                    out=y_bank[:, first - s0 : first - s0 + width],
+                    out=y_bank[:, r0 - s0 : r0 - s0 + width],
                     lhsT=w2_codes[:, e, 2 * b * P : 2 * (b + 1) * P].bitcast(FP4X4),
                     lhsT_scale=w2_plane[:, e, b * P : (b + 1) * P],
-                    rhs=h_operand[first][0][:].bitcast(FP8X4),
-                    rhs_scale=h_operand[first][1][:],
+                    rhs=h_operand[r0][0][:].bitcast(FP8X4),
+                    rhs_scale=h_operand[r0][1][:],
                     start=True,
                     stop=True,
                 )
-                y_banks[first, b] = (y_bank, first - s0)
+                y_banks[r0, b] = (y_bank, r0 - s0)
 
         def keep_y(slots, b, engine):
             s0, width = slots

@@ -257,8 +257,9 @@ def tile_moe_pre_mlp_relu_kernel(
         keep_y(CHUNK_B, 0, scalar)
         for block in (BLOCK_8, BLOCK_9):
             quantize_h(block)
+        for block, engine in ((BLOCK_8, vector), (BLOCK_9, scalar)):
             second_layer([block], 0)
-            keep_y(block, 0, scalar)
+            keep_y(block, 0, engine)
 
         for chunk, parts in ((CHUNK_A, EXPERT[0:2]), (CHUNK_B, EXPERT[2:4]), (CHUNK_C, [BLOCK_8, BLOCK_9])):
             second_layer(parts, 1)

@@ -95,12 +95,12 @@ def tile_moe_pre_mlp_relu_kernel(
         nc.sync.dma_start(first_slots[:], pos1)
         nc.sync.dma_start(second_slots[:], pos2)
 
-        x_grouped, a_banks = {}, {}
+        x_gathered, x_grouped, a_banks = {}, {}, {}
         h_rows, h_turned, h_grouped, h_operand = {}, {}, {}, {}
         y_banks, first_results = {}, {}
         vector, scalar = nc.vector, nc.scalar
 
-        def fetch_x(slots, g, chunk, first_cut=None):
+        def gather_x(slots, g, first_cut=None):
             s0, width = slots
             gathered = ring_tile(vector, [P, PACK, width], F32, "gathered")
             for d in range(PACK):
@@ -108,10 +108,22 @@ def tile_moe_pre_mlp_relu_kernel(
                 for c0, c1 in zip(cuts, cuts[1:]):
                     offsets = slot_tokens[:, (s0 + c0) // LIST_COLUMN : (s0 + c1) // LIST_COLUMN]
                     nc.vector.tensor_tensor(gathered[:, d, c0:c1], tokens[g][d][:].indirect(offsets), gates[:, s0 + c0 : s0 + c1], MULT)
-            if s0 == chunk[0]:
-                x_grouped[chunk, g] = ring_tile(scalar, [P, chunk[1], PACK], BF16, "x_grouped")
-            grouped = x_grouped[chunk, g][:, s0 - chunk[0] : s0 - chunk[0] + width, :]
-            nc.scalar.activation(grouped.rearrange("p (c i) d -> p c d i", i=4), gathered[:].rearrange("p d (c i) -> p c d i", i=4), COPY)
+            x_gathered[slots, g] = gathered
+
+        def group_x(part, g, slots, chunk, engine):
+            s0, width = part
+            if (chunk, g) not in x_grouped:
+                x_grouped[chunk, g] = ring_tile(engine, [P, chunk[1], PACK], BF16, "x_grouped")
+            grouped = x_grouped[chunk, g][:, s0 - chunk[0] : s0 - chunk[0] + width, :].rearrange("p (c i) d -> p c d i", i=4)
+            planes = x_gathered[slots, g][:, :, s0 - slots[0] : s0 - slots[0] + width].rearrange("p d (c i) -> p c d i", i=4)
+            if engine is nc.vector:
+                nc.vector.tensor_copy(grouped, planes)
+            else:
+                nc.scalar.activation(grouped, planes, COPY)
+
+        def fetch_x(slots, g, chunk, first_cut=None):
+            gather_x(slots, g, first_cut)
+            group_x(slots, g, slots, chunk, scalar)
 
         def first_layer(slots, g, chunk):
             s0, width = slots
@@ -232,32 +244,37 @@ def tile_moe_pre_mlp_relu_kernel(
         fetch_x(CHUNK_C, 1, CHUNK_C)
         first_layer(CHUNK_C, 0, CHUNK_C)
         relu(last_of_b)
-        fetch_x(C_FRONT, 2, CHUNK_C)
+        gather_x(C_FRONT, 2)
+        group_x(BLOCK_8, 2, C_FRONT, BLOCK_8, scalar)
         turn_h(EXPERT[3])
         first_layer(CHUNK_C, 1, CHUNK_C)
-        fetch_x(C_BACK, 2, CHUNK_C)
+        gather_x(C_BACK, 2)
 
-        first_layer(BLOCK_8, 2, CHUNK_C)
-        for slots in EXPERT[0:2]:
-            quantize_h(slots)
-        second_layer(EXPERT[0:2], 0)
-        first_layer(BLOCK_9, 2, CHUNK_C)
         group_h(EXPERT[2], scalar)
+        first_layer(BLOCK_8, 2, BLOCK_8)
+        group_x(C_BACK, 2, C_BACK, BLOCK_9, vector)
+        group_x((BLOCK_9[0], P - LAST_GATHER), 2, C_FRONT, BLOCK_9, scalar)
+        group_h(EXPERT[3], scalar)
+        quantize_h(EXPERT[0])
+        first_layer(BLOCK_9, 2, BLOCK_9)
+        second_layer(EXPERT[0:1], 0)
         relu(BLOCK_8[0])
-        group_h(EXPERT[3], vector)
-        relu_by_quarters(BLOCK_9[0])
-        keep_y(EXPERT[0], 0, scalar)
-        for slots in EXPERT[2:4]:
+        for slots in EXPERT[1:3]:
             quantize_h(slots)
-        keep_y(EXPERT[1], 0, vector)
-        for block in (BLOCK_8, BLOCK_9):
-            turn_h(block)
-            group_h(block, scalar)
+        second_layer(EXPERT[1:2], 0)
+        relu_by_quarters(BLOCK_9[0])
+        turn_h(BLOCK_8)
+        quantize_h(EXPERT[3])
+        keep_y(EXPERT[0], 0, vector)
+        keep_y(EXPERT[1], 0, scalar)
+        group_h(BLOCK_8, scalar)
+        turn_h(BLOCK_9)
         second_layer(EXPERT[2:4], 0)
-        keep_y(CHUNK_B, 0, scalar)
+        group_h(BLOCK_9, vector)
         for block in (BLOCK_8, BLOCK_9):
             quantize_h(block)
-        for block, engine in ((BLOCK_8, vector), (BLOCK_9, scalar)):
+        keep_y(CHUNK_B, 0, scalar)
+        for block, engine in ((BLOCK_8, scalar), (BLOCK_9, vector)):
             second_layer([block], 0)
             keep_y(block, 0, engine)
 

@@ -10,6 +10,8 @@ PACK = 4
 PASSES = K // (P * PACK)
 LIST_COLUMN = 16
 QUADRANT = 32
+SCALE_ROWS = 16
+LAST = E - 1
 
 FLOPS = 2 * S * (K * H + H * N)
 BYTES = 4 * K * T + E * (K * H + H * N) // 2 + E * (K * H + H * N) // 32 + 4 * S + 2 * P * (S + 2 * T) // 16 + 4 * N * T
@@ -41,6 +43,7 @@ def tile_moe_pre_mlp_relu_kernel(
     tc, xT, w1_words, w1_scales, w2_words, w2_scales, gate, offs, pos1, pos2, out
 ):
     nc = tc.nc
+    vector, scalar = nc.vector, nc.scalar
     with ExitStack() as ctx:
         keep = ctx.enter_context(tc.tile_pool(name="keep", bufs=1))
         v_ring = ctx.enter_context(tc.tile_pool(name="v_ring", bufs=VECTOR_RING))
@@ -49,15 +52,21 @@ def tile_moe_pre_mlp_relu_kernel(
         psum = ctx.enter_context(tc.psum_pool(name="psum", bufs=PSUM_BANKS))
 
         def ring_tile(engine, shape, dtype, name):
-            if engine is nc.vector:
+            if engine is vector:
                 return v_ring.tile(shape, dtype, name=name, tag="v", align_bytes=64)
             return s_ring.tile(shape, dtype, name=name, tag="s", align_bytes=64)
 
         def copy(engine, dst, src):
-            if engine is nc.vector:
-                nc.vector.tensor_copy(dst, src)
+            if engine is vector:
+                vector.tensor_copy(dst, src)
             else:
-                nc.scalar.copy(dst, src)
+                scalar.copy(dst, src)
+
+        def relu(engine, dst, src):
+            if engine is vector:
+                vector.tensor_scalar_max(dst, src, 0.0)
+            else:
+                scalar.activation(dst, src, RELU)
 
         slot_tokens = keep.tile([P, S // LIST_COLUMN], U16, name="slot_tokens")
         first_slots = keep.tile([P, T // LIST_COLUMN], U16, name="first_slots")
@@ -66,13 +75,15 @@ def tile_moe_pre_mlp_relu_kernel(
         gates = keep.tile([P, S], F32, name="gates", align_bytes=64)
         w1_codes = [keep.tile([P, PASSES, 2 * H], U8, name="w1_codes_%d" % e, align_bytes=64) for e in range(E)]
         w1_plane = keep.tile([P, E * PASSES, H], U8, name="w1_plane", align_bytes=64)
+        last_rows = keep.tile([P, H], U8, name="last_rows", align_bytes=64)
         w2_codes = keep.tile([P, E, 2 * N], U8, name="w2_codes", align_bytes=64)
         w2_plane = keep.tile([P, E, N], U8, name="w2_plane", align_bytes=64)
         identity = keep.tile([P, P], F32, name="identity", align_bytes=64)
         y_half = [keep.tile([P, S], F32, name="y_half_%d" % b, align_bytes=64) for b in range(N // P)]
 
-        nc.vector.memset(w1_plane[:].rearrange("p a b -> p (a b)").bitcast(I32), 0)
-        nc.vector.memset(w2_plane[:].rearrange("p a b -> p (a b)").bitcast(I32), 0)
+        vector.memset(w1_plane[:].rearrange("p a b -> p (a b)").bitcast(I32), 0)
+        vector.memset(w2_plane[:].rearrange("p a b -> p (a b)").bitcast(I32), 0)
+        vector.memset(last_rows[:].bitcast(I32), 0)
         make_identity(nc, identity[:])
 
         x_rows = xT.rearrange("(g p d) t -> g d p t", p=P, d=PACK)
@@ -85,11 +96,15 @@ def tile_moe_pre_mlp_relu_kernel(
             g, d = divmod(row, PACK)
             nc.sync.dma_start(tokens[g][d][:], x_rows[g, d])
         nc.sync.dma_start(gates[:, end_a:S], gate[0:P, end_a:S])
-        for plane, scales in ((w1_plane, w1_scales), (w2_plane, w2_scales)):
-            scale_rows = scales.rearrange("e s q i -> q (e s) i").bitcast(I32)
+        w1_rows = w1_scales[0:LAST].rearrange("e s q i -> q (e s) i").bitcast(I32)
+        w2_rows = w2_scales.rearrange("e s q i -> q (e s) i").bitcast(I32)
+        for plane, scale_rows in ((w1_plane[:, 0 : LAST * PASSES, :], w1_rows), (w2_plane[:], w2_rows)):
             for quad in range(P // QUADRANT):
                 nc.sync.dma_start(plane[QUADRANT * quad : QUADRANT * quad + 4].bitcast(I32), scale_rows[4 * quad : 4 * quad + 4])
-        for e in range(E):
+        rows_of_last = w1_scales[LAST].rearrange("s q i -> (s q) i").bitcast(I32)
+        for r0, r1 in ((0, 2 * SCALE_ROWS), (2 * SCALE_ROWS, PASSES * SCALE_ROWS)):
+            nc.sync.dma_start(last_rows[r0:r1].bitcast(I32), rows_of_last[r0:r1])
+        for e in (0, 1, LAST, 2, 3):
             nc.sync.dma_start(w1_codes[e][:].bitcast(I32), w1_words[e].rearrange("s p b -> p s b").bitcast(I32))
         nc.sync.dma_start(w2_codes[:].bitcast(I32), w2_words.rearrange("e s p b -> p (e s) b").bitcast(I32))
         nc.sync.dma_start(first_slots[:], pos1)
@@ -97,8 +112,24 @@ def tile_moe_pre_mlp_relu_kernel(
 
         x_gathered, x_grouped, a_banks = {}, {}, {}
         h_rows, h_turned, h_grouped, h_operand = {}, {}, {}, {}
-        y_banks, first_results = {}, {}
-        vector, scalar = nc.vector, nc.scalar
+        y_banks, first_results, sorted_words = {}, {}, {}
+
+        def sort_last_words(engine):
+            words = ring_tile(engine, [P, PASSES, 2 * H], U8, "sorted_words")
+            dst = words[:].rearrange("p g b -> p (g b)").bitcast(U16).rearrange("p (g t m) -> p g t m", g=PASSES, t=PACK)
+            src = w1_codes[LAST][:].rearrange("p g b -> p (g b)").bitcast(U16).rearrange("p (g m t) -> p g t m", g=PASSES, t=PACK)
+            copy(engine, dst, src)
+            sorted_words[LAST] = words
+
+        def sort_last_scales():
+            rows = ring_tile(vector, [P, H], U8, "sorted_rows")
+            vector.tensor_copy(rows[:].rearrange("p (t m) -> p t m", t=PACK), last_rows[:].rearrange("p (m t) -> p t m", t=PACK))
+            for g in range(PASSES):
+                for quad in range(P // QUADRANT):
+                    r0 = SCALE_ROWS * g + 4 * quad
+                    nc.sync.dma_start(
+                        w1_plane[QUADRANT * quad : QUADRANT * quad + 4, LAST * PASSES + g, :].bitcast(I32), rows[r0 : r0 + 4].bitcast(I32)
+                    )
 
         def gather_x(slots, g, first_cut=None):
             s0, width = slots
@@ -107,7 +138,7 @@ def tile_moe_pre_mlp_relu_kernel(
                 cuts = [0, first_cut, width] if first_cut and d == 0 else [0, width]
                 for c0, c1 in zip(cuts, cuts[1:]):
                     offsets = slot_tokens[:, (s0 + c0) // LIST_COLUMN : (s0 + c1) // LIST_COLUMN]
-                    nc.vector.tensor_tensor(gathered[:, d, c0:c1], tokens[g][d][:].indirect(offsets), gates[:, s0 + c0 : s0 + c1], MULT)
+                    vector.tensor_tensor(gathered[:, d, c0:c1], tokens[g][d][:].indirect(offsets), gates[:, s0 + c0 : s0 + c1], MULT)
             x_gathered[slots, g] = gathered
 
         def group_x(part, g, slots, chunk, engine):
@@ -116,53 +147,58 @@ def tile_moe_pre_mlp_relu_kernel(
                 x_grouped[chunk, g] = ring_tile(engine, [P, chunk[1], PACK], BF16, "x_grouped")
             grouped = x_grouped[chunk, g][:, s0 - chunk[0] : s0 - chunk[0] + width, :].rearrange("p (c i) d -> p c d i", i=4)
             planes = x_gathered[slots, g][:, :, s0 - slots[0] : s0 - slots[0] + width].rearrange("p d (c i) -> p c d i", i=4)
-            if engine is nc.vector:
-                nc.vector.tensor_copy(grouped, planes)
+            if engine is vector:
+                vector.tensor_copy(grouped, planes)
             else:
-                nc.scalar.activation(grouped, planes, COPY)
+                scalar.activation(grouped, planes, COPY)
 
-        def fetch_x(slots, g, chunk, first_cut=None):
-            gather_x(slots, g, first_cut)
-            group_x(slots, g, slots, chunk, scalar)
+        def fetch_x(chunk, g, first_cut=None):
+            gather_x(chunk, g, first_cut)
+            group_x(chunk, g, chunk, chunk, scalar)
 
-        def first_layer(slots, g, chunk):
-            s0, width = slots
+        def first_layer(chunk, g):
+            s0, width = chunk
             x_codes = codes.tile([P, width], U32, name="x_codes", align_bytes=64)
             x_plane = ring_tile(vector, [P, width], U8, "x_plane")
-            grouped = x_grouped[chunk, g][:, s0 - chunk[0] : s0 - chunk[0] + width, :]
-            nc.vector.quantize_mx(out=x_codes[:].bitcast(FP8X4), scales=x_plane[:], in_=grouped.rearrange("p c d -> p (c d)"))
+            vector.quantize_mx(out=x_codes[:].bitcast(FP8X4), scales=x_plane[:], in_=x_grouped[chunk, g][:].rearrange("p c d -> p (c d)"))
             for c0 in range(0, width, P):
                 b0 = s0 + c0
                 e = b0 // C
-                columns = P if b0 == BLOCK_9[0] else H
-                for i0 in range(0, H, columns):
-                    if g == 0:
-                        a_banks[b0, i0] = psum.tile([P, columns], F32, name="a_bank", tag="bank")
+                x_operand = (x_codes[:, c0 : c0 + P].bitcast(FP8X4), x_plane[:, c0 : c0 + P])
+                if g == 0:
+                    a_banks[b0] = psum.tile([P, H], F32, name="a_bank", tag="bank")
+                if e < LAST:
                     nc.tensor.matmul_mx(
-                        out=a_banks[b0, i0][:],
-                        lhsT=x_codes[:, c0 : c0 + P].bitcast(FP8X4),
-                        lhsT_scale=x_plane[:, c0 : c0 + P],
-                        rhs=w1_codes[e][:, g, 2 * i0 : 2 * (i0 + columns)].bitcast(FP4X4),
-                        rhs_scale=w1_plane[:, e * PASSES + g, i0 : i0 + columns],
+                        out=a_banks[b0][:],
+                        lhsT=x_operand[0],
+                        lhsT_scale=x_operand[1],
+                        rhs=w1_codes[e][:, g, :].bitcast(FP4X4),
+                        rhs_scale=w1_plane[:, e * PASSES + g, :],
                         start=(g == 0),
                         stop=(g == PASSES - 1),
                     )
-
-        def relu(b0):
-            rows = ring_tile(scalar, [P, 2, P, 2], BF16, "h_rows")
-            nc.scalar.activation(rows[:], a_banks[b0, 0][:].rearrange("s (p u v) -> s u p v", u=2, v=2), RELU)
-            h_rows[b0] = rows
-
-        def relu_by_quarters(b0):
-            rows = ring_tile(vector, [P, 2, P, 2], BF16, "h_rows")
-            for quarter, i0 in enumerate(range(0, H, P)):
-                quarter_rows = rows[:, :, i0 // PACK : (i0 + P) // PACK, :]
-                sums = a_banks[b0, i0][:].rearrange("s (p u v) -> s u p v", u=2, v=2)
-                if quarter % 2 == 0:
-                    nc.vector.tensor_scalar_max(quarter_rows, sums, 0.0)
                 else:
-                    nc.scalar.activation(quarter_rows, sums, RELU)
+                    for t in range(PACK):
+                        nc.tensor.matmul_mx(
+                            out=a_banks[b0][:, t * P : (t + 1) * P],
+                            lhsT=sorted_words[e][:, g, 2 * t * P : 2 * (t + 1) * P].bitcast(FP4X4),
+                            lhsT_scale=w1_plane[:, e * PASSES + g, t * P : (t + 1) * P],
+                            rhs=x_operand[0],
+                            rhs_scale=x_operand[1],
+                            start=(g == 0 and t == 0),
+                            stop=(g == PASSES - 1 and t == PACK - 1),
+                        )
+
+        def relu_rows(b0):
+            rows = ring_tile(scalar, [P, 2, P, 2], BF16, "h_rows")
+            relu(scalar, rows[:], a_banks[b0][:].rearrange("s (p u v) -> s u p v", u=2, v=2))
             h_rows[b0] = rows
+
+        def relu_grouped(block, engine):
+            s0, width = block
+            grouped = ring_tile(engine, [P, width * PACK], BF16, "h_grouped")
+            relu(engine, grouped[:].rearrange("p (c i t) -> p c t i", t=PACK, i=2), a_banks[s0][:].rearrange("p (t c i) -> p c t i", t=PACK, i=2))
+            h_grouped[s0] = grouped
 
         def turn_h(slots):
             s0, width = slots
@@ -183,7 +219,7 @@ def tile_moe_pre_mlp_relu_kernel(
             s0, width = slots
             h_codes = codes.tile([P, width], U32, name="h_codes", align_bytes=64)
             h_plane = ring_tile(vector, [P, width], U8, "h_plane")
-            nc.vector.quantize_mx(out=h_codes[:].bitcast(FP8X4), scales=h_plane[:], in_=h_grouped[s0][:])
+            vector.quantize_mx(out=h_codes[:].bitcast(FP8X4), scales=h_plane[:], in_=h_grouped[s0][:])
             h_operand[s0] = (h_codes, h_plane)
 
         def second_layer(parts, b):
@@ -211,70 +247,65 @@ def tile_moe_pre_mlp_relu_kernel(
             if t0 == 0:
                 first_results[b] = ring_tile(vector, [P, T], F32, "first_result")
             offsets = first_slots[:, t0 // LIST_COLUMN : t1 // LIST_COLUMN]
-            nc.vector.tensor_copy(first_results[b][:, t0:t1], y_half[b][:].indirect(offsets))
+            vector.tensor_copy(first_results[b][:, t0:t1], y_half[b][:].indirect(offsets))
 
         def add_second(b, t0, t1):
             total = ring_tile(vector, [P, t1 - t0], F32, "total")
             offsets = second_slots[:, t0 // LIST_COLUMN : t1 // LIST_COLUMN]
-            nc.vector.tensor_tensor(total[:], y_half[b][:].indirect(offsets), first_results[b][:, t0:t1], ADD)
+            vector.tensor_tensor(total[:], y_half[b][:].indirect(offsets), first_results[b][:, t0:t1], ADD)
             nc.sync.dma_start(out[b * P : (b + 1) * P, t0:t1], total[:])
 
-        fetch_x(CHUNK_A, 0, CHUNK_A, FIRST_GATHER)
+        fetch_x(CHUNK_A, 0, FIRST_GATHER)
         for g in range(1, PASSES):
-            fetch_x(CHUNK_A, g, CHUNK_A)
-            first_layer(CHUNK_A, g - 1, CHUNK_A)
-        fetch_x(CHUNK_B, 0, CHUNK_B)
-        first_layer(CHUNK_A, PASSES - 1, CHUNK_A)
+            fetch_x(CHUNK_A, g)
+            first_layer(CHUNK_A, g - 1)
+        sort_last_words(scalar)
+        fetch_x(CHUNK_B, 0)
+        first_layer(CHUNK_A, PASSES - 1)
+        sort_last_scales()
         for b0 in range(0, end_a, P):
-            relu(b0)
+            relu_rows(b0)
         for slots in EXPERT[0:2]:
             turn_h(slots)
-        fetch_x(CHUNK_B, 1, CHUNK_B)
-        first_layer(CHUNK_B, 0, CHUNK_B)
+        fetch_x(CHUNK_B, 1)
+        first_layer(CHUNK_B, 0)
         for slots in EXPERT[0:2]:
             group_h(slots, scalar)
-        fetch_x(CHUNK_B, 2, CHUNK_B)
-        first_layer(CHUNK_B, 1, CHUNK_B)
-        fetch_x(CHUNK_C, 0, CHUNK_C)
-        first_layer(CHUNK_B, 2, CHUNK_B)
+        fetch_x(CHUNK_B, 2)
+        first_layer(CHUNK_B, 1)
+        fetch_x(CHUNK_C, 0)
+        first_layer(CHUNK_B, 2)
         last_of_b = CHUNK_C[0] - P
         for b0 in range(end_a, last_of_b, P):
-            relu(b0)
+            relu_rows(b0)
         turn_h(EXPERT[2])
-        fetch_x(CHUNK_C, 1, CHUNK_C)
-        first_layer(CHUNK_C, 0, CHUNK_C)
-        relu(last_of_b)
+        fetch_x(CHUNK_C, 1)
+        first_layer(CHUNK_C, 0)
+        relu_rows(last_of_b)
         gather_x(C_FRONT, 2)
         group_x(BLOCK_8, 2, C_FRONT, BLOCK_8, scalar)
         turn_h(EXPERT[3])
-        first_layer(CHUNK_C, 1, CHUNK_C)
+        first_layer(CHUNK_C, 1)
         gather_x(C_BACK, 2)
 
         group_h(EXPERT[2], scalar)
-        first_layer(BLOCK_8, 2, BLOCK_8)
+        first_layer(BLOCK_8, 2)
         group_x(C_BACK, 2, C_BACK, BLOCK_9, vector)
         group_x((BLOCK_9[0], P - LAST_GATHER), 2, C_FRONT, BLOCK_9, scalar)
         group_h(EXPERT[3], scalar)
         quantize_h(EXPERT[0])
-        first_layer(BLOCK_9, 2, BLOCK_9)
-        second_layer(EXPERT[0:1], 0)
-        relu(BLOCK_8[0])
-        for slots in EXPERT[1:3]:
+        first_layer(BLOCK_9, 2)
+        relu_grouped(BLOCK_8, scalar)
+        for slots in EXPERT[1:4]:
             quantize_h(slots)
-        second_layer(EXPERT[1:2], 0)
-        relu_by_quarters(BLOCK_9[0])
-        turn_h(BLOCK_8)
-        quantize_h(EXPERT[3])
-        keep_y(EXPERT[0], 0, vector)
-        keep_y(EXPERT[1], 0, scalar)
-        group_h(BLOCK_8, scalar)
-        turn_h(BLOCK_9)
+        second_layer(EXPERT[0:2], 0)
+        relu_grouped(BLOCK_9, scalar)
+        quantize_h(BLOCK_8)
         second_layer(EXPERT[2:4], 0)
-        group_h(BLOCK_9, vector)
-        for block in (BLOCK_8, BLOCK_9):
-            quantize_h(block)
+        keep_y(CHUNK_A, 0, vector)
         keep_y(CHUNK_B, 0, scalar)
-        for block, engine in ((BLOCK_8, scalar), (BLOCK_9, vector)):
+        quantize_h(BLOCK_9)
+        for block, engine in ((BLOCK_8, vector), (BLOCK_9, scalar)):
             second_layer([block], 0)
             keep_y(block, 0, engine)
 

@@ -49,7 +49,8 @@ def tile_moe_pre_mlp_relu_kernel(
         v_ring = ctx.enter_context(tc.tile_pool(name="v_ring", bufs=VECTOR_RING))
         s_ring = ctx.enter_context(tc.tile_pool(name="s_ring", bufs=SCALAR_RING))
         codes = ctx.enter_context(tc.tile_pool(name="codes", bufs=CODE_RING))
-        psum = ctx.enter_context(tc.psum_pool(name="psum", bufs=PSUM_BANKS))
+        psum = ctx.enter_context(tc.psum_pool(name="psum", bufs=PSUM_BANKS - 1))
+        shared_bank = ctx.enter_context(tc.psum_pool(name="shared_bank", bufs=1))
 
         def ring_tile(engine, shape, dtype, name):
             if engine is vector:
@@ -75,7 +76,7 @@ def tile_moe_pre_mlp_relu_kernel(
         gates = keep.tile([P, S], F32, name="gates", align_bytes=64)
         w1_codes = [keep.tile([P, PASSES, 2 * H], U8, name="w1_codes_%d" % e, align_bytes=64) for e in range(E)]
         w1_plane = keep.tile([P, E * PASSES, H], U8, name="w1_plane", align_bytes=64)
-        last_rows = keep.tile([P, H], U8, name="last_rows", align_bytes=64)
+        last_rows = keep.tile([P, H // 2], U8, name="last_rows", align_bytes=64)
         w2_codes = keep.tile([P, E, 2 * N], U8, name="w2_codes", align_bytes=64)
         w2_plane = keep.tile([P, E, N], U8, name="w2_plane", align_bytes=64)
         identity = keep.tile([P, P], F32, name="identity", align_bytes=64)
@@ -83,12 +84,16 @@ def tile_moe_pre_mlp_relu_kernel(
 
         vector.memset(w1_plane[:].rearrange("p a b -> p (a b)").bitcast(I32), 0)
         vector.memset(w2_plane[:].rearrange("p a b -> p (a b)").bitcast(I32), 0)
-        vector.memset(last_rows[:].bitcast(I32), 0)
+        half_rows = 2 * PASSES * SCALE_ROWS
+        vector.memset(last_rows[half_rows:P].bitcast(I32), 0)
+        rows_of_last = w1_scales[LAST].rearrange("s q (f c) -> (s q f) c", f=2).bitcast(I32)
         make_identity(nc, identity[:])
 
         x_rows = xT.rearrange("(g p d) t -> g d p t", p=P, d=PACK)
         end_a = CHUNK_A[1]
         nc.sync.dma_start(tokens[0][0][:], x_rows[0, 0])
+        for r0, r1 in ((0, P // 2), (P // 2, half_rows)):
+            nc.sync.dma_start(last_rows[r0:r1].bitcast(I32), rows_of_last[r0:r1])
         nc.sync.dma_start(slot_tokens[:], offs)
         nc.sync.dma_start(gates[:, 0:FIRST_GATHER], gate[0:P, 0:FIRST_GATHER])
         nc.sync.dma_start(gates[:, FIRST_GATHER:end_a], gate[0:P, FIRST_GATHER:end_a])
@@ -101,9 +106,6 @@ def tile_moe_pre_mlp_relu_kernel(
         for plane, scale_rows in ((w1_plane[:, 0 : LAST * PASSES, :], w1_rows), (w2_plane[:], w2_rows)):
             for quad in range(P // QUADRANT):
                 nc.sync.dma_start(plane[QUADRANT * quad : QUADRANT * quad + 4].bitcast(I32), scale_rows[4 * quad : 4 * quad + 4])
-        rows_of_last = w1_scales[LAST].rearrange("s q i -> (s q) i").bitcast(I32)
-        for r0, r1 in ((0, 2 * SCALE_ROWS), (2 * SCALE_ROWS, PASSES * SCALE_ROWS)):
-            nc.sync.dma_start(last_rows[r0:r1].bitcast(I32), rows_of_last[r0:r1])
         for e in (0, 1, LAST, 2, 3):
             nc.sync.dma_start(w1_codes[e][:].bitcast(I32), w1_words[e].rearrange("s p b -> p s b").bitcast(I32))
         nc.sync.dma_start(w2_codes[:].bitcast(I32), w2_words.rearrange("e s p b -> p (e s) b").bitcast(I32))
@@ -122,14 +124,14 @@ def tile_moe_pre_mlp_relu_kernel(
             sorted_words[LAST] = words
 
         def sort_last_scales():
-            rows = ring_tile(vector, [P, H], U8, "sorted_rows")
-            vector.tensor_copy(rows[:].rearrange("p (t m) -> p t m", t=PACK), last_rows[:].rearrange("p (m t) -> p t m", t=PACK))
+            rows = keep.tile([P, PACK, H // 2 // PACK], U8, name="sorted_rows", align_bytes=64)
+            vector.tensor_copy(rows[:], last_rows[:].rearrange("p (m t) -> p t m", t=PACK))
             for g in range(PASSES):
+                plane = w1_plane[:, LAST * PASSES + g, :].rearrange("p (t f m) -> p f t m", t=PACK, f=2)
                 for quad in range(P // QUADRANT):
-                    r0 = SCALE_ROWS * g + 4 * quad
-                    nc.sync.dma_start(
-                        w1_plane[QUADRANT * quad : QUADRANT * quad + 4, LAST * PASSES + g, :].bitcast(I32), rows[r0 : r0 + 4].bitcast(I32)
-                    )
+                    for f in range(2):
+                        r0 = 2 * (SCALE_ROWS * g + 4 * quad) + f
+                        nc.sync.dma_start(plane[QUADRANT * quad : QUADRANT * quad + 4, f].bitcast(I32), rows[r0 : r0 + 7 : 2].bitcast(I32))
 
         def gather_x(slots, g, first_cut=None):
             s0, width = slots
@@ -166,7 +168,7 @@ def tile_moe_pre_mlp_relu_kernel(
                 e = b0 // C
                 x_operand = (x_codes[:, c0 : c0 + P].bitcast(FP8X4), x_plane[:, c0 : c0 + P])
                 if g == 0:
-                    a_banks[b0] = psum.tile([P, H], F32, name="a_bank", tag="bank")
+                    a_banks[b0] = (shared_bank if b0 == BLOCK_8[0] else psum).tile([P, H], F32, name="a_bank", tag="bank")
                 if e < LAST:
                     nc.tensor.matmul_mx(
                         out=a_banks[b0][:],
@@ -222,9 +224,9 @@ def tile_moe_pre_mlp_relu_kernel(
             vector.quantize_mx(out=h_codes[:].bitcast(FP8X4), scales=h_plane[:], in_=h_grouped[s0][:])
             h_operand[s0] = (h_codes, h_plane)
 
-        def second_layer(parts, b):
+        def second_layer(parts, b, pool=psum):
             s0 = parts[0][0]
-            y_bank = psum.tile([P, sum(width for r0, width in parts)], F32, name="y_bank", tag="bank")
+            y_bank = pool.tile([P, sum(width for r0, width in parts)], F32, name="y_bank", tag="bank")
             for r0, width in parts:
                 e = r0 // C
                 nc.tensor.matmul_mx(
@@ -255,6 +257,7 @@ def tile_moe_pre_mlp_relu_kernel(
             vector.tensor_tensor(total[:], y_half[b][:].indirect(offsets), first_results[b][:, t0:t1], ADD)
             nc.sync.dma_start(out[b * P : (b + 1) * P, t0:t1], total[:])
 
+        sort_last_scales()
         fetch_x(CHUNK_A, 0, FIRST_GATHER)
         for g in range(1, PASSES):
             fetch_x(CHUNK_A, g)
@@ -262,7 +265,6 @@ def tile_moe_pre_mlp_relu_kernel(
         sort_last_words(scalar)
         fetch_x(CHUNK_B, 0)
         first_layer(CHUNK_A, PASSES - 1)
-        sort_last_scales()
         for b0 in range(0, end_a, P):
             relu_rows(b0)
         for slots in EXPERT[0:2]:
@@ -298,16 +300,15 @@ def tile_moe_pre_mlp_relu_kernel(
         relu_grouped(BLOCK_8, scalar)
         for slots in EXPERT[1:4]:
             quantize_h(slots)
-        second_layer(EXPERT[0:2], 0)
+        second_layer(EXPERT[0:2], 0, shared_bank)
         relu_grouped(BLOCK_9, scalar)
         quantize_h(BLOCK_8)
+        second_layer([BLOCK_8], 0)
         second_layer(EXPERT[2:4], 0)
-        keep_y(CHUNK_A, 0, vector)
-        keep_y(CHUNK_B, 0, scalar)
         quantize_h(BLOCK_9)
-        for block, engine in ((BLOCK_8, vector), (BLOCK_9, scalar)):
-            second_layer([block], 0)
-            keep_y(block, 0, engine)
+        second_layer([BLOCK_9], 0)
+        for slots, engine in ((CHUNK_A, scalar), (BLOCK_8, scalar), (CHUNK_B, vector), (BLOCK_9, scalar)):
+            keep_y(slots, 0, engine)
 
         for chunk, parts in ((CHUNK_A, EXPERT[0:2]), (CHUNK_B, EXPERT[2:4]), (CHUNK_C, [BLOCK_8, BLOCK_9])):
             second_layer(parts, 1)

@@ -10,8 +10,6 @@ PACK = 4
 PASSES = K // (P * PACK)
 LIST_COLUMN = 16
 QUADRANT = 32
-SCALE_ROWS = 16
-LAST = E - 1
 
 FLOPS = 2 * S * (K * H + H * N)
 BYTES = 4 * K * T + E * (K * H + H * N) // 2 + E * (K * H + H * N) // 32 + 4 * S + 2 * P * (S + 2 * T) // 16 + 4 * N * T
@@ -29,14 +27,8 @@ ADD = mybir.AluOpType.add
 COPY = mybir.ActivationFunctionType.Copy
 RELU = mybir.ActivationFunctionType.Relu
 
-CHUNK_A, CHUNK_B, CHUNK_C = (0, 512), (512, 512), (1024, 256)
-EXPERT = [(e * C, C) for e in range(E)]
-BLOCK_8, BLOCK_9 = (1024, P), (1152, P)
-FIRST_GATHER = 192
-LAST_GATHER = 96
-C_FRONT, C_BACK = (CHUNK_C[0], C - LAST_GATHER), (S - LAST_GATHER, LAST_GATHER)
-LAST_STORE = 256
-VECTOR_RING, SCALAR_RING, CODE_RING, PSUM_BANKS = 10, 12, 10, 8
+VECTOR_RING, SCALAR_RING, GATHER_RING, CODE_RING, PSUM_BANKS = 14, 12, 3, 16, 8
+W1_LOADS = (([0, 1, 2, 3, 4], [0]), ([0, 1], [2]), ([0, 1], [1]), ([2, 3, 4], [1]), ([2, 3, 4], [2]))
 
 
 def tile_moe_pre_mlp_relu_kernel(
@@ -48,11 +40,13 @@ def tile_moe_pre_mlp_relu_kernel(
         keep = ctx.enter_context(tc.tile_pool(name="keep", bufs=1))
         v_ring = ctx.enter_context(tc.tile_pool(name="v_ring", bufs=VECTOR_RING))
         s_ring = ctx.enter_context(tc.tile_pool(name="s_ring", bufs=SCALAR_RING))
+        g_ring = ctx.enter_context(tc.tile_pool(name="g_ring", bufs=GATHER_RING))
         codes = ctx.enter_context(tc.tile_pool(name="codes", bufs=CODE_RING))
-        psum = ctx.enter_context(tc.psum_pool(name="psum", bufs=PSUM_BANKS - 1))
-        shared_bank = ctx.enter_context(tc.psum_pool(name="shared_bank", bufs=1))
+        psum = ctx.enter_context(tc.psum_pool(name="psum", bufs=PSUM_BANKS))
 
-        def ring_tile(engine, shape, dtype, name):
+        def ring_tile(engine, shape, dtype, name, paced=False):
+            if paced:
+                return g_ring.tile(shape, dtype, name=name, tag="g", align_bytes=64)
             if engine is vector:
                 return v_ring.tile(shape, dtype, name=name, tag="v", align_bytes=64)
             return s_ring.tile(shape, dtype, name=name, tag="s", align_bytes=64)
@@ -63,20 +57,13 @@ def tile_moe_pre_mlp_relu_kernel(
             else:
                 scalar.copy(dst, src)
 
-        def relu(engine, dst, src):
-            if engine is vector:
-                vector.tensor_scalar_max(dst, src, 0.0)
-            else:
-                scalar.activation(dst, src, RELU)
-
         slot_tokens = keep.tile([P, S // LIST_COLUMN], U16, name="slot_tokens")
         first_slots = keep.tile([P, T // LIST_COLUMN], U16, name="first_slots")
         second_slots = keep.tile([P, T // LIST_COLUMN], U16, name="second_slots")
         tokens = [[keep.tile([P, T], F32, name="tokens_%d_%d" % (g, d), align_bytes=64) for d in range(PACK)] for g in range(PASSES)]
         gates = keep.tile([P, S], F32, name="gates", align_bytes=64)
-        w1_codes = [keep.tile([P, PASSES, 2 * H], U8, name="w1_codes_%d" % e, align_bytes=64) for e in range(E)]
+        w1_codes = {}
         w1_plane = keep.tile([P, E * PASSES, H], U8, name="w1_plane", align_bytes=64)
-        last_rows = keep.tile([P, H // 2], U8, name="last_rows", align_bytes=64)
         w2_codes = keep.tile([P, E, 2 * N], U8, name="w2_codes", align_bytes=64)
         w2_plane = keep.tile([P, E, N], U8, name="w2_plane", align_bytes=64)
         identity = keep.tile([P, P], F32, name="identity", align_bytes=64)
@@ -84,241 +71,258 @@ def tile_moe_pre_mlp_relu_kernel(
 
         vector.memset(w1_plane[:].rearrange("p a b -> p (a b)").bitcast(I32), 0)
         vector.memset(w2_plane[:].rearrange("p a b -> p (a b)").bitcast(I32), 0)
-        half_rows = 2 * PASSES * SCALE_ROWS
-        vector.memset(last_rows[half_rows:P].bitcast(I32), 0)
-        rows_of_last = w1_scales[LAST].rearrange("s q (f c) -> (s q f) c", f=2).bitcast(I32)
         make_identity(nc, identity[:])
 
         x_rows = xT.rearrange("(g p d) t -> g d p t", p=P, d=PACK)
-        end_a = CHUNK_A[1]
-        nc.sync.dma_start(tokens[0][0][:], x_rows[0, 0])
-        for r0, r1 in ((0, P // 2), (P // 2, half_rows)):
-            nc.sync.dma_start(last_rows[r0:r1].bitcast(I32), rows_of_last[r0:r1])
-        nc.sync.dma_start(slot_tokens[:], offs)
-        nc.sync.dma_start(gates[:, 0:FIRST_GATHER], gate[0:P, 0:FIRST_GATHER])
-        nc.sync.dma_start(gates[:, FIRST_GATHER:end_a], gate[0:P, FIRST_GATHER:end_a])
-        for row in range(1, PASSES * PACK):
+
+        def load_tokens(row):
             g, d = divmod(row, PACK)
             nc.sync.dma_start(tokens[g][d][:], x_rows[g, d])
-        nc.sync.dma_start(gates[:, end_a:S], gate[0:P, end_a:S])
-        w1_rows = w1_scales[0:LAST].rearrange("e s q i -> q (e s) i").bitcast(I32)
-        w2_rows = w2_scales.rearrange("e s q i -> q (e s) i").bitcast(I32)
-        for plane, scale_rows in ((w1_plane[:, 0 : LAST * PASSES, :], w1_rows), (w2_plane[:], w2_rows)):
-            for quad in range(P // QUADRANT):
-                nc.sync.dma_start(plane[QUADRANT * quad : QUADRANT * quad + 4].bitcast(I32), scale_rows[4 * quad : 4 * quad + 4])
-        for e in (0, 1, LAST, 2, 3):
-            nc.sync.dma_start(w1_codes[e][:].bitcast(I32), w1_words[e].rearrange("s p b -> p s b").bitcast(I32))
-        nc.sync.dma_start(w2_codes[:].bitcast(I32), w2_words.rearrange("e s p b -> p (e s) b").bitcast(I32))
+
+        def load_gates(s0, s1):
+            nc.sync.dma_start(gates[:, s0:s1], gate[0:P, s0:s1])
+
+        def load_weights():
+            w1_rows = w1_scales.rearrange("e s q i -> q (e s) i").bitcast(I32)
+            w2_rows = w2_scales.rearrange("e s q i -> q (e s) i").bitcast(I32)
+            for plane, scale_rows in ((w1_plane, w1_rows), (w2_plane, w2_rows)):
+                for quad in range(P // QUADRANT):
+                    nc.sync.dma_start(plane[QUADRANT * quad : QUADRANT * quad + 4].bitcast(I32), scale_rows[4 * quad : 4 * quad + 4])
+            for experts, passes in W1_LOADS:
+                rows = [(e, g) for e in experts for g in passes]
+                words = keep.tile([P, len(rows), 2 * H], U8, name="w1_codes_%d_%d" % rows[0], align_bytes=64)
+                source = w1_words[experts[0] : experts[-1] + 1, passes[0] : passes[-1] + 1]
+                nc.sync.dma_start(words[:].bitcast(I32), source.rearrange("e s p b -> p (e s) b").bitcast(I32))
+                for place, row in enumerate(rows):
+                    w1_codes[row] = words[:, place, :]
+            nc.sync.dma_start(w2_codes[:].bitcast(I32), w2_words.rearrange("e s p b -> p (e s) b").bitcast(I32))
+
+        warm = keep.tile([P, 16], F32, name="warm")
+        nc.gpsimd.memset(warm[:, 0:8], 0.0)
+        scalar.activation(warm[:, 8:16], warm[:, 0:8], COPY)
+
+        load_tokens(0)
+        nc.sync.dma_start(slot_tokens[:], offs)
+        load_gates(896, 1024)
+        load_gates(1024, S)
+        for row in range(1, PACK):
+            load_tokens(row)
+        load_gates(0, 384)
+        load_tokens(4)
+        load_tokens(5)
+        load_gates(384, 896)
+        for row in range(6, PASSES * PACK):
+            load_tokens(row)
+        load_weights()
         nc.sync.dma_start(first_slots[:], pos1)
         nc.sync.dma_start(second_slots[:], pos2)
 
-        x_gathered, x_grouped, a_banks = {}, {}, {}
+        x_gathered, x_grouped, x_operand, a_banks, a_passes = {}, {}, {}, {}, {}
         h_rows, h_turned, h_grouped, h_operand = {}, {}, {}, {}
-        y_banks, first_results, sorted_words = {}, {}, {}
+        y_banks, first_results = {}, {}
 
-        def sort_last_words(engine):
-            words = ring_tile(engine, [P, PASSES, 2 * H], U8, "sorted_words")
-            dst = words[:].rearrange("p g b -> p (g b)").bitcast(U16).rearrange("p (g t m) -> p g t m", g=PASSES, t=PACK)
-            src = w1_codes[LAST][:].rearrange("p g b -> p (g b)").bitcast(U16).rearrange("p (g m t) -> p g t m", g=PASSES, t=PACK)
-            copy(engine, dst, src)
-            sorted_words[LAST] = words
-
-        def sort_last_scales():
-            rows = keep.tile([P, PACK, H // 2 // PACK], U8, name="sorted_rows", align_bytes=64)
-            vector.tensor_copy(rows[:], last_rows[:].rearrange("p (m t) -> p t m", t=PACK))
-            for g in range(PASSES):
-                plane = w1_plane[:, LAST * PASSES + g, :].rearrange("p (t f m) -> p f t m", t=PACK, f=2)
-                for quad in range(P // QUADRANT):
-                    for f in range(2):
-                        r0 = 2 * (SCALE_ROWS * g + 4 * quad) + f
-                        nc.sync.dma_start(plane[QUADRANT * quad : QUADRANT * quad + 4, f].bitcast(I32), rows[r0 : r0 + 7 : 2].bitcast(I32))
-
-        def gather_x(slots, g, first_cut=None):
-            s0, width = slots
-            gathered = ring_tile(vector, [P, PACK, width], F32, "gathered")
-            for d in range(PACK):
-                cuts = [0, first_cut, width] if first_cut and d == 0 else [0, width]
+        def gather_x(engine, g, s0, s1, planes=range(PACK), first_cut=None):
+            if (g, s0) not in x_gathered:
+                x_gathered[g, s0] = (engine, ring_tile(engine, [P, PACK, s1 - s0], F32, "gathered_%d_%d" % (g, s0), paced=engine is scalar))
+            gathered = x_gathered[g, s0][1]
+            for d in planes:
+                cuts = [s0, first_cut, s1] if first_cut and d == 0 else [s0, s1]
                 for c0, c1 in zip(cuts, cuts[1:]):
-                    offsets = slot_tokens[:, (s0 + c0) // LIST_COLUMN : (s0 + c1) // LIST_COLUMN]
-                    vector.tensor_tensor(gathered[:, d, c0:c1], tokens[g][d][:].indirect(offsets), gates[:, s0 + c0 : s0 + c1], MULT)
-            x_gathered[slots, g] = gathered
+                    window = tokens[g][d][:].indirect(slot_tokens[:, c0 // LIST_COLUMN : c1 // LIST_COLUMN])
+                    if engine is vector:
+                        vector.tensor_tensor(gathered[:, d, c0 - s0 : c1 - s0], window, gates[:, c0:c1], MULT)
+                    else:
+                        scalar.activation(gathered[:, d, c0 - s0 : c1 - s0], window, COPY)
 
-        def group_x(part, g, slots, chunk, engine):
-            s0, width = part
-            if (chunk, g) not in x_grouped:
-                x_grouped[chunk, g] = ring_tile(engine, [P, chunk[1], PACK], BF16, "x_grouped")
-            grouped = x_grouped[chunk, g][:, s0 - chunk[0] : s0 - chunk[0] + width, :].rearrange("p (c i) d -> p c d i", i=4)
-            planes = x_gathered[slots, g][:, :, s0 - slots[0] : s0 - slots[0] + width].rearrange("p d (c i) -> p c d i", i=4)
+        def group_x(g, s0, s1, into=None):
+            t0, t1 = into or (s0, s1)
+            if (g, t0) not in x_grouped:
+                x_grouped[g, t0] = ring_tile(vector, [P, t1 - t0, PACK], BF16, "x_grouped_%d_%d" % (g, t0))
+            engine, gathered = x_gathered[g, s0]
+            grouped = x_grouped[g, t0][:, s0 - t0 : s1 - t0, :].rearrange("p (c i) d -> p c d i", i=4)
+            planes = gathered[:].rearrange("p d (c i) -> p c d i", i=4)
             if engine is vector:
                 vector.tensor_copy(grouped, planes)
             else:
-                scalar.activation(grouped, planes, COPY)
+                weights = gates[:, s0:s1].rearrange("p (c o i) -> p c o i", o=1, i=4).to_broadcast([P, (s1 - s0) // 4, PACK, 4])
+                vector.tensor_tensor(grouped, planes, weights, MULT)
 
-        def fetch_x(chunk, g, first_cut=None):
-            gather_x(chunk, g, first_cut)
-            group_x(chunk, g, chunk, chunk, scalar)
+        def quantize_x(g, s0, s1):
+            x_codes = codes.tile([P, s1 - s0], U32, name="x_codes_%d_%d" % (g, s0), tag="codes", align_bytes=64)
+            x_plane = ring_tile(vector, [P, s1 - s0], U8, "x_plane")
+            vector.quantize_mx(out=x_codes[:].bitcast(FP8X4), scales=x_plane[:], in_=x_grouped[g, s0][:].rearrange("p c d -> p (c d)"))
+            for b0 in range(s0, s1, P):
+                x_operand[g, b0] = (x_codes[:, b0 - s0 : b0 - s0 + P].bitcast(FP8X4), x_plane[:, b0 - s0 : b0 - s0 + P])
 
-        def first_layer(chunk, g):
-            s0, width = chunk
-            x_codes = codes.tile([P, width], U32, name="x_codes", align_bytes=64)
-            x_plane = ring_tile(vector, [P, width], U8, "x_plane")
-            vector.quantize_mx(out=x_codes[:].bitcast(FP8X4), scales=x_plane[:], in_=x_grouped[chunk, g][:].rearrange("p c d -> p (c d)"))
-            for c0 in range(0, width, P):
-                b0 = s0 + c0
+        def first_layer(passes, s0, s1):
+            for b0 in range(s0, s1, P):
                 e = b0 // C
-                x_operand = (x_codes[:, c0 : c0 + P].bitcast(FP8X4), x_plane[:, c0 : c0 + P])
-                if g == 0:
-                    a_banks[b0] = (shared_bank if b0 == BLOCK_8[0] else psum).tile([P, H], F32, name="a_bank", tag="bank")
-                if e < LAST:
+                for g in passes:
+                    done = a_passes.setdefault(b0, [])
+                    done.append(g)
+                    if len(done) == 1:
+                        a_banks[b0] = psum.tile([P, H], F32, name="a_bank_%d" % b0, tag="bank")
                     nc.tensor.matmul_mx(
                         out=a_banks[b0][:],
-                        lhsT=x_operand[0],
-                        lhsT_scale=x_operand[1],
-                        rhs=w1_codes[e][:, g, :].bitcast(FP4X4),
+                        lhsT=x_operand[g, b0][0],
+                        lhsT_scale=x_operand[g, b0][1],
+                        rhs=w1_codes[e, g].bitcast(FP4X4),
                         rhs_scale=w1_plane[:, e * PASSES + g, :],
-                        start=(g == 0),
-                        stop=(g == PASSES - 1),
+                        start=(len(done) == 1),
+                        stop=(len(done) == PASSES),
                     )
+
+        def relu_rows(engine, s0, s1):
+            rows = ring_tile(engine, [P, (s1 - s0) // P, H], BF16, "h_rows_%d" % s0, paced=s0 == 0)
+            for b0 in range(s0, s1, P):
+                h_rows[b0] = rows[:, (b0 - s0) // P, :]
+                dst = h_rows[b0].rearrange("s (u p v) -> s u p v", u=2, v=2)
+                src = a_banks[b0][:].rearrange("s (p u v) -> s u p v", u=2, v=2)
+                if engine is vector:
+                    vector.tensor_scalar_max(dst, src, 0.0)
                 else:
-                    for t in range(PACK):
-                        nc.tensor.matmul_mx(
-                            out=a_banks[b0][:, t * P : (t + 1) * P],
-                            lhsT=sorted_words[e][:, g, 2 * t * P : 2 * (t + 1) * P].bitcast(FP4X4),
-                            lhsT_scale=w1_plane[:, e * PASSES + g, t * P : (t + 1) * P],
-                            rhs=x_operand[0],
-                            rhs_scale=x_operand[1],
-                            start=(g == 0 and t == 0),
-                            stop=(g == PASSES - 1 and t == PACK - 1),
-                        )
+                    scalar.activation(dst, src, RELU)
 
-        def relu_rows(b0):
-            rows = ring_tile(scalar, [P, 2, P, 2], BF16, "h_rows")
-            relu(scalar, rows[:], a_banks[b0][:].rearrange("s (p u v) -> s u p v", u=2, v=2))
-            h_rows[b0] = rows
-
-        def relu_grouped(block, engine):
-            s0, width = block
-            grouped = ring_tile(engine, [P, width * PACK], BF16, "h_grouped")
-            relu(engine, grouped[:].rearrange("p (c i t) -> p c t i", t=PACK, i=2), a_banks[s0][:].rearrange("p (t c i) -> p c t i", t=PACK, i=2))
-            h_grouped[s0] = grouped
-
-        def turn_h(slots):
-            s0, width = slots
-            turned = psum.tile([P, 2, width], F32, name="turned", tag="bank")
-            for c0 in range(0, width, P):
-                pairs = h_rows[s0 + c0][:].rearrange("s u p v -> s (u p v)").bitcast(F32)
+        def turn_h(s0, s1):
+            turned = psum.tile([P, 2, s1 - s0], F32, name="turned_%d" % s0, tag="bank")
+            for b0 in range(s0, s1, P):
+                pairs = h_rows[b0].bitcast(F32)
                 for u in range(2):
-                    nc.tensor.transpose(turned[:, u, c0 : c0 + P], pairs[:, u * P : (u + 1) * P], identity[:])
+                    nc.tensor.transpose(turned[:, u, b0 - s0 : b0 - s0 + P], pairs[:, u * P : (u + 1) * P], identity[:])
             h_turned[s0] = turned
 
-        def group_h(slots, engine):
-            s0, width = slots
-            grouped = ring_tile(engine, [P, width * PACK], BF16, "h_grouped")
+        def group_h(engine, s0, s1):
+            grouped = ring_tile(engine, [P, (s1 - s0) * PACK], BF16, "h_grouped_%d" % s0)
             copy(engine, grouped[:].bitcast(F32).rearrange("p (s u) -> p s u", u=2), h_turned[s0][:].rearrange("p u s -> p s u"))
             h_grouped[s0] = grouped
 
-        def quantize_h(slots):
-            s0, width = slots
-            h_codes = codes.tile([P, width], U32, name="h_codes", align_bytes=64)
-            h_plane = ring_tile(vector, [P, width], U8, "h_plane")
+        def quantize_h(s0, s1):
+            h_codes = codes.tile([P, s1 - s0], U32, name="h_codes_%d" % s0, tag="codes", align_bytes=64)
+            h_plane = ring_tile(vector, [P, s1 - s0], U8, "h_plane")
             vector.quantize_mx(out=h_codes[:].bitcast(FP8X4), scales=h_plane[:], in_=h_grouped[s0][:])
             h_operand[s0] = (h_codes, h_plane)
 
-        def second_layer(parts, b, pool=psum):
-            s0 = parts[0][0]
-            y_bank = pool.tile([P, sum(width for r0, width in parts)], F32, name="y_bank", tag="bank")
-            for r0, width in parts:
-                e = r0 // C
+        def second_layer(b, *cuts):
+            y_bank = psum.tile([P, cuts[-1] - cuts[0]], F32, name="y_bank_%d_%d" % (b, cuts[0]), tag="bank")
+            for s0, s1 in zip(cuts, cuts[1:]):
+                e = s0 // C
                 nc.tensor.matmul_mx(
-                    out=y_bank[:, r0 - s0 : r0 - s0 + width],
+                    out=y_bank[:, s0 - cuts[0] : s1 - cuts[0]],
                     lhsT=w2_codes[:, e, 2 * b * P : 2 * (b + 1) * P].bitcast(FP4X4),
                     lhsT_scale=w2_plane[:, e, b * P : (b + 1) * P],
-                    rhs=h_operand[r0][0][:].bitcast(FP8X4),
-                    rhs_scale=h_operand[r0][1][:],
+                    rhs=h_operand[s0][0][:].bitcast(FP8X4),
+                    rhs_scale=h_operand[s0][1][:],
                     start=True,
                     stop=True,
                 )
-                y_banks[r0, b] = (y_bank, r0 - s0)
+            y_banks[b, cuts[0]] = y_bank
 
-        def keep_y(slots, b, engine):
-            s0, width = slots
-            y_bank, c0 = y_banks[s0, b]
-            copy(engine, y_half[b][:, s0 : s0 + width], y_bank[:, c0 : c0 + width])
+        def keep_y(engine, b, s0, s1):
+            copy(engine, y_half[b][:, s0:s1], y_banks[b, s0][:])
 
         def fetch_first(b, t0, t1):
-            if t0 == 0:
-                first_results[b] = ring_tile(vector, [P, T], F32, "first_result")
+            first_results[b, t0] = ring_tile(scalar, [P, t1 - t0], F32, "first_result_%d_%d" % (b, t0))
             offsets = first_slots[:, t0 // LIST_COLUMN : t1 // LIST_COLUMN]
-            vector.tensor_copy(first_results[b][:, t0:t1], y_half[b][:].indirect(offsets))
+            scalar.activation(first_results[b, t0][:], y_half[b][:].indirect(offsets), COPY)
 
-        def add_second(b, t0, t1):
-            total = ring_tile(vector, [P, t1 - t0], F32, "total")
+        def add_second(b, t0, t1, total=None, base=None):
+            if total is None:
+                total, base = ring_tile(vector, [P, T], F32, "total_%d_%d" % (b, t0)), t0
             offsets = second_slots[:, t0 // LIST_COLUMN : t1 // LIST_COLUMN]
-            vector.tensor_tensor(total[:], y_half[b][:].indirect(offsets), first_results[b][:, t0:t1], ADD)
-            nc.sync.dma_start(out[b * P : (b + 1) * P, t0:t1], total[:])
+            vector.tensor_tensor(total[:, t0 - base : t1 - base], y_half[b][:].indirect(offsets), first_results[b, t0][:], ADD)
+            return total, base
 
-        sort_last_scales()
-        fetch_x(CHUNK_A, 0, FIRST_GATHER)
-        for g in range(1, PASSES):
-            fetch_x(CHUNK_A, g)
-            first_layer(CHUNK_A, g - 1)
-        sort_last_words(scalar)
-        fetch_x(CHUNK_B, 0)
-        first_layer(CHUNK_A, PASSES - 1)
-        for b0 in range(0, end_a, P):
-            relu_rows(b0)
-        for slots in EXPERT[0:2]:
-            turn_h(slots)
-        fetch_x(CHUNK_B, 1)
-        first_layer(CHUNK_B, 0)
-        for slots in EXPERT[0:2]:
-            group_h(slots, scalar)
-        fetch_x(CHUNK_B, 2)
-        first_layer(CHUNK_B, 1)
-        fetch_x(CHUNK_C, 0)
-        first_layer(CHUNK_B, 2)
-        last_of_b = CHUNK_C[0] - P
-        for b0 in range(end_a, last_of_b, P):
-            relu_rows(b0)
-        turn_h(EXPERT[2])
-        fetch_x(CHUNK_C, 1)
-        first_layer(CHUNK_C, 0)
-        relu_rows(last_of_b)
-        gather_x(C_FRONT, 2)
-        group_x(BLOCK_8, 2, C_FRONT, BLOCK_8, scalar)
-        turn_h(EXPERT[3])
-        first_layer(CHUNK_C, 1)
-        gather_x(C_BACK, 2)
+        def store(b, t1, total, base):
+            nc.sync.dma_start(out[b * P : (b + 1) * P, base:t1], total[:, 0 : t1 - base])
 
-        group_h(EXPERT[2], scalar)
-        first_layer(BLOCK_8, 2)
-        group_x(C_BACK, 2, C_BACK, BLOCK_9, vector)
-        group_x((BLOCK_9[0], P - LAST_GATHER), 2, C_FRONT, BLOCK_9, scalar)
-        group_h(EXPERT[3], scalar)
-        quantize_h(EXPERT[0])
-        first_layer(BLOCK_9, 2)
-        relu_grouped(BLOCK_8, scalar)
-        for slots in EXPERT[1:4]:
-            quantize_h(slots)
-        second_layer(EXPERT[0:2], 0, shared_bank)
-        relu_grouped(BLOCK_9, scalar)
-        quantize_h(BLOCK_8)
-        second_layer([BLOCK_8], 0)
-        second_layer(EXPERT[2:4], 0)
-        quantize_h(BLOCK_9)
-        second_layer([BLOCK_9], 0)
-        for slots, engine in ((CHUNK_A, scalar), (BLOCK_8, scalar), (CHUNK_B, vector), (BLOCK_9, scalar)):
-            keep_y(slots, 0, engine)
+        gather_x(vector, 0, 896, 1280, first_cut=1024)
+        for d in range(PACK):
+            gather_x(scalar, 0, 0, 384, planes=[d])
+            gather_x(scalar, 0, 384, 896, planes=[d])
+        group_x(0, 896, 1280)
+        gather_x(vector, 1, 0, 256)
+        quantize_x(0, 896, 1280)
+        group_x(1, 0, 256, (0, 512))
+        gather_x(scalar, 2, 0, 512)
+        group_x(0, 0, 384)
+        group_x(0, 384, 896)
+        quantize_x(0, 0, 384)
+        gather_x(vector, 1, 256, 512, planes=[0])
+        quantize_x(0, 384, 896)
+        first_layer([0], 0, 1024)
+        gather_x(vector, 1, 256, 512, planes=[1, 2, 3])
+        gather_x(scalar, 1, 512, 1024)
+        group_x(2, 0, 512)
+        group_x(1, 256, 512, (0, 512))
+        quantize_x(2, 0, 512)
+        quantize_x(1, 0, 512)
+        first_layer([2], 0, 512)
+        first_layer([1], 0, 512)
+        gather_x(scalar, 2, 512, 1024)
+        group_x(1, 512, 1024)
+        gather_x(vector, 2, 1024, 1152, planes=[0, 1])
+        quantize_x(1, 512, 1024)
+        first_layer([1], 512, 1024)
+        relu_rows(scalar, 0, 256)
+        gather_x(scalar, 1, 1024, 1280)
+        turn_h(0, 256)
+        first_layer([0], 1024, 1152)
+        group_x(2, 512, 1024)
+        gather_x(vector, 2, 1024, 1152, planes=[2, 3])
+        relu_rows(scalar, 256, 512)
+        first_layer([0], 1152, 1280)
+        quantize_x(2, 512, 1024)
+        first_layer([2], 512, 1024)
+        group_h(scalar, 0, 256)
+        turn_h(256, 512)
+        group_x(2, 1024, 1152)
+        group_x(1, 1024, 1280)
+        gather_x(vector, 2, 1152, 1280, planes=[0, 1])
+        quantize_x(2, 1024, 1152)
+        quantize_x(1, 1024, 1280)
+        relu_rows(scalar, 512, 768)
+        turn_h(512, 768)
+        first_layer([2, 1], 1024, 1152)
+        first_layer([1], 1152, 1280)
+        relu_rows(scalar, 768, 1024)
+        gather_x(vector, 2, 1152, 1280, planes=[2, 3])
+        quantize_h(0, 256)
+        group_h(scalar, 256, 512)
+        group_x(2, 1152, 1280)
+        turn_h(768, 1024)
+        relu_rows(scalar, 1024, 1152)
+        quantize_x(2, 1152, 1280)
+        first_layer([2], 1152, 1280)
+        turn_h(1024, 1152)
+        group_h(vector, 512, 768)
+        group_h(scalar, 768, 1024)
+        quantize_h(256, 512)
+        relu_rows(scalar, 1152, 1280)
+        second_layer(0, 0, 256, 512)
+        quantize_h(512, 768)
+        quantize_h(768, 1024)
+        second_layer(0, 512, 768, 1024)
+        turn_h(1152, 1280)
+        group_h(scalar, 1024, 1152)
+        second_layer(1, 0, 256, 512)
+        keep_y(vector, 0, 0, 512)
+        group_h(scalar, 1152, 1280)
+        quantize_h(1024, 1152)
+        second_layer(1, 512, 768, 1024)
+        keep_y(scalar, 0, 512, 1024)
+        quantize_h(1152, 1280)
+        second_layer(0, 1024, 1152, 1280)
+        second_layer(1, 1024, 1152, 1280)
+        keep_y(vector, 1, 0, 512)
+        keep_y(scalar, 0, 1024, 1280)
+        keep_y(vector, 1, 512, 1024)
+        keep_y(vector, 1, 1024, 1280)
 
-        for chunk, parts in ((CHUNK_A, EXPERT[0:2]), (CHUNK_B, EXPERT[2:4]), (CHUNK_C, [BLOCK_8, BLOCK_9])):
-            second_layer(parts, 1)
-            keep_y(chunk, 1, scalar)
-
-        cut = T - LAST_STORE
-        fetch_first(0, 0, cut)
-        fetch_first(0, cut, T)
-        add_second(0, 0, cut)
-        fetch_first(1, 0, T)
-        add_second(0, cut, T)
-        add_second(1, 0, cut)
-        add_second(1, cut, T)
+        for b, t0, t1 in ((0, 0, 128), (0, 128, 384), (0, 384, 640), (1, 0, 384), (1, 384, 640)):
+            fetch_first(b, t0, t1)
+        total = add_second(0, 0, 128)
+        add_second(0, 128, 384, *total)
+        add_second(0, 384, 640, *total)
+        store(0, 640, *total)
+        store(1, 384, *add_second(1, 0, 384))
+        store(1, 640, *add_second(1, 384, 640))

@@ -27,29 +27,20 @@ ADD = mybir.AluOpType.add
 COPY = mybir.ActivationFunctionType.Copy
 RELU = mybir.ActivationFunctionType.Relu
 
-VECTOR_RING, SCALAR_RING, GATHER_RING, CODE_RING, PSUM_BANKS = 14, 12, 3, 16, 8
-W1_LOADS = (([0, 1, 2, 3, 4], [0]), ([0, 1], [2]), ([0, 1], [1]), ([2, 3, 4], [1]), ([2, 3, 4], [2]))
+PSUM_BANKS, BANK, GATE_ROWS = 8, 512, 8
 
 
 def tile_moe_pre_mlp_relu_kernel(
     tc, xT, w1_words, w1_scales, w2_words, w2_scales, gate, offs, pos1, pos2, out
 ):
     nc = tc.nc
-    vector, scalar = nc.vector, nc.scalar
+    vector, scalar, gpsimd = nc.vector, nc.scalar, nc.gpsimd
     with ExitStack() as ctx:
         keep = ctx.enter_context(tc.tile_pool(name="keep", bufs=1))
-        v_ring = ctx.enter_context(tc.tile_pool(name="v_ring", bufs=VECTOR_RING))
-        s_ring = ctx.enter_context(tc.tile_pool(name="s_ring", bufs=SCALAR_RING))
-        g_ring = ctx.enter_context(tc.tile_pool(name="g_ring", bufs=GATHER_RING))
-        codes = ctx.enter_context(tc.tile_pool(name="codes", bufs=CODE_RING))
         psum = ctx.enter_context(tc.psum_pool(name="psum", bufs=PSUM_BANKS))
 
-        def ring_tile(engine, shape, dtype, name, paced=False):
-            if paced:
-                return g_ring.tile(shape, dtype, name=name, tag="g", align_bytes=64)
-            if engine is vector:
-                return v_ring.tile(shape, dtype, name=name, tag="v", align_bytes=64)
-            return s_ring.tile(shape, dtype, name=name, tag="s", align_bytes=64)
+        def sbuf(shape, dtype, name, buffer=None):
+            return keep.tile(shape, dtype, name=name, tag=buffer or name, align_bytes=64)
 
         def copy(engine, dst, src):
             if engine is vector:
@@ -60,97 +51,130 @@ def tile_moe_pre_mlp_relu_kernel(
         slot_tokens = keep.tile([P, S // LIST_COLUMN], U16, name="slot_tokens")
         first_slots = keep.tile([P, T // LIST_COLUMN], U16, name="first_slots")
         second_slots = keep.tile([P, T // LIST_COLUMN], U16, name="second_slots")
-        tokens = [[keep.tile([P, T], F32, name="tokens_%d_%d" % (g, d), align_bytes=64) for d in range(PACK)] for g in range(PASSES)]
-        gates = keep.tile([P, S], F32, name="gates", align_bytes=64)
+        tokens = [[sbuf([P, T], F32, "tokens_%d_%d" % (g, d)) for d in range(PACK)] for g in range(PASSES)]
+        gates = sbuf([P, S], F32, "gates")
+        gate_rows = sbuf([P, P], F32, "gate_rows")
         w1_codes = {}
-        w1_plane = keep.tile([P, E * PASSES, H], U8, name="w1_plane", align_bytes=64)
-        w2_codes = keep.tile([P, E, 2 * N], U8, name="w2_codes", align_bytes=64)
-        w2_plane = keep.tile([P, E, N], U8, name="w2_plane", align_bytes=64)
-        identity = keep.tile([P, P], F32, name="identity", align_bytes=64)
-        y_half = [keep.tile([P, S], F32, name="y_half_%d" % b, align_bytes=64) for b in range(N // P)]
+        w1_plane = sbuf([P, E * PASSES, H], U8, "w1_plane")
+        w2_codes = sbuf([P, E, 2 * N], U8, "w2_codes")
+        w2_plane = sbuf([P, E, N], U8, "w2_plane")
+        identity = sbuf([P, P], F32, "identity")
+        y_half = [sbuf([P, S], F32, "y_half_%d" % b) for b in range(N // P)]
 
+        vector.memset(gate_rows[:], 0.0)
         vector.memset(w1_plane[:].rearrange("p a b -> p (a b)").bitcast(I32), 0)
         vector.memset(w2_plane[:].rearrange("p a b -> p (a b)").bitcast(I32), 0)
         make_identity(nc, identity[:])
-
-        x_rows = xT.rearrange("(g p d) t -> g d p t", p=P, d=PACK)
-
-        def load_tokens(row):
-            g, d = divmod(row, PACK)
-            nc.sync.dma_start(tokens[g][d][:], x_rows[g, d])
-
-        def load_gates(s0, s1):
-            nc.sync.dma_start(gates[:, s0:s1], gate[0:P, s0:s1])
-
-        def load_weights():
-            w1_rows = w1_scales.rearrange("e s q i -> q (e s) i").bitcast(I32)
-            w2_rows = w2_scales.rearrange("e s q i -> q (e s) i").bitcast(I32)
-            for plane, scale_rows in ((w1_plane, w1_rows), (w2_plane, w2_rows)):
-                for quad in range(P // QUADRANT):
-                    nc.sync.dma_start(plane[QUADRANT * quad : QUADRANT * quad + 4].bitcast(I32), scale_rows[4 * quad : 4 * quad + 4])
-            for experts, passes in W1_LOADS:
-                rows = [(e, g) for e in experts for g in passes]
-                words = keep.tile([P, len(rows), 2 * H], U8, name="w1_codes_%d_%d" % rows[0], align_bytes=64)
-                source = w1_words[experts[0] : experts[-1] + 1, passes[0] : passes[-1] + 1]
-                nc.sync.dma_start(words[:].bitcast(I32), source.rearrange("e s p b -> p (e s) b").bitcast(I32))
-                for place, row in enumerate(rows):
-                    w1_codes[row] = words[:, place, :]
-            nc.sync.dma_start(w2_codes[:].bitcast(I32), w2_words.rearrange("e s p b -> p (e s) b").bitcast(I32))
 
         warm = keep.tile([P, 16], F32, name="warm")
         nc.gpsimd.memset(warm[:, 0:8], 0.0)
         scalar.activation(warm[:, 8:16], warm[:, 0:8], COPY)
 
+        x_rows = xT.rearrange("(g p d) t -> g d p t", p=P, d=PACK)
+
+        def load_tokens(*rows):
+            for row in rows:
+                g, d = divmod(row, PACK)
+                nc.sync.dma_start(tokens[g][d][:], x_rows[g, d])
+
+        def load_gates(s0, s1):
+            nc.sync.dma_start(gates[:, s0:s1], gate[0:P, s0:s1])
+
+        def load_scales(plane, scales):
+            scale_rows = scales.rearrange("e s q i -> q (e s) i").bitcast(I32)
+            for quad in range(P // QUADRANT):
+                nc.sync.dma_start(plane[QUADRANT * quad : QUADRANT * quad + 4].bitcast(I32), scale_rows[4 * quad : 4 * quad + 4])
+
+        def load_w1(experts, passes):
+            rows = [(e, g) for e in experts for g in passes]
+            words = sbuf([P, len(rows), 2 * H], U8, "w1_codes_%d_%d" % rows[0])
+            source = w1_words[experts[0] : experts[-1] + 1, passes[0] : passes[-1] + 1]
+            nc.sync.dma_start(words[:].bitcast(I32), source.rearrange("e s p b -> p (e s) b").bitcast(I32))
+            for place, row in enumerate(rows):
+                w1_codes[row] = words[:, place, :]
+
+        def load_w2_and_lists():
+            load_scales(w2_plane, w2_scales)
+            nc.sync.dma_start(w2_codes[:].bitcast(I32), w2_words.rearrange("e s p b -> p (e s) b").bitcast(I32))
+            nc.sync.dma_start(first_slots[:], pos1)
+            nc.sync.dma_start(second_slots[:], pos2)
+
         load_tokens(0)
         nc.sync.dma_start(slot_tokens[:], offs)
-        load_gates(896, 1024)
-        load_gates(1024, S)
-        for row in range(1, PACK):
-            load_tokens(row)
-        load_gates(0, 384)
-        load_tokens(4)
-        load_tokens(5)
-        load_gates(384, 896)
-        for row in range(6, PASSES * PACK):
-            load_tokens(row)
-        load_weights()
-        nc.sync.dma_start(first_slots[:], pos1)
-        nc.sync.dma_start(second_slots[:], pos2)
+        nc.sync.dma_start(gate_rows[0:GATE_ROWS, :], gate[0, 0 : GATE_ROWS * P].rearrange("(b m) -> b m", m=P))
+        load_tokens(1, 2, 3, 4)
+        load_gates(896, S)
+        load_tokens(5, 6, 7)
+        load_gates(0, 512)
+        load_tokens(8, 9, 10, 11)
+
+        for experts in ([0, 1], [2, 3], [4]):
+            rows = slice(experts[0] * PASSES, (experts[-1] + 1) * PASSES)
+            load_scales(w1_plane[:, rows, :], w1_scales[experts[0] : experts[-1] + 1])
+            load_w1(experts, [0, 1, 2])
+        load_w2_and_lists()
 
         x_gathered, x_grouped, x_operand, a_banks, a_passes = {}, {}, {}, {}, {}
         h_rows, h_turned, h_grouped, h_operand = {}, {}, {}, {}
-        y_banks, first_results = {}, {}
+        y_banks, first_results, gate_banks = {}, {}, {}
 
-        def gather_x(engine, g, s0, s1, planes=range(PACK), first_cut=None):
+        def gather_x(engine, g, s0, s1, planes=range(PACK), gated=False, buffer=None, first_cut=None):
             if (g, s0) not in x_gathered:
-                x_gathered[g, s0] = (engine, ring_tile(engine, [P, PACK, s1 - s0], F32, "gathered_%d_%d" % (g, s0), paced=engine is scalar))
-            gathered = x_gathered[g, s0][1]
+                x_gathered[g, s0] = (gated, sbuf([P, PACK, s1 - s0], F32, "gathered_%d_%d" % (g, s0), buffer))
+            gated, gathered = x_gathered[g, s0]
             for d in planes:
                 cuts = [s0, first_cut, s1] if first_cut and d == 0 else [s0, s1]
                 for c0, c1 in zip(cuts, cuts[1:]):
                     window = tokens[g][d][:].indirect(slot_tokens[:, c0 // LIST_COLUMN : c1 // LIST_COLUMN])
-                    if engine is vector:
-                        vector.tensor_tensor(gathered[:, d, c0 - s0 : c1 - s0], window, gates[:, c0:c1], MULT)
+                    plane = gathered[:, d, c0 - s0 : c1 - s0]
+                    if gated:
+                        vector.tensor_tensor(plane, window, gates[:, c0:c1], MULT)
+                    elif engine is vector:
+                        vector.tensor_copy(plane, window)
                     else:
-                        scalar.activation(gathered[:, d, c0 - s0 : c1 - s0], window, COPY)
+                        scalar.activation(plane, window, COPY)
 
-        def group_x(g, s0, s1, into=None):
-            t0, t1 = into or (s0, s1)
+        def open_grouped(buffer, *parts):
+            name = "x_grouped_%d_%d" % parts[0][0:2]
+            tile = sbuf([P, sum(s1 - s0 for g, s0, s1 in parts), PACK], BF16, name, buffer)
+            c0 = 0
+            for g, s0, s1 in parts:
+                x_grouped[g, s0] = tile[:, c0 : c0 + s1 - s0, :]
+                c0 = c0 + s1 - s0
+
+        def group_x(engine, g, s0, s1, unit=None, part=None, spread=False):
+            u0 = s0 if unit is None else unit
+            t0 = s0 if part is None else part
             if (g, t0) not in x_grouped:
-                x_grouped[g, t0] = ring_tile(vector, [P, t1 - t0, PACK], BF16, "x_grouped_%d_%d" % (g, t0))
-            engine, gathered = x_gathered[g, s0]
+                open_grouped(None, (g, s0, s1))
+            gated, gathered = x_gathered[g, u0]
             grouped = x_grouped[g, t0][:, s0 - t0 : s1 - t0, :].rearrange("p (c i) d -> p c d i", i=4)
-            planes = gathered[:].rearrange("p d (c i) -> p c d i", i=4)
-            if engine is vector:
+            planes = gathered[:, :, s0 - u0 : s1 - u0].rearrange("p d (c i) -> p c d i", i=4)
+            if gated:
                 vector.tensor_copy(grouped, planes)
             else:
-                weights = gates[:, s0:s1].rearrange("p (c o i) -> p c o i", o=1, i=4).to_broadcast([P, (s1 - s0) // 4, PACK, 4])
-                vector.tensor_tensor(grouped, planes, weights, MULT)
+                bank0 = s0 // BANK * BANK
+                source = gate_banks[bank0][:, s0 - bank0 : s1 - bank0] if spread else gates[:, s0:s1]
+                weights = source.rearrange("p (c o i) -> p c o i", o=1, i=4).to_broadcast([P, (s1 - s0) // 4, PACK, 4])
+                engine.tensor_tensor(grouped, planes, weights, MULT)
 
-        def quantize_x(g, s0, s1):
-            x_codes = codes.tile([P, s1 - s0], U32, name="x_codes_%d_%d" % (g, s0), tag="codes", align_bytes=64)
-            x_plane = ring_tile(vector, [P, s1 - s0], U8, "x_plane")
-            vector.quantize_mx(out=x_codes[:].bitcast(FP8X4), scales=x_plane[:], in_=x_grouped[g, s0][:].rearrange("p c d -> p (c d)"))
+        def spread_gates(s0, s1):
+            turned = psum.tile([P, P], F32, name="gate_turned", tag="bank")
+            nc.tensor.transpose(turned[:], gate_rows[:], identity[:])
+            columns = sbuf([P, GATE_ROWS], F32, "gate_columns")
+            vector.tensor_copy(columns[:], turned[:, 0:GATE_ROWS])
+            for b0 in range(s0, s1, P):
+                bank0 = b0 // BANK * BANK
+                if bank0 not in gate_banks:
+                    gate_banks[bank0] = psum.tile([P, BANK], F32, name="gate_bank_%d" % bank0, tag="bank")
+                column = columns[:, b0 // P : b0 // P + 1].to_broadcast([P, P])
+                nc.tensor.transpose(gate_banks[bank0][:, b0 - bank0 : b0 - bank0 + P], column, identity[:])
+
+        def quantize_x(g, s0, s1, x_plane=None):
+            x_codes = sbuf([P, s1 - s0], U32, "x_codes_%d_%d" % (g, s0))
+            if x_plane is None:
+                x_plane = sbuf([P, s1 - s0], U8, "x_plane_%d_%d" % (g, s0))[:]
+            vector.quantize_mx(out=x_codes[:].bitcast(FP8X4), scales=x_plane, in_=x_grouped[g, s0].rearrange("p c d -> p (c d)"))
             for b0 in range(s0, s1, P):
                 x_operand[g, b0] = (x_codes[:, b0 - s0 : b0 - s0 + P].bitcast(FP8X4), x_plane[:, b0 - s0 : b0 - s0 + P])
 
@@ -172,11 +196,10 @@ def tile_moe_pre_mlp_relu_kernel(
                         stop=(len(done) == PASSES),
                     )
 
-        def relu_rows(engine, s0, s1):
-            rows = ring_tile(engine, [P, (s1 - s0) // P, H], BF16, "h_rows_%d" % s0, paced=s0 == 0)
+        def relu_rows(engine, s0, s1, buffer=None):
             for b0 in range(s0, s1, P):
-                h_rows[b0] = rows[:, (b0 - s0) // P, :]
-                dst = h_rows[b0].rearrange("s (u p v) -> s u p v", u=2, v=2)
+                h_rows[b0] = sbuf([P, H], BF16, "h_rows_%d" % b0, buffer)
+                dst = h_rows[b0][:].rearrange("s (u p v) -> s u p v", u=2, v=2)
                 src = a_banks[b0][:].rearrange("s (p u v) -> s u p v", u=2, v=2)
                 if engine is vector:
                     vector.tensor_scalar_max(dst, src, 0.0)
@@ -186,19 +209,19 @@ def tile_moe_pre_mlp_relu_kernel(
         def turn_h(s0, s1):
             turned = psum.tile([P, 2, s1 - s0], F32, name="turned_%d" % s0, tag="bank")
             for b0 in range(s0, s1, P):
-                pairs = h_rows[b0].bitcast(F32)
+                pairs = h_rows[b0][:].bitcast(F32)
                 for u in range(2):
                     nc.tensor.transpose(turned[:, u, b0 - s0 : b0 - s0 + P], pairs[:, u * P : (u + 1) * P], identity[:])
             h_turned[s0] = turned
 
-        def group_h(engine, s0, s1):
-            grouped = ring_tile(engine, [P, (s1 - s0) * PACK], BF16, "h_grouped_%d" % s0)
+        def group_h(engine, s0, s1, buffer=None):
+            grouped = sbuf([P, (s1 - s0) * PACK], BF16, "h_grouped_%d" % s0, buffer)
             copy(engine, grouped[:].bitcast(F32).rearrange("p (s u) -> p s u", u=2), h_turned[s0][:].rearrange("p u s -> p s u"))
             h_grouped[s0] = grouped
 
         def quantize_h(s0, s1):
-            h_codes = codes.tile([P, s1 - s0], U32, name="h_codes_%d" % s0, tag="codes", align_bytes=64)
-            h_plane = ring_tile(vector, [P, s1 - s0], U8, "h_plane")
+            h_codes = sbuf([P, s1 - s0], U32, "h_codes_%d" % s0)
+            h_plane = sbuf([P, s1 - s0], U8, "h_plane_%d" % s0)
             vector.quantize_mx(out=h_codes[:].bitcast(FP8X4), scales=h_plane[:], in_=h_grouped[s0][:])
             h_operand[s0] = (h_codes, h_plane)
 
@@ -221,13 +244,13 @@ def tile_moe_pre_mlp_relu_kernel(
             copy(engine, y_half[b][:, s0:s1], y_banks[b, s0][:])
 
         def fetch_first(b, t0, t1):
-            first_results[b, t0] = ring_tile(scalar, [P, t1 - t0], F32, "first_result_%d_%d" % (b, t0))
+            first_results[b, t0] = sbuf([P, t1 - t0], F32, "first_result_%d_%d" % (b, t0))
             offsets = first_slots[:, t0 // LIST_COLUMN : t1 // LIST_COLUMN]
             scalar.activation(first_results[b, t0][:], y_half[b][:].indirect(offsets), COPY)
 
         def add_second(b, t0, t1, total=None, base=None):
             if total is None:
-                total, base = ring_tile(vector, [P, T], F32, "total_%d_%d" % (b, t0)), t0
+                total, base = sbuf([P, T - t0], F32, "total_%d_%d" % (b, t0)), t0
             offsets = second_slots[:, t0 // LIST_COLUMN : t1 // LIST_COLUMN]
             vector.tensor_tensor(total[:, t0 - base : t1 - base], y_half[b][:].indirect(offsets), first_results[b, t0][:], ADD)
             return total, base
@@ -235,94 +258,103 @@ def tile_moe_pre_mlp_relu_kernel(
         def store(b, t1, total, base):
             nc.sync.dma_start(out[b * P : (b + 1) * P, base:t1], total[:, 0 : t1 - base])
 
-        gather_x(vector, 0, 896, 1280, first_cut=1024)
+        gather_x(vector, 0, 896, 1280, planes=[0], buffer="spread")
+        spread_gates(0, 1024)
+        gather_x(vector, 0, 896, 1280, planes=[1, 2, 3])
         for d in range(PACK):
-            gather_x(scalar, 0, 0, 384, planes=[d])
-            gather_x(scalar, 0, 384, 896, planes=[d])
-        group_x(0, 896, 1280)
-        gather_x(vector, 1, 0, 256)
-        quantize_x(0, 896, 1280)
-        group_x(1, 0, 256, (0, 512))
-        gather_x(scalar, 2, 0, 512)
-        group_x(0, 0, 384)
-        group_x(0, 384, 896)
-        quantize_x(0, 0, 384)
-        gather_x(vector, 1, 256, 512, planes=[0])
-        quantize_x(0, 384, 896)
-        first_layer([0], 0, 1024)
-        gather_x(vector, 1, 256, 512, planes=[1, 2, 3])
-        gather_x(scalar, 1, 512, 1024)
-        group_x(2, 0, 512)
-        group_x(1, 256, 512, (0, 512))
-        quantize_x(2, 0, 512)
-        quantize_x(1, 0, 512)
-        first_layer([2], 0, 512)
+            gather_x(scalar, 0, 0, 512, planes=[d], buffer="scalar_a")
+            gather_x(scalar, 0, 512, 896, planes=[d], buffer="scalar_b")
+        group_x(gpsimd, 0, 896, 1280)
+        gather_x(vector, 1, 0, 608, buffer="early")
+        gather_x(scalar, 1, 608, 1024)
+        group_x(gpsimd, 0, 0, 128)
+        open_grouped("last_of_gpsimd", (1, 0, 512))
+        group_x(gpsimd, 1, 0, 512)
+        open_grouped("spread", (1, 512, 1024), (0, 128, 512), (0, 512, 896))
+        group_x(vector, 1, 512, 608, unit=0, spread=True)
+        group_x(vector, 0, 128, 512, unit=0, spread=True)
+        gather_x(scalar, 2, 0, 512, buffer="scalar_a")
+        group_x(vector, 0, 512, 896, spread=True)
+        group_x(vector, 1, 608, 1024, part=512, spread=True)
+        gather_x(scalar, 2, 512, 1024, buffer="scalar_b")
+        early_planes = sbuf([P, S + 1024], U8, "early_planes", "early")
+        quantize_x(1, 0, 512, early_planes[:, S : S + 512])
+        quantize_x(0, 0, 128, early_planes[:, 0:128])
+        quantize_x(0, 128, 512, early_planes[:, 128:512])
+        first_layer([0], 0, 512)
+        quantize_x(0, 512, 896, early_planes[:, 512:896])
+        quantize_x(0, 896, 1280, early_planes[:, 896:S])
         first_layer([1], 0, 512)
-        gather_x(scalar, 2, 512, 1024)
-        group_x(1, 512, 1024)
-        gather_x(vector, 2, 1024, 1152, planes=[0, 1])
-        quantize_x(1, 512, 1024)
-        first_layer([1], 512, 1024)
-        relu_rows(scalar, 0, 256)
-        gather_x(scalar, 1, 1024, 1280)
+        first_layer([0], 512, 768)
+        open_grouped("last_of_gpsimd", (2, 0, 512))
+        group_x(vector, 2, 0, 512, spread=True)
+        quantize_x(1, 512, 1024, early_planes[:, S + 512 : S + 1024])
+        quantize_x(2, 0, 512)
+        first_layer([2], 0, 512)
+        gather_x(vector, 2, 1024, 1152, gated=True, buffer="scalar_a")
+        relu_rows(scalar, 0, 128, buffer="first_rows")
+        relu_rows(scalar, 128, 256)
         turn_h(0, 256)
-        first_layer([0], 1024, 1152)
-        group_x(2, 512, 1024)
-        gather_x(vector, 2, 1024, 1152, planes=[2, 3])
+        first_layer([1], 512, 768)
+        first_layer([0, 1], 768, 1024)
         relu_rows(scalar, 256, 512)
-        first_layer([0], 1152, 1280)
+        gather_x(scalar, 1, 1024, 1280, buffer="first_rows")
+        open_grouped("spread", (2, 512, 1024))
+        group_x(vector, 2, 512, 1024, spread=True)
+        first_layer([0], 1024, 1280)
+        group_x(vector, 2, 1024, 1152)
         quantize_x(2, 512, 1024)
         first_layer([2], 512, 1024)
-        group_h(scalar, 0, 256)
-        turn_h(256, 512)
-        group_x(2, 1024, 1152)
-        group_x(1, 1024, 1280)
-        gather_x(vector, 2, 1152, 1280, planes=[0, 1])
         quantize_x(2, 1024, 1152)
-        quantize_x(1, 1024, 1280)
+        first_layer([2], 1024, 1152)
+        gather_x(vector, 2, 1152, 1280, gated=True, buffer="last_of_gpsimd")
+        turn_h(256, 512)
+        group_x(vector, 1, 1024, 1280)
         relu_rows(scalar, 512, 768)
-        turn_h(512, 768)
-        first_layer([2, 1], 1024, 1152)
-        first_layer([1], 1152, 1280)
-        relu_rows(scalar, 768, 1024)
-        gather_x(vector, 2, 1152, 1280, planes=[2, 3])
-        quantize_h(0, 256)
-        group_h(scalar, 256, 512)
-        group_x(2, 1152, 1280)
-        turn_h(768, 1024)
-        relu_rows(scalar, 1024, 1152)
+        group_x(vector, 2, 1152, 1280)
+        quantize_x(1, 1024, 1280)
         quantize_x(2, 1152, 1280)
+        turn_h(512, 768)
+        first_layer([1], 1024, 1280)
         first_layer([2], 1152, 1280)
-        turn_h(1024, 1152)
+        group_h(vector, 0, 256)
+        relu_rows(scalar, 768, 1024)
+
+        group_h(scalar, 256, 512)
         group_h(vector, 512, 768)
-        group_h(scalar, 768, 1024)
-        quantize_h(256, 512)
+        relu_rows(vector, 1024, 1152)
         relu_rows(scalar, 1152, 1280)
+        turn_h(768, 1024)
+        quantize_h(0, 256)
+        quantize_h(256, 512)
+        turn_h(1024, 1280)
         second_layer(0, 0, 256, 512)
+        group_h(scalar, 768, 1024)
         quantize_h(512, 768)
+        group_h(scalar, 1024, 1280)
+        second_layer(1, 0, 256, 512)
         quantize_h(768, 1024)
         second_layer(0, 512, 768, 1024)
-        turn_h(1152, 1280)
-        group_h(scalar, 1024, 1152)
-        second_layer(1, 0, 256, 512)
-        keep_y(vector, 0, 0, 512)
-        group_h(scalar, 1152, 1280)
-        quantize_h(1024, 1152)
+        keep_y(scalar, 0, 0, 512)
+        quantize_h(1024, 1280)
+        second_layer(0, 1024, 1280)
         second_layer(1, 512, 768, 1024)
-        keep_y(scalar, 0, 512, 1024)
-        quantize_h(1152, 1280)
-        second_layer(0, 1024, 1152, 1280)
-        second_layer(1, 1024, 1152, 1280)
-        keep_y(vector, 1, 0, 512)
+        second_layer(1, 1024, 1280)
+        keep_y(vector, 0, 512, 1024)
+        keep_y(scalar, 1, 0, 512)
         keep_y(scalar, 0, 1024, 1280)
         keep_y(vector, 1, 512, 1024)
         keep_y(vector, 1, 1024, 1280)
 
-        for b, t0, t1 in ((0, 0, 128), (0, 128, 384), (0, 384, 640), (1, 0, 384), (1, 384, 640)):
-            fetch_first(b, t0, t1)
-        total = add_second(0, 0, 128)
-        add_second(0, 128, 384, *total)
-        add_second(0, 384, 640, *total)
+        pieces = ((0, 192), (192, 416), (416, 640))
+        for b in range(2):
+            for t0, t1 in pieces:
+                fetch_first(b, t0, t1)
+        total = add_second(0, *pieces[0])
+        add_second(0, *pieces[1], *total)
+        add_second(0, *pieces[2], *total)
         store(0, 640, *total)
-        store(1, 384, *add_second(1, 0, 384))
-        store(1, 640, *add_second(1, 384, 640))
+        total = add_second(1, *pieces[0])
+        add_second(1, *pieces[1], *total)
+        store(1, 416, *total)
+        store(1, 640, *add_second(1, *pieces[2]))

@@ -116,7 +116,7 @@ def tile_moe_pre_mlp_relu_kernel(
 
         x_gathered, x_grouped, x_operand, a_banks, a_passes = {}, {}, {}, {}, {}
         h_rows, h_turned, h_grouped, h_operand = {}, {}, {}, {}
-        y_banks, first_results, gate_banks = {}, {}, {}
+        y_banks, first_results, gate_banks, x_whole = {}, {}, {}, {}
 
         def gather_x(engine, g, s0, s1, planes=range(PACK), gated=False, buffer=None, first_cut=None):
             if (g, s0) not in x_gathered:
@@ -141,6 +141,7 @@ def tile_moe_pre_mlp_relu_kernel(
             for g, s0, s1 in parts:
                 x_grouped[g, s0] = tile[:, c0 : c0 + s1 - s0, :]
                 c0 = c0 + s1 - s0
+            x_whole[parts[0][0:2]] = tile
 
         def group_x(engine, g, s0, s1, unit=None, part=None, spread=False):
             u0 = s0 if unit is None else unit
@@ -157,6 +158,12 @@ def tile_moe_pre_mlp_relu_kernel(
                 source = gate_banks[bank0][:, s0 - bank0 : s1 - bank0] if spread else gates[:, s0:s1]
                 weights = source.rearrange("p (c o i) -> p c o i", o=1, i=4).to_broadcast([P, (s1 - s0) // 4, PACK, 4])
                 engine.tensor_tensor(grouped, planes, weights, MULT)
+
+        def group_all(engine, g, s0, s1):
+            grouped = x_whole[g, s0][:].rearrange("p (c i) d -> p c d i", i=4)
+            planes = x_gathered[g, s0][1][:].rearrange("p d (c i) -> p c d i", i=4)
+            weights = gates[:, s0:s1].rearrange("p (c o i) -> p c o i", o=1, i=4).to_broadcast([P, (s1 - s0) // 4, PACK, 4])
+            engine.tensor_tensor(grouped, planes, weights, MULT)
 
         def spread_gates(s0, s1):
             turned = psum.tile([P, P], F32, name="gate_turned", tag="bank")
@@ -214,10 +221,12 @@ def tile_moe_pre_mlp_relu_kernel(
                     nc.tensor.transpose(turned[:, u, b0 - s0 : b0 - s0 + P], pairs[:, u * P : (u + 1) * P], identity[:])
             h_turned[s0] = turned
 
-        def group_h(engine, s0, s1, buffer=None):
-            grouped = sbuf([P, (s1 - s0) * PACK], BF16, "h_grouped_%d" % s0, buffer)
-            copy(engine, grouped[:].bitcast(F32).rearrange("p (s u) -> p s u", u=2), h_turned[s0][:].rearrange("p u s -> p s u"))
-            h_grouped[s0] = grouped
+        def group_h(engine, s0, s1, into=None):
+            t0, t1 = into or (s0, s1)
+            if t0 not in h_grouped:
+                h_grouped[t0] = sbuf([P, (t1 - t0) * PACK], BF16, "h_grouped_%d" % t0)
+            grouped = h_grouped[t0][:, (s0 - t0) * PACK : (s1 - t0) * PACK]
+            copy(engine, grouped.bitcast(F32).rearrange("p (s u) -> p s u", u=2), h_turned[s0][:].rearrange("p u s -> p s u"))
 
         def quantize_h(s0, s1):
             h_codes = sbuf([P, s1 - s0], U32, "h_codes_%d" % s0)
@@ -264,31 +273,33 @@ def tile_moe_pre_mlp_relu_kernel(
         for d in range(PACK):
             gather_x(scalar, 0, 0, 512, planes=[d], buffer="scalar_a")
             gather_x(scalar, 0, 512, 896, planes=[d], buffer="scalar_b")
-        group_x(gpsimd, 0, 896, 1280)
-        gather_x(vector, 1, 0, 608, buffer="early")
-        gather_x(scalar, 1, 608, 1024)
+        open_grouped(None, (0, 896, 1024), (0, 1024, 1280))
+        group_all(gpsimd, 0, 896, 1280)
+        gather_x(vector, 1, 0, 576, buffer="early")
+        gather_x(scalar, 1, 576, 1024)
         group_x(gpsimd, 0, 0, 128)
         open_grouped("last_of_gpsimd", (1, 0, 512))
-        group_x(gpsimd, 1, 0, 512)
+        group_x(gpsimd, 1, 0, 256)
         open_grouped("spread", (1, 512, 1024), (0, 128, 512), (0, 512, 896))
-        group_x(vector, 1, 512, 608, unit=0, spread=True)
+        group_x(vector, 1, 512, 576, unit=0, spread=True)
         group_x(vector, 0, 128, 512, unit=0, spread=True)
+        group_x(vector, 1, 256, 512, unit=0, part=0, spread=True)
         gather_x(scalar, 2, 0, 512, buffer="scalar_a")
         group_x(vector, 0, 512, 896, spread=True)
-        group_x(vector, 1, 608, 1024, part=512, spread=True)
+        group_x(vector, 1, 576, 1024, part=512, spread=True)
         gather_x(scalar, 2, 512, 1024, buffer="scalar_b")
-        early_planes = sbuf([P, S + 1024], U8, "early_planes", "early")
-        quantize_x(1, 0, 512, early_planes[:, S : S + 512])
+        early_planes = sbuf([P, 2048], U8, "early_planes", "early")
+        quantize_x(1, 0, 512, early_planes[:, 1024:1536])
         quantize_x(0, 0, 128, early_planes[:, 0:128])
         quantize_x(0, 128, 512, early_planes[:, 128:512])
         first_layer([0], 0, 512)
         quantize_x(0, 512, 896, early_planes[:, 512:896])
-        quantize_x(0, 896, 1280, early_planes[:, 896:S])
+        quantize_x(0, 896, 1024, early_planes[:, 896:1024])
         first_layer([1], 0, 512)
         first_layer([0], 512, 768)
         open_grouped("last_of_gpsimd", (2, 0, 512))
         group_x(vector, 2, 0, 512, spread=True)
-        quantize_x(1, 512, 1024, early_planes[:, S + 512 : S + 1024])
+        quantize_x(1, 512, 1024, early_planes[:, 1536:2048])
         quantize_x(2, 0, 512)
         first_layer([2], 0, 512)
         gather_x(vector, 2, 1024, 1152, gated=True, buffer="scalar_a")
@@ -301,42 +312,46 @@ def tile_moe_pre_mlp_relu_kernel(
         gather_x(scalar, 1, 1024, 1280, buffer="first_rows")
         open_grouped("spread", (2, 512, 1024))
         group_x(vector, 2, 512, 1024, spread=True)
-        first_layer([0], 1024, 1280)
         group_x(vector, 2, 1024, 1152)
         quantize_x(2, 512, 1024)
         first_layer([2], 512, 1024)
         quantize_x(2, 1024, 1152)
-        first_layer([2], 1024, 1152)
         gather_x(vector, 2, 1152, 1280, gated=True, buffer="last_of_gpsimd")
+        late_plane = sbuf([P, 256], U8, "late_plane", "spread")
+        quantize_x(0, 1024, 1280, late_plane[:])
         turn_h(256, 512)
+        first_layer([0, 2], 1024, 1152)
+        first_layer([0], 1152, 1280)
+        group_x(vector, 2, 1152, 1280)
         group_x(vector, 1, 1024, 1280)
         relu_rows(scalar, 512, 768)
-        group_x(vector, 2, 1152, 1280)
-        quantize_x(1, 1024, 1280)
         quantize_x(2, 1152, 1280)
         turn_h(512, 768)
-        first_layer([1], 1024, 1280)
         first_layer([2], 1152, 1280)
-        group_h(vector, 0, 256)
         relu_rows(scalar, 768, 1024)
-
+        quantize_x(1, 1024, 1280)
+        first_layer([1], 1152, 1280)
+        first_layer([1], 1024, 1152)
+        turn_h(768, 1024)
+        group_h(scalar, 0, 256)
         group_h(scalar, 256, 512)
         group_h(vector, 512, 768)
-        relu_rows(vector, 1024, 1152)
-        relu_rows(scalar, 1152, 1280)
-        turn_h(768, 1024)
         quantize_h(0, 256)
-        quantize_h(256, 512)
-        turn_h(1024, 1280)
-        second_layer(0, 0, 256, 512)
+        relu_rows(scalar, 1152, 1280)
+        relu_rows(vector, 1024, 1152)
+        turn_h(1152, 1280)
+        turn_h(1024, 1152)
         group_h(scalar, 768, 1024)
+        quantize_h(256, 512)
+        second_layer(0, 0, 256, 512)
+        group_h(scalar, 1152, 1280, (1024, 1280))
+        group_h(scalar, 1024, 1152, (1024, 1280))
         quantize_h(512, 768)
-        group_h(scalar, 1024, 1280)
         second_layer(1, 0, 256, 512)
         quantize_h(768, 1024)
         second_layer(0, 512, 768, 1024)
-        keep_y(scalar, 0, 0, 512)
         quantize_h(1024, 1280)
+        keep_y(scalar, 0, 0, 512)
         second_layer(0, 1024, 1280)
         second_layer(1, 512, 768, 1024)
         second_layer(1, 1024, 1280)

@@ -103,10 +103,11 @@ def tile_moe_pre_mlp_relu_kernel(
         nc.sync.dma_start(slot_tokens[:], offs)
         nc.sync.dma_start(gate_rows[0:GATE_ROWS, :], gate[0, 0 : GATE_ROWS * P].rearrange("(b m) -> b m", m=P))
         load_tokens(1, 2, 3, 4)
-        load_gates(896, S)
+        load_gates(864, S)
         load_tokens(5, 6, 7)
         load_gates(0, 512)
         load_tokens(8, 9, 10, 11)
+        load_gates(768, 864)
 
         for experts in ([0, 1], [2, 3], [4]):
             rows = slice(experts[0] * PASSES, (experts[-1] + 1) * PASSES)
@@ -159,8 +160,9 @@ def tile_moe_pre_mlp_relu_kernel(
                 weights = source.rearrange("p (c o i) -> p c o i", o=1, i=4).to_broadcast([P, (s1 - s0) // 4, PACK, 4])
                 engine.tensor_tensor(grouped, planes, weights, MULT)
 
-        def group_all(engine, g, s0, s1):
-            grouped = x_whole[g, s0][:].rearrange("p (c i) d -> p c d i", i=4)
+        def group_all(engine, g, s0, s1, t0=None):
+            t0 = s0 if t0 is None else t0
+            grouped = x_whole[g, t0][:, s0 - t0 : s1 - t0, :].rearrange("p (c i) d -> p c d i", i=4)
             planes = x_gathered[g, s0][1][:].rearrange("p d (c i) -> p c d i", i=4)
             weights = gates[:, s0:s1].rearrange("p (c o i) -> p c o i", o=1, i=4).to_broadcast([P, (s1 - s0) // 4, PACK, 4])
             engine.tensor_tensor(grouped, planes, weights, MULT)
@@ -267,57 +269,67 @@ def tile_moe_pre_mlp_relu_kernel(
         def store(b, t1, total, base):
             nc.sync.dma_start(out[b * P : (b + 1) * P, base:t1], total[:, 0 : t1 - base])
 
-        gather_x(vector, 0, 896, 1280, planes=[0], buffer="spread")
+        gather_x(vector, 0, 864, 1280, planes=[0], buffer="spread")
         spread_gates(0, 1024)
-        gather_x(vector, 0, 896, 1280, planes=[1, 2, 3])
+        gather_x(vector, 0, 864, 1280, planes=[1, 2, 3])
         for d in range(PACK):
             gather_x(scalar, 0, 0, 512, planes=[d], buffer="scalar_a")
-            gather_x(scalar, 0, 512, 896, planes=[d], buffer="scalar_b")
-        open_grouped(None, (0, 896, 1024), (0, 1024, 1280))
-        group_all(gpsimd, 0, 896, 1280)
-        gather_x(vector, 1, 0, 576, buffer="early")
-        gather_x(scalar, 1, 576, 1024)
+            gather_x(scalar, 0, 512, 864, planes=[d], buffer="scalar_b")
+        open_grouped(None, (0, 768, 1024), (0, 1024, 1280))
+        group_all(gpsimd, 0, 864, 1280, 768)
+        gather_x(vector, 1, 0, 608, buffer="early")
+        gather_x(scalar, 1, 608, 1024)
+        open_grouped("first_block", (0, 0, 128))
         group_x(gpsimd, 0, 0, 128)
         open_grouped("last_of_gpsimd", (1, 0, 512))
         group_x(gpsimd, 1, 0, 256)
-        open_grouped("spread", (1, 512, 1024), (0, 128, 512), (0, 512, 896))
-        group_x(vector, 1, 512, 576, unit=0, spread=True)
+        open_grouped("spread", (1, 512, 768), (0, 128, 512), (0, 512, 768))
         group_x(vector, 0, 128, 512, unit=0, spread=True)
+        group_x(vector, 1, 512, 608, unit=0, spread=True)
         group_x(vector, 1, 256, 512, unit=0, part=0, spread=True)
         gather_x(scalar, 2, 0, 512, buffer="scalar_a")
-        group_x(vector, 0, 512, 896, spread=True)
-        group_x(vector, 1, 576, 1024, part=512, spread=True)
+        group_x(vector, 0, 512, 768, spread=True)
+        group_x(vector, 0, 768, 864, unit=512, spread=True)
+        group_x(vector, 1, 608, 768, part=512, spread=True)
         gather_x(scalar, 2, 512, 1024, buffer="scalar_b")
-        early_planes = sbuf([P, 2048], U8, "early_planes", "early")
-        quantize_x(1, 0, 512, early_planes[:, 1024:1536])
+        early_planes = sbuf([P, 1792], U8, "early_planes", "early")
         quantize_x(0, 0, 128, early_planes[:, 0:128])
         quantize_x(0, 128, 512, early_planes[:, 128:512])
         first_layer([0], 0, 512)
-        quantize_x(0, 512, 896, early_planes[:, 512:896])
-        quantize_x(0, 896, 1024, early_planes[:, 896:1024])
+        quantize_x(0, 512, 768, early_planes[:, 512:768])
+        quantize_x(0, 768, 1024, early_planes[:, 768:1024])
+        quantize_x(1, 0, 512, early_planes[:, 1024:1536])
         first_layer([1], 0, 512)
         first_layer([0], 512, 768)
-        open_grouped("last_of_gpsimd", (2, 0, 512))
+        open_grouped("last_of_gpsimd", (1, 768, 896))
+        group_x(gpsimd, 1, 768, 896, unit=608)
+        open_grouped("first_block", (2, 0, 512))
         group_x(vector, 2, 0, 512, spread=True)
-        quantize_x(1, 512, 1024, early_planes[:, 1536:2048])
+        quantize_x(1, 512, 768, early_planes[:, 1536:1792])
         quantize_x(2, 0, 512)
         first_layer([2], 0, 512)
-        gather_x(vector, 2, 1024, 1152, gated=True, buffer="scalar_a")
+        quantize_x(1, 768, 896)
+        open_grouped("last_of_gpsimd", (1, 896, 1024))
+        group_x(gpsimd, 1, 896, 1024, unit=608)
+        gather_x(vector, 2, 1024, 1152, buffer="scalar_a")
+        group_x(gpsimd, 2, 1024, 1152)
         relu_rows(scalar, 0, 128, buffer="first_rows")
         relu_rows(scalar, 128, 256)
         turn_h(0, 256)
         first_layer([1], 512, 768)
-        first_layer([0, 1], 768, 1024)
+        first_layer([0, 1], 768, 896)
+        first_layer([0], 896, 1024)
         relu_rows(scalar, 256, 512)
         gather_x(scalar, 1, 1024, 1280, buffer="first_rows")
-        open_grouped("spread", (2, 512, 1024))
+        open_grouped("first_block", (2, 512, 1024))
         group_x(vector, 2, 512, 1024, spread=True)
-        group_x(vector, 2, 1024, 1152)
+        quantize_x(1, 896, 1024)
+        first_layer([1], 896, 1024)
+        quantize_x(2, 1024, 1152)
         quantize_x(2, 512, 1024)
         first_layer([2], 512, 1024)
-        quantize_x(2, 1024, 1152)
-        gather_x(vector, 2, 1152, 1280, gated=True, buffer="last_of_gpsimd")
-        late_plane = sbuf([P, 256], U8, "late_plane", "spread")
+        gather_x(vector, 2, 1152, 1280, gated=True, buffer="scalar_b")
+        late_plane = sbuf([P, 256], U8, "late_plane", "first_block")
         quantize_x(0, 1024, 1280, late_plane[:])
         turn_h(256, 512)
         first_layer([0, 2], 1024, 1152)

@@ -103,11 +103,11 @@ def tile_moe_pre_mlp_relu_kernel(
         nc.sync.dma_start(slot_tokens[:], offs)
         nc.sync.dma_start(gate_rows[0:GATE_ROWS, :], gate[0, 0 : GATE_ROWS * P].rearrange("(b m) -> b m", m=P))
         load_tokens(1, 2, 3, 4)
-        load_gates(864, S)
+        load_gates(800, S)
         load_tokens(5, 6, 7)
         load_gates(0, 512)
         load_tokens(8, 9, 10, 11)
-        load_gates(768, 864)
+        load_gates(768, 800)
 
         for experts in ([0, 1], [2, 3], [4]):
             rows = slice(experts[0] * PASSES, (experts[-1] + 1) * PASSES)
@@ -158,13 +158,17 @@ def tile_moe_pre_mlp_relu_kernel(
                 bank0 = s0 // BANK * BANK
                 source = gate_banks[bank0][:, s0 - bank0 : s1 - bank0] if spread else gates[:, s0:s1]
                 weights = source.rearrange("p (c o i) -> p c o i", o=1, i=4).to_broadcast([P, (s1 - s0) // 4, PACK, 4])
+                if engine is gpsimd:
+                    grouped = x_grouped[g, t0][:, s0 - t0 : s1 - t0, :]
+                    planes = gathered[:, :, s0 - u0 : s1 - u0].rearrange("p d s -> p s d")
+                    weights = source.rearrange("p (s o) -> p s o", o=1).to_broadcast([P, s1 - s0, PACK])
                 engine.tensor_tensor(grouped, planes, weights, MULT)
 
         def group_all(engine, g, s0, s1, t0=None):
             t0 = s0 if t0 is None else t0
-            grouped = x_whole[g, t0][:, s0 - t0 : s1 - t0, :].rearrange("p (c i) d -> p c d i", i=4)
-            planes = x_gathered[g, s0][1][:].rearrange("p d (c i) -> p c d i", i=4)
-            weights = gates[:, s0:s1].rearrange("p (c o i) -> p c o i", o=1, i=4).to_broadcast([P, (s1 - s0) // 4, PACK, 4])
+            grouped = x_whole[g, t0][:, s0 - t0 : s1 - t0, :]
+            planes = x_gathered[g, s0][1][:].rearrange("p d s -> p s d")
+            weights = gates[:, s0:s1].rearrange("p (s o) -> p s o", o=1).to_broadcast([P, s1 - s0, PACK])
             engine.tensor_tensor(grouped, planes, weights, MULT)
 
         def spread_gates(s0, s1):
@@ -269,27 +273,27 @@ def tile_moe_pre_mlp_relu_kernel(
         def store(b, t1, total, base):
             nc.sync.dma_start(out[b * P : (b + 1) * P, base:t1], total[:, 0 : t1 - base])
 
-        gather_x(vector, 0, 864, 1280, planes=[0], buffer="spread")
+        gather_x(vector, 0, 800, 1280, planes=[0], buffer="spread")
         spread_gates(0, 1024)
-        gather_x(vector, 0, 864, 1280, planes=[1, 2, 3])
+        gather_x(vector, 0, 800, 1280, planes=[1, 2, 3])
         for d in range(PACK):
-            gather_x(scalar, 0, 0, 512, planes=[d], buffer="scalar_a")
-            gather_x(scalar, 0, 512, 864, planes=[d], buffer="scalar_b")
+            gather_x(scalar, 0, 0, 512, planes=[d])
+            gather_x(scalar, 0, 512, 800, planes=[d], buffer="scalar_b")
         open_grouped(None, (0, 768, 1024), (0, 1024, 1280))
-        group_all(gpsimd, 0, 864, 1280, 768)
+        group_all(gpsimd, 0, 800, 1280, 768)
         gather_x(vector, 1, 0, 608, buffer="early")
         gather_x(scalar, 1, 608, 1024)
         open_grouped("first_block", (0, 0, 128))
         group_x(gpsimd, 0, 0, 128)
         open_grouped("last_of_gpsimd", (1, 0, 512))
-        group_x(gpsimd, 1, 0, 256)
+        group_x(gpsimd, 1, 0, 320)
         open_grouped("spread", (1, 512, 768), (0, 128, 512), (0, 512, 768))
         group_x(vector, 0, 128, 512, unit=0, spread=True)
         group_x(vector, 1, 512, 608, unit=0, spread=True)
-        group_x(vector, 1, 256, 512, unit=0, part=0, spread=True)
-        gather_x(scalar, 2, 0, 512, buffer="scalar_a")
+        group_x(vector, 1, 320, 512, unit=0, part=0, spread=True)
+        gather_x(scalar, 2, 0, 512)
         group_x(vector, 0, 512, 768, spread=True)
-        group_x(vector, 0, 768, 864, unit=512, spread=True)
+        group_x(vector, 0, 768, 800, unit=512, spread=True)
         group_x(vector, 1, 608, 768, part=512, spread=True)
         gather_x(scalar, 2, 512, 1024, buffer="scalar_b")
         early_planes = sbuf([P, 1792], U8, "early_planes", "early")
@@ -311,7 +315,7 @@ def tile_moe_pre_mlp_relu_kernel(
         quantize_x(1, 768, 896)
         open_grouped("last_of_gpsimd", (1, 896, 1024))
         group_x(gpsimd, 1, 896, 1024, unit=608)
-        gather_x(vector, 2, 1024, 1152, buffer="scalar_a")
+        gather_x(vector, 2, 1024, 1152, buffer="spread")
         group_x(gpsimd, 2, 1024, 1152)
         relu_rows(scalar, 0, 128, buffer="first_rows")
         relu_rows(scalar, 128, 256)

@@ -61,14 +61,14 @@ def tile_moe_pre_mlp_relu_kernel(
         identity = sbuf([P, P], F32, "identity")
         y_half = [sbuf([P, S], F32, "y_half_%d" % b) for b in range(N // P)]
 
+        warm = keep.tile([P, 16], F32, name="warm")
+        vector.memset(warm[:, 0:8], 0.0)
+        scalar.activation(warm[:, 8:16], warm[:, 0:8], COPY)
+
         vector.memset(gate_rows[:], 0.0)
         vector.memset(w1_plane[:].rearrange("p a b -> p (a b)").bitcast(I32), 0)
         vector.memset(w2_plane[:].rearrange("p a b -> p (a b)").bitcast(I32), 0)
         make_identity(nc, identity[:])
-
-        warm = keep.tile([P, 16], F32, name="warm")
-        nc.gpsimd.memset(warm[:, 0:8], 0.0)
-        scalar.activation(warm[:, 8:16], warm[:, 0:8], COPY)
 
         x_rows = xT.rearrange("(g p d) t -> g d p t", p=P, d=PACK)
 
@@ -227,10 +227,10 @@ def tile_moe_pre_mlp_relu_kernel(
                     nc.tensor.transpose(turned[:, u, b0 - s0 : b0 - s0 + P], pairs[:, u * P : (u + 1) * P], identity[:])
             h_turned[s0] = turned
 
-        def group_h(engine, s0, s1, into=None):
+        def group_h(engine, s0, s1, into=None, buffer=None):
             t0, t1 = into or (s0, s1)
             if t0 not in h_grouped:
-                h_grouped[t0] = sbuf([P, (t1 - t0) * PACK], BF16, "h_grouped_%d" % t0)
+                h_grouped[t0] = sbuf([P, (t1 - t0) * PACK], BF16, "h_grouped_%d" % t0, buffer)
             grouped = h_grouped[t0][:, (s0 - t0) * PACK : (s1 - t0) * PACK]
             copy(engine, grouped.bitcast(F32).rearrange("p (s u) -> p s u", u=2), h_turned[s0][:].rearrange("p u s -> p s u"))
 
@@ -286,11 +286,11 @@ def tile_moe_pre_mlp_relu_kernel(
         open_grouped("first_block", (0, 0, 128))
         group_x(gpsimd, 0, 0, 128)
         open_grouped("last_of_gpsimd", (1, 0, 512))
-        group_x(gpsimd, 1, 0, 320)
+        group_x(gpsimd, 1, 0, 288)
         open_grouped("spread", (1, 512, 768), (0, 128, 512), (0, 512, 768))
         group_x(vector, 0, 128, 512, unit=0, spread=True)
         group_x(vector, 1, 512, 608, unit=0, spread=True)
-        group_x(vector, 1, 320, 512, unit=0, part=0, spread=True)
+        group_x(vector, 1, 288, 512, unit=0, part=0, spread=True)
         gather_x(scalar, 2, 0, 512)
         group_x(vector, 0, 512, 768, spread=True)
         group_x(vector, 0, 768, 800, unit=512, spread=True)

@@ -10,6 +10,15 @@ PACK = 4
 PASSES = K // (P * PACK)
 LIST_COLUMN = 16
 QUADRANT = 32
+PSUM_BANKS = 8
+BANK = 512
+GATE_ROWS = 8
+WALK = 4
+
+FIRST_SPLIT = 800
+SECOND_SPLIT = 608
+POOL_SPLIT = 288
+RESULT_CUTS = (0, 192, 416, T)
 
 FLOPS = 2 * S * (K * H + H * N)
 BYTES = 4 * K * T + E * (K * H + H * N) // 2 + E * (K * H + H * N) // 32 + 4 * S + 2 * P * (S + 2 * T) // 16 + 4 * N * T
@@ -26,8 +35,6 @@ MULT = mybir.AluOpType.mult
 ADD = mybir.AluOpType.add
 COPY = mybir.ActivationFunctionType.Copy
 RELU = mybir.ActivationFunctionType.Relu
-
-PSUM_BANKS, BANK, GATE_ROWS = 8, 512, 8
 
 
 def tile_moe_pre_mlp_relu_kernel(
@@ -85,55 +92,45 @@ def tile_moe_pre_mlp_relu_kernel(
             for quad in range(P // QUADRANT):
                 nc.sync.dma_start(plane[QUADRANT * quad : QUADRANT * quad + 4].bitcast(I32), scale_rows[4 * quad : 4 * quad + 4])
 
-        def load_w1(experts, passes):
-            rows = [(e, g) for e in experts for g in passes]
-            words = sbuf([P, len(rows), 2 * H], U8, "w1_codes_%d_%d" % rows[0])
-            source = w1_words[experts[0] : experts[-1] + 1, passes[0] : passes[-1] + 1]
-            nc.sync.dma_start(words[:].bitcast(I32), source.rearrange("e s p b -> p (e s) b").bitcast(I32))
-            for place, row in enumerate(rows):
-                w1_codes[row] = words[:, place, :]
-
-        def load_w2_and_lists():
-            load_scales(w2_plane, w2_scales)
-            nc.sync.dma_start(w2_codes[:].bitcast(I32), w2_words.rearrange("e s p b -> p (e s) b").bitcast(I32))
-            nc.sync.dma_start(first_slots[:], pos1)
-            nc.sync.dma_start(second_slots[:], pos2)
+        def load_w1(e0, e1):
+            load_scales(w1_plane[:, e0 * PASSES : e1 * PASSES, :], w1_scales[e0:e1])
+            words = sbuf([P, (e1 - e0) * PASSES, 2 * H], U8, "w1_codes_%d" % e0)
+            nc.sync.dma_start(words[:].bitcast(I32), w1_words[e0:e1].rearrange("e s p b -> p (e s) b").bitcast(I32))
+            for row in range((e1 - e0) * PASSES):
+                w1_codes[e0 * PASSES + row] = words[:, row, :]
 
         load_tokens(0)
         nc.sync.dma_start(slot_tokens[:], offs)
         nc.sync.dma_start(gate_rows[0:GATE_ROWS, :], gate[0, 0 : GATE_ROWS * P].rearrange("(b m) -> b m", m=P))
         load_tokens(1, 2, 3, 4)
-        load_gates(800, S)
+        load_gates(6 * P, S)
         load_tokens(5, 6, 7)
-        load_gates(0, 512)
+        load_gates(0, POOL_SPLIT)
         load_tokens(8, 9, 10, 11)
-        load_gates(768, 800)
-
-        for experts in ([0, 1], [2, 3], [4]):
-            rows = slice(experts[0] * PASSES, (experts[-1] + 1) * PASSES)
-            load_scales(w1_plane[:, rows, :], w1_scales[experts[0] : experts[-1] + 1])
-            load_w1(experts, [0, 1, 2])
-        load_w2_and_lists()
+        load_w1(0, 2)
+        load_w1(2, 4)
+        load_w1(4, 5)
+        load_scales(w2_plane, w2_scales)
+        nc.sync.dma_start(w2_codes[:].bitcast(I32), w2_words.rearrange("e s p b -> p (e s) b").bitcast(I32))
+        nc.sync.dma_start(first_slots[:], pos1)
+        nc.sync.dma_start(second_slots[:], pos2)
 
         x_gathered, x_grouped, x_operand, a_banks, a_passes = {}, {}, {}, {}, {}
         h_rows, h_turned, h_grouped, h_operand = {}, {}, {}, {}
-        y_banks, first_results, gate_banks, x_whole = {}, {}, {}, {}
+        y_banks, first_results, gate_banks = {}, {}, {}
 
-        def gather_x(engine, g, s0, s1, planes=range(PACK), gated=False, buffer=None, first_cut=None):
+        def gather_x(engine, g, s0, s1, planes=range(PACK), gated=False, buffer=None):
             if (g, s0) not in x_gathered:
-                x_gathered[g, s0] = (gated, sbuf([P, PACK, s1 - s0], F32, "gathered_%d_%d" % (g, s0), buffer))
-            gated, gathered = x_gathered[g, s0]
+                x_gathered[g, s0] = sbuf([P, PACK, s1 - s0], F32, "gathered_%d_%d" % (g, s0), buffer)
             for d in planes:
-                cuts = [s0, first_cut, s1] if first_cut and d == 0 else [s0, s1]
-                for c0, c1 in zip(cuts, cuts[1:]):
-                    window = tokens[g][d][:].indirect(slot_tokens[:, c0 // LIST_COLUMN : c1 // LIST_COLUMN])
-                    plane = gathered[:, d, c0 - s0 : c1 - s0]
-                    if gated:
-                        vector.tensor_tensor(plane, window, gates[:, c0:c1], MULT)
-                    elif engine is vector:
-                        vector.tensor_copy(plane, window)
-                    else:
-                        scalar.activation(plane, window, COPY)
+                window = tokens[g][d][:].indirect(slot_tokens[:, s0 // LIST_COLUMN : s1 // LIST_COLUMN])
+                plane = x_gathered[g, s0][:, d, :]
+                if gated:
+                    vector.tensor_tensor(plane, window, gates[:, s0:s1], MULT)
+                elif engine is vector:
+                    vector.tensor_copy(plane, window)
+                else:
+                    scalar.activation(plane, window, COPY)
 
         def open_grouped(buffer, *parts):
             name = "x_grouped_%d_%d" % parts[0][0:2]
@@ -142,41 +139,37 @@ def tile_moe_pre_mlp_relu_kernel(
             for g, s0, s1 in parts:
                 x_grouped[g, s0] = tile[:, c0 : c0 + s1 - s0, :]
                 c0 = c0 + s1 - s0
-            x_whole[parts[0][0:2]] = tile
 
-        def group_x(engine, g, s0, s1, unit=None, part=None, spread=False):
-            u0 = s0 if unit is None else unit
-            t0 = s0 if part is None else part
-            if (g, t0) not in x_grouped:
+        def operands(g, s0, s1, unit, part):
+            unit = s0 if unit is None else unit
+            part = s0 if part is None else part
+            if (g, part) not in x_grouped:
                 open_grouped(None, (g, s0, s1))
-            gated, gathered = x_gathered[g, u0]
-            grouped = x_grouped[g, t0][:, s0 - t0 : s1 - t0, :].rearrange("p (c i) d -> p c d i", i=4)
-            planes = gathered[:, :, s0 - u0 : s1 - u0].rearrange("p d (c i) -> p c d i", i=4)
-            if gated:
-                vector.tensor_copy(grouped, planes)
-            else:
-                bank0 = s0 // BANK * BANK
-                source = gate_banks[bank0][:, s0 - bank0 : s1 - bank0] if spread else gates[:, s0:s1]
-                weights = source.rearrange("p (c o i) -> p c o i", o=1, i=4).to_broadcast([P, (s1 - s0) // 4, PACK, 4])
-                if engine is gpsimd:
-                    grouped = x_grouped[g, t0][:, s0 - t0 : s1 - t0, :]
-                    planes = gathered[:, :, s0 - u0 : s1 - u0].rearrange("p d s -> p s d")
-                    weights = source.rearrange("p (s o) -> p s o", o=1).to_broadcast([P, s1 - s0, PACK])
-                engine.tensor_tensor(grouped, planes, weights, MULT)
+            return x_grouped[g, part][:, s0 - part : s1 - part, :], x_gathered[g, unit][:, :, s0 - unit : s1 - unit]
 
-        def group_all(engine, g, s0, s1, t0=None):
-            t0 = s0 if t0 is None else t0
-            grouped = x_whole[g, t0][:, s0 - t0 : s1 - t0, :]
-            planes = x_gathered[g, s0][1][:].rearrange("p d s -> p s d")
+        def multiply_on_gpsimd(g, s0, s1, unit=None, part=None):
+            grouped, planes = operands(g, s0, s1, unit, part)
             weights = gates[:, s0:s1].rearrange("p (s o) -> p s o", o=1).to_broadcast([P, s1 - s0, PACK])
-            engine.tensor_tensor(grouped, planes, weights, MULT)
+            gpsimd.tensor_tensor(grouped, planes.rearrange("p d s -> p s d"), weights, MULT)
 
-        def spread_gates(s0, s1):
+        def multiply_on_vector(g, s0, s1, unit=None, part=None):
+            grouped, planes = operands(g, s0, s1, unit, part)
+            bank0 = s0 // BANK * BANK
+            source = gate_banks[bank0][:, s0 - bank0 : s1 - bank0] if bank0 in gate_banks else gates[:, s0:s1]
+            weights = source.rearrange("p (c o i) -> p c o i", o=1, i=WALK).to_broadcast([P, (s1 - s0) // WALK, PACK, WALK])
+            grouped = grouped.rearrange("p (c i) d -> p c d i", i=WALK)
+            vector.tensor_tensor(grouped, planes.rearrange("p d (c i) -> p c d i", i=WALK), weights, MULT)
+
+        def round_gated(g, s0, s1):
+            grouped, planes = operands(g, s0, s1, None, None)
+            vector.tensor_copy(grouped.rearrange("p (c i) d -> p c d i", i=WALK), planes.rearrange("p d (c i) -> p c d i", i=WALK))
+
+        def spread_gates():
             turned = psum.tile([P, P], F32, name="gate_turned", tag="bank")
             nc.tensor.transpose(turned[:], gate_rows[:], identity[:])
             columns = sbuf([P, GATE_ROWS], F32, "gate_columns")
             vector.tensor_copy(columns[:], turned[:, 0:GATE_ROWS])
-            for b0 in range(s0, s1, P):
+            for b0 in range(0, GATE_ROWS * P, P):
                 bank0 = b0 // BANK * BANK
                 if bank0 not in gate_banks:
                     gate_banks[bank0] = psum.tile([P, BANK], F32, name="gate_bank_%d" % bank0, tag="bank")
@@ -203,7 +196,7 @@ def tile_moe_pre_mlp_relu_kernel(
                         out=a_banks[b0][:],
                         lhsT=x_operand[g, b0][0],
                         lhsT_scale=x_operand[g, b0][1],
-                        rhs=w1_codes[e, g].bitcast(FP4X4),
+                        rhs=w1_codes[e * PASSES + g].bitcast(FP4X4),
                         rhs_scale=w1_plane[:, e * PASSES + g, :],
                         start=(len(done) == 1),
                         stop=(len(done) == PASSES),
@@ -227,10 +220,10 @@ def tile_moe_pre_mlp_relu_kernel(
                     nc.tensor.transpose(turned[:, u, b0 - s0 : b0 - s0 + P], pairs[:, u * P : (u + 1) * P], identity[:])
             h_turned[s0] = turned
 
-        def group_h(engine, s0, s1, into=None, buffer=None):
+        def group_h(engine, s0, s1, into=None):
             t0, t1 = into or (s0, s1)
             if t0 not in h_grouped:
-                h_grouped[t0] = sbuf([P, (t1 - t0) * PACK], BF16, "h_grouped_%d" % t0, buffer)
+                h_grouped[t0] = sbuf([P, (t1 - t0) * PACK], BF16, "h_grouped_%d" % t0)
             grouped = h_grouped[t0][:, (s0 - t0) * PACK : (s1 - t0) * PACK]
             copy(engine, grouped.bitcast(F32).rearrange("p (s u) -> p s u", u=2), h_turned[s0][:].rearrange("p u s -> p s u"))
 
@@ -238,7 +231,8 @@ def tile_moe_pre_mlp_relu_kernel(
             h_codes = sbuf([P, s1 - s0], U32, "h_codes_%d" % s0)
             h_plane = sbuf([P, s1 - s0], U8, "h_plane_%d" % s0)
             vector.quantize_mx(out=h_codes[:].bitcast(FP8X4), scales=h_plane[:], in_=h_grouped[s0][:])
-            h_operand[s0] = (h_codes, h_plane)
+            for b0 in range(s0, s1, P):
+                h_operand[b0] = (h_codes[:, b0 - s0 :], h_plane[:, b0 - s0 :])
 
         def second_layer(b, *cuts):
             y_bank = psum.tile([P, cuts[-1] - cuts[0]], F32, name="y_bank_%d_%d" % (b, cuts[0]), tag="bank")
@@ -248,8 +242,8 @@ def tile_moe_pre_mlp_relu_kernel(
                     out=y_bank[:, s0 - cuts[0] : s1 - cuts[0]],
                     lhsT=w2_codes[:, e, 2 * b * P : 2 * (b + 1) * P].bitcast(FP4X4),
                     lhsT_scale=w2_plane[:, e, b * P : (b + 1) * P],
-                    rhs=h_operand[s0][0][:].bitcast(FP8X4),
-                    rhs_scale=h_operand[s0][1][:],
+                    rhs=h_operand[s0][0][:, 0 : s1 - s0].bitcast(FP8X4),
+                    rhs_scale=h_operand[s0][1][:, 0 : s1 - s0],
                     start=True,
                     stop=True,
                 )
@@ -263,129 +257,129 @@ def tile_moe_pre_mlp_relu_kernel(
             offsets = first_slots[:, t0 // LIST_COLUMN : t1 // LIST_COLUMN]
             scalar.activation(first_results[b, t0][:], y_half[b][:].indirect(offsets), COPY)
 
-        def add_second(b, t0, t1, total=None, base=None):
-            if total is None:
-                total, base = sbuf([P, T - t0], F32, "total_%d_%d" % (b, t0)), t0
+        def add_second(b, total, base, t0, t1):
             offsets = second_slots[:, t0 // LIST_COLUMN : t1 // LIST_COLUMN]
             vector.tensor_tensor(total[:, t0 - base : t1 - base], y_half[b][:].indirect(offsets), first_results[b, t0][:], ADD)
-            return total, base
 
-        def store(b, t1, total, base):
-            nc.sync.dma_start(out[b * P : (b + 1) * P, base:t1], total[:, 0 : t1 - base])
-
-        gather_x(vector, 0, 800, 1280, planes=[0], buffer="spread")
-        spread_gates(0, 1024)
-        gather_x(vector, 0, 800, 1280, planes=[1, 2, 3])
+        gather_x(vector, 0, FIRST_SPLIT, S, planes=[0], buffer="first_unit")
+        spread_gates()
+        gather_x(vector, 0, FIRST_SPLIT, S, planes=[1, 2, 3])
         for d in range(PACK):
-            gather_x(scalar, 0, 0, 512, planes=[d])
-            gather_x(scalar, 0, 512, 800, planes=[d], buffer="scalar_b")
-        open_grouped(None, (0, 768, 1024), (0, 1024, 1280))
-        group_all(gpsimd, 0, 800, 1280, 768)
-        gather_x(vector, 1, 0, 608, buffer="early")
-        gather_x(scalar, 1, 608, 1024)
-        open_grouped("first_block", (0, 0, 128))
-        group_x(gpsimd, 0, 0, 128)
-        open_grouped("last_of_gpsimd", (1, 0, 512))
-        group_x(gpsimd, 1, 0, 288)
-        open_grouped("spread", (1, 512, 768), (0, 128, 512), (0, 512, 768))
-        group_x(vector, 0, 128, 512, unit=0, spread=True)
-        group_x(vector, 1, 512, 608, unit=0, spread=True)
-        group_x(vector, 1, 288, 512, unit=0, part=0, spread=True)
-        gather_x(scalar, 2, 0, 512)
-        group_x(vector, 0, 512, 768, spread=True)
-        group_x(vector, 0, 768, 800, unit=512, spread=True)
-        group_x(vector, 1, 608, 768, part=512, spread=True)
-        gather_x(scalar, 2, 512, 1024, buffer="scalar_b")
-        early_planes = sbuf([P, 1792], U8, "early_planes", "early")
-        quantize_x(0, 0, 128, early_planes[:, 0:128])
-        quantize_x(0, 128, 512, early_planes[:, 128:512])
-        first_layer([0], 0, 512)
-        quantize_x(0, 512, 768, early_planes[:, 512:768])
-        quantize_x(0, 768, 1024, early_planes[:, 768:1024])
-        quantize_x(1, 0, 512, early_planes[:, 1024:1536])
-        first_layer([1], 0, 512)
-        first_layer([0], 512, 768)
-        open_grouped("last_of_gpsimd", (1, 768, 896))
-        group_x(gpsimd, 1, 768, 896, unit=608)
-        open_grouped("first_block", (2, 0, 512))
-        group_x(vector, 2, 0, 512, spread=True)
-        quantize_x(1, 512, 768, early_planes[:, 1536:1792])
-        quantize_x(2, 0, 512)
-        first_layer([2], 0, 512)
-        quantize_x(1, 768, 896)
-        open_grouped("last_of_gpsimd", (1, 896, 1024))
-        group_x(gpsimd, 1, 896, 1024, unit=608)
-        gather_x(vector, 2, 1024, 1152, buffer="spread")
-        group_x(gpsimd, 2, 1024, 1152)
-        relu_rows(scalar, 0, 128, buffer="first_rows")
-        relu_rows(scalar, 128, 256)
-        turn_h(0, 256)
-        first_layer([1], 512, 768)
-        first_layer([0, 1], 768, 896)
-        first_layer([0], 896, 1024)
-        relu_rows(scalar, 256, 512)
-        gather_x(scalar, 1, 1024, 1280, buffer="first_rows")
-        open_grouped("first_block", (2, 512, 1024))
-        group_x(vector, 2, 512, 1024, spread=True)
-        quantize_x(1, 896, 1024)
-        first_layer([1], 896, 1024)
-        quantize_x(2, 1024, 1152)
-        quantize_x(2, 512, 1024)
-        first_layer([2], 512, 1024)
-        gather_x(vector, 2, 1152, 1280, gated=True, buffer="scalar_b")
-        late_plane = sbuf([P, 256], U8, "late_plane", "first_block")
-        quantize_x(0, 1024, 1280, late_plane[:])
-        turn_h(256, 512)
-        first_layer([0, 2], 1024, 1152)
-        first_layer([0], 1152, 1280)
-        group_x(vector, 2, 1152, 1280)
-        group_x(vector, 1, 1024, 1280)
-        relu_rows(scalar, 512, 768)
-        quantize_x(2, 1152, 1280)
-        turn_h(512, 768)
-        first_layer([2], 1152, 1280)
-        relu_rows(scalar, 768, 1024)
-        quantize_x(1, 1024, 1280)
-        first_layer([1], 1152, 1280)
-        first_layer([1], 1024, 1152)
-        turn_h(768, 1024)
-        group_h(scalar, 0, 256)
-        group_h(scalar, 256, 512)
-        group_h(vector, 512, 768)
-        quantize_h(0, 256)
-        relu_rows(scalar, 1152, 1280)
-        relu_rows(vector, 1024, 1152)
-        turn_h(1152, 1280)
-        turn_h(1024, 1152)
-        group_h(scalar, 768, 1024)
-        quantize_h(256, 512)
-        second_layer(0, 0, 256, 512)
-        group_h(scalar, 1152, 1280, (1024, 1280))
-        group_h(scalar, 1024, 1152, (1024, 1280))
-        quantize_h(512, 768)
-        second_layer(1, 0, 256, 512)
-        quantize_h(768, 1024)
-        second_layer(0, 512, 768, 1024)
-        quantize_h(1024, 1280)
-        keep_y(scalar, 0, 0, 512)
-        second_layer(0, 1024, 1280)
-        second_layer(1, 512, 768, 1024)
-        second_layer(1, 1024, 1280)
-        keep_y(vector, 0, 512, 1024)
-        keep_y(scalar, 1, 0, 512)
-        keep_y(scalar, 0, 1024, 1280)
-        keep_y(vector, 1, 512, 1024)
-        keep_y(vector, 1, 1024, 1280)
+            gather_x(scalar, 0, 0, 4 * P, planes=[d])
+            gather_x(scalar, 0, 4 * P, FIRST_SPLIT, planes=[d], buffer="scalar_unit")
+        first_pass_rest = sbuf([P, S - 4 * P, PACK], BF16, "x_grouped_first_rest")
+        x_grouped[0, 4 * P] = first_pass_rest[:, 0 : 4 * P, :]
+        x_grouped[0, 8 * P] = first_pass_rest[:, 4 * P : 6 * P, :]
+        x_grouped[0, FIRST_SPLIT] = first_pass_rest[:, FIRST_SPLIT - 4 * P : 6 * P, :]
+        multiply_on_gpsimd(0, FIRST_SPLIT, S)
+        gather_x(vector, 1, 0, SECOND_SPLIT, buffer="second_unit")
+        gather_x(scalar, 1, SECOND_SPLIT, 8 * P)
+        open_grouped("wide_out", (0, 0, P))
+        multiply_on_gpsimd(0, 0, P)
+        open_grouped("pool_out", (1, 0, 4 * P))
+        multiply_on_gpsimd(1, 0, POOL_SPLIT)
+        open_grouped("first_unit", (1, 4 * P, 6 * P), (0, P, 4 * P))
+        multiply_on_vector(0, P, 4 * P, unit=0)
+        multiply_on_vector(1, 4 * P, SECOND_SPLIT, unit=0)
+        multiply_on_vector(1, POOL_SPLIT, 4 * P, unit=0, part=0)
+        gather_x(scalar, 2, 0, 4 * P)
+        multiply_on_vector(0, 4 * P, FIRST_SPLIT)
+        multiply_on_vector(1, SECOND_SPLIT, 6 * P, part=4 * P)
+        gather_x(scalar, 2, 4 * P, 8 * P, buffer="scalar_unit")
+        early_planes = sbuf([P, 14 * P], U8, "early_planes", "second_unit")
+        quantize_x(0, 0, P, early_planes[:, 0:P])
+        quantize_x(0, P, 4 * P, early_planes[:, P : 4 * P])
+        first_layer([0], 0, 4 * P)
+        quantize_x(0, 4 * P, 8 * P, early_planes[:, 4 * P : 8 * P])
+        quantize_x(1, 0, 4 * P, early_planes[:, 8 * P : 12 * P])
+        first_layer([1], 0, 4 * P)
+        first_layer([0], 4 * P, 6 * P)
 
-        pieces = ((0, 192), (192, 416), (416, 640))
-        for b in range(2):
+        open_grouped("pool_out", (1, 6 * P, 7 * P))
+        multiply_on_gpsimd(1, 6 * P, 7 * P, unit=SECOND_SPLIT)
+        open_grouped("wide_out", (2, 0, 4 * P))
+        multiply_on_vector(2, 0, 4 * P)
+        quantize_x(1, 4 * P, 6 * P, early_planes[:, 12 * P : 14 * P])
+        quantize_x(2, 0, 4 * P)
+        first_layer([2], 0, 4 * P)
+        quantize_x(1, 6 * P, 7 * P)
+
+        open_grouped("pool_out", (1, 7 * P, 8 * P))
+        multiply_on_gpsimd(1, 7 * P, 8 * P, unit=SECOND_SPLIT)
+        gather_x(vector, 2, 8 * P, 9 * P, buffer="first_unit")
+        multiply_on_gpsimd(2, 8 * P, 9 * P)
+        relu_rows(scalar, 0, P, buffer="first_rows")
+        relu_rows(scalar, P, 2 * P)
+        turn_h(0, 2 * P)
+        first_layer([1], 4 * P, 6 * P)
+        first_layer([0, 1], 6 * P, 7 * P)
+        first_layer([0], 7 * P, 8 * P)
+        relu_rows(scalar, 2 * P, 4 * P)
+        gather_x(scalar, 1, 8 * P, S, buffer="first_rows")
+        open_grouped("wide_out", (2, 4 * P, 8 * P))
+        multiply_on_vector(2, 4 * P, 8 * P)
+        quantize_x(1, 7 * P, 8 * P)
+        first_layer([1], 7 * P, 8 * P)
+        quantize_x(2, 8 * P, 9 * P)
+        quantize_x(2, 4 * P, 8 * P)
+        first_layer([2], 4 * P, 8 * P)
+
+        gather_x(vector, 2, 9 * P, S, gated=True, buffer="scalar_unit")
+        late_plane = sbuf([P, C], U8, "late_plane", "wide_out")
+        quantize_x(0, 8 * P, S, late_plane[:])
+        turn_h(2 * P, 4 * P)
+        first_layer([0, 2], 8 * P, 9 * P)
+        first_layer([0], 9 * P, S)
+        round_gated(2, 9 * P, S)
+        multiply_on_vector(1, 8 * P, S)
+        relu_rows(scalar, 4 * P, 6 * P)
+        quantize_x(2, 9 * P, S)
+        turn_h(4 * P, 6 * P)
+        first_layer([2], 9 * P, S)
+        relu_rows(scalar, 6 * P, 8 * P)
+        quantize_x(1, 8 * P, S)
+        first_layer([1], 9 * P, S)
+        first_layer([1], 8 * P, 9 * P)
+        turn_h(6 * P, 8 * P)
+
+        group_h(scalar, 0, C)
+        group_h(scalar, C, 2 * C)
+        group_h(vector, 2 * C, 3 * C)
+        quantize_h(0, C)
+        relu_rows(scalar, 9 * P, S)
+        relu_rows(vector, 8 * P, 9 * P)
+        turn_h(9 * P, S)
+        turn_h(8 * P, 9 * P)
+        group_h(scalar, 3 * C, 4 * C)
+        quantize_h(C, 2 * C)
+        second_layer(0, 0, C, 2 * C)
+        group_h(scalar, 9 * P, S, (4 * C, S))
+        group_h(scalar, 8 * P, 9 * P, (4 * C, S))
+        quantize_h(2 * C, 3 * C)
+        second_layer(1, 0, C, 2 * C)
+        quantize_h(3 * C, 4 * C)
+        second_layer(0, 2 * C, 3 * C, 4 * C)
+        quantize_h(4 * C, S)
+        keep_y(scalar, 0, 0, 2 * C)
+        second_layer(0, 8 * P, 9 * P)
+        second_layer(0, 9 * P, S)
+        second_layer(1, 2 * C, 3 * C, 4 * C)
+        second_layer(1, 4 * C, S)
+        keep_y(vector, 0, 2 * C, 4 * C)
+        keep_y(scalar, 1, 0, 2 * C)
+        keep_y(vector, 0, 8 * P, 9 * P)
+        keep_y(scalar, 0, 9 * P, S)
+        keep_y(vector, 1, 2 * C, 4 * C)
+        keep_y(vector, 1, 4 * C, S)
+
+        pieces = list(zip(RESULT_CUTS, RESULT_CUTS[1:]))
+        for b in range(N // P):
             for t0, t1 in pieces:
                 fetch_first(b, t0, t1)
-        total = add_second(0, *pieces[0])
-        add_second(0, *pieces[1], *total)
-        add_second(0, *pieces[2], *total)
-        store(0, 640, *total)
-        total = add_second(1, *pieces[0])
-        add_second(1, *pieces[1], *total)
-        store(1, 416, *total)
-        store(1, 640, *add_second(1, *pieces[2]))
+        last = len(pieces) - 1
+        for b, first, end in ((0, 0, last + 1), (1, 0, last), (1, last, last + 1)):
+            base, stop = pieces[first][0], pieces[end - 1][1]
+            total = sbuf([P, T - base], F32, "total_%d_%d" % (b, base))
+            for t0, t1 in pieces[first:end]:
+                add_second(b, total, base, t0, t1)
+            nc.sync.dma_start(out[b * P : (b + 1) * P, base:stop], total[:, 0 : stop - base])

from contextlib import ExitStack

import concourse.mybir as mybir
from concourse.masks import make_identity

K, T, E, C, H, N = 1536, 640, 5, 256, 512, 256
S = E * C
P = 128
PACK = 4
PASSES = K // (P * PACK)
LIST_COLUMN = 16
QUADRANT = 32
PSUM_BANKS = 8
BANK = 512
GATE_ROWS = 8
WALK = 4

FIRST_SPLIT = 800
SECOND_SPLIT = 608
POOL_SPLIT = 288
RESULT_CUTS = (0, 192, 416, T)

FLOPS = 2 * S * (K * H + H * N)
BYTES = 4 * K * T + E * (K * H + H * N) // 2 + E * (K * H + H * N) // 32 + 4 * S + 2 * P * (S + 2 * T) // 16 + 4 * N * T

F32 = mybir.dt.float32
BF16 = mybir.dt.bfloat16
I32 = mybir.dt.int32
U32 = mybir.dt.uint32
U16 = mybir.dt.uint16
U8 = mybir.dt.uint8
FP8X4 = mybir.dt.float8_e4m3fn_x4
FP4X4 = mybir.dt.float4_e2m1fn_x4
MULT = mybir.AluOpType.mult
ADD = mybir.AluOpType.add
COPY = mybir.ActivationFunctionType.Copy
RELU = mybir.ActivationFunctionType.Relu


def tile_moe_pre_mlp_relu_kernel(
    tc, xT, w1_words, w1_scales, w2_words, w2_scales, gate, offs, pos1, pos2, out
):
    nc = tc.nc
    vector, scalar, gpsimd = nc.vector, nc.scalar, nc.gpsimd
    with ExitStack() as ctx:
        keep = ctx.enter_context(tc.tile_pool(name="keep", bufs=1))
        psum = ctx.enter_context(tc.psum_pool(name="psum", bufs=PSUM_BANKS))

        def sbuf(shape, dtype, name, buffer=None):
            return keep.tile(shape, dtype, name=name, tag=buffer or name, align_bytes=64)

        def copy(engine, dst, src):
            if engine is vector:
                vector.tensor_copy(dst, src)
            else:
                scalar.copy(dst, src)

        slot_tokens = keep.tile([P, S // LIST_COLUMN], U16, name="slot_tokens")
        first_slots = keep.tile([P, T // LIST_COLUMN], U16, name="first_slots")
        second_slots = keep.tile([P, T // LIST_COLUMN], U16, name="second_slots")
        tokens = [[sbuf([P, T], F32, "tokens_%d_%d" % (g, d)) for d in range(PACK)] for g in range(PASSES)]
        gates = sbuf([P, S], F32, "gates")
        gate_rows = sbuf([P, P], F32, "gate_rows")
        w1_codes = {}
        w1_plane = sbuf([P, E * PASSES, H], U8, "w1_plane")
        w2_codes = sbuf([P, E, 2 * N], U8, "w2_codes")
        w2_plane = sbuf([P, E, N], U8, "w2_plane")
        identity = sbuf([P, P], F32, "identity")
        y_half = [sbuf([P, S], F32, "y_half_%d" % b) for b in range(N // P)]

        warm = keep.tile([P, 16], F32, name="warm")
        vector.memset(warm[:, 0:8], 0.0)
        scalar.activation(warm[:, 8:16], warm[:, 0:8], COPY)

        vector.memset(gate_rows[:], 0.0)
        vector.memset(w1_plane[:].rearrange("p a b -> p (a b)").bitcast(I32), 0)
        vector.memset(w2_plane[:].rearrange("p a b -> p (a b)").bitcast(I32), 0)
        make_identity(nc, identity[:])

        x_rows = xT.rearrange("(g p d) t -> g d p t", p=P, d=PACK)

        def load_tokens(*rows):
            for row in rows:
                g, d = divmod(row, PACK)
                nc.sync.dma_start(tokens[g][d][:], x_rows[g, d])

        def load_gates(s0, s1):
            nc.sync.dma_start(gates[:, s0:s1], gate[0:P, s0:s1])

        def load_scales(plane, scales):
            scale_rows = scales.rearrange("e s q i -> q (e s) i").bitcast(I32)
            for quad in range(P // QUADRANT):
                nc.sync.dma_start(plane[QUADRANT * quad : QUADRANT * quad + 4].bitcast(I32), scale_rows[4 * quad : 4 * quad + 4])

        def load_w1(e0, e1):
            load_scales(w1_plane[:, e0 * PASSES : e1 * PASSES, :], w1_scales[e0:e1])
            words = sbuf([P, (e1 - e0) * PASSES, 2 * H], U8, "w1_codes_%d" % e0)
            nc.sync.dma_start(words[:].bitcast(I32), w1_words[e0:e1].rearrange("e s p b -> p (e s) b").bitcast(I32))
            for row in range((e1 - e0) * PASSES):
                w1_codes[e0 * PASSES + row] = words[:, row, :]

        load_tokens(0)
        nc.sync.dma_start(slot_tokens[:], offs)
        nc.sync.dma_start(gate_rows[0:GATE_ROWS, :], gate[0, 0 : GATE_ROWS * P].rearrange("(b m) -> b m", m=P))
        load_tokens(1, 2, 3, 4)
        load_gates(6 * P, S)
        load_tokens(5, 6, 7)
        load_gates(0, POOL_SPLIT)
        load_tokens(8, 9, 10, 11)
        load_w1(0, 2)
        load_w1(2, 4)
        load_w1(4, 5)
        load_scales(w2_plane, w2_scales)
        nc.sync.dma_start(w2_codes[:].bitcast(I32), w2_words.rearrange("e s p b -> p (e s) b").bitcast(I32))
        nc.sync.dma_start(first_slots[:], pos1)
        nc.sync.dma_start(second_slots[:], pos2)

        x_gathered, x_grouped, x_operand, a_banks, a_passes = {}, {}, {}, {}, {}
        h_rows, h_turned, h_grouped, h_operand = {}, {}, {}, {}
        y_banks, first_results, gate_banks = {}, {}, {}

        def gather_x(engine, g, s0, s1, planes=range(PACK), gated=False, buffer=None):
            if (g, s0) not in x_gathered:
                x_gathered[g, s0] = sbuf([P, PACK, s1 - s0], F32, "gathered_%d_%d" % (g, s0), buffer)
            for d in planes:
                window = tokens[g][d][:].indirect(slot_tokens[:, s0 // LIST_COLUMN : s1 // LIST_COLUMN])
                plane = x_gathered[g, s0][:, d, :]
                if gated:
                    vector.tensor_tensor(plane, window, gates[:, s0:s1], MULT)
                elif engine is vector:
                    vector.tensor_copy(plane, window)
                else:
                    scalar.activation(plane, window, COPY)

        def open_grouped(buffer, *parts):
            name = "x_grouped_%d_%d" % parts[0][0:2]
            tile = sbuf([P, sum(s1 - s0 for g, s0, s1 in parts), PACK], BF16, name, buffer)
            c0 = 0
            for g, s0, s1 in parts:
                x_grouped[g, s0] = tile[:, c0 : c0 + s1 - s0, :]
                c0 = c0 + s1 - s0

        def operands(g, s0, s1, unit, part):
            unit = s0 if unit is None else unit
            part = s0 if part is None else part
            if (g, part) not in x_grouped:
                open_grouped(None, (g, s0, s1))
            return x_grouped[g, part][:, s0 - part : s1 - part, :], x_gathered[g, unit][:, :, s0 - unit : s1 - unit]

        def multiply_on_gpsimd(g, s0, s1, unit=None, part=None):
            grouped, planes = operands(g, s0, s1, unit, part)
            weights = gates[:, s0:s1].rearrange("p (s o) -> p s o", o=1).to_broadcast([P, s1 - s0, PACK])
            gpsimd.tensor_tensor(grouped, planes.rearrange("p d s -> p s d"), weights, MULT)

        def multiply_on_vector(g, s0, s1, unit=None, part=None):
            grouped, planes = operands(g, s0, s1, unit, part)
            bank0 = s0 // BANK * BANK
            source = gate_banks[bank0][:, s0 - bank0 : s1 - bank0] if bank0 in gate_banks else gates[:, s0:s1]
            weights = source.rearrange("p (c o i) -> p c o i", o=1, i=WALK).to_broadcast([P, (s1 - s0) // WALK, PACK, WALK])
            grouped = grouped.rearrange("p (c i) d -> p c d i", i=WALK)
            vector.tensor_tensor(grouped, planes.rearrange("p d (c i) -> p c d i", i=WALK), weights, MULT)

        def round_gated(g, s0, s1):
            grouped, planes = operands(g, s0, s1, None, None)
            vector.tensor_copy(grouped.rearrange("p (c i) d -> p c d i", i=WALK), planes.rearrange("p d (c i) -> p c d i", i=WALK))

        def spread_gates():
            turned = psum.tile([P, P], F32, name="gate_turned", tag="bank")
            nc.tensor.transpose(turned[:], gate_rows[:], identity[:])
            columns = sbuf([P, GATE_ROWS], F32, "gate_columns")
            vector.tensor_copy(columns[:], turned[:, 0:GATE_ROWS])
            for b0 in range(0, GATE_ROWS * P, P):
                bank0 = b0 // BANK * BANK
                if bank0 not in gate_banks:
                    gate_banks[bank0] = psum.tile([P, BANK], F32, name="gate_bank_%d" % bank0, tag="bank")
                column = columns[:, b0 // P : b0 // P + 1].to_broadcast([P, P])
                nc.tensor.transpose(gate_banks[bank0][:, b0 - bank0 : b0 - bank0 + P], column, identity[:])

        def quantize_x(g, s0, s1, x_plane=None):
            x_codes = sbuf([P, s1 - s0], U32, "x_codes_%d_%d" % (g, s0))
            if x_plane is None:
                x_plane = sbuf([P, s1 - s0], U8, "x_plane_%d_%d" % (g, s0))[:]
            vector.quantize_mx(out=x_codes[:].bitcast(FP8X4), scales=x_plane, in_=x_grouped[g, s0].rearrange("p c d -> p (c d)"))
            for b0 in range(s0, s1, P):
                x_operand[g, b0] = (x_codes[:, b0 - s0 : b0 - s0 + P].bitcast(FP8X4), x_plane[:, b0 - s0 : b0 - s0 + P])

        def first_layer(passes, s0, s1):
            for b0 in range(s0, s1, P):
                e = b0 // C
                for g in passes:
                    done = a_passes.setdefault(b0, [])
                    done.append(g)
                    if len(done) == 1:
                        a_banks[b0] = psum.tile([P, H], F32, name="a_bank_%d" % b0, tag="bank")
                    nc.tensor.matmul_mx(
                        out=a_banks[b0][:],
                        lhsT=x_operand[g, b0][0],
                        lhsT_scale=x_operand[g, b0][1],
                        rhs=w1_codes[e * PASSES + g].bitcast(FP4X4),
                        rhs_scale=w1_plane[:, e * PASSES + g, :],
                        start=(len(done) == 1),
                        stop=(len(done) == PASSES),
                    )

        def relu_rows(engine, s0, s1, buffer=None):
            for b0 in range(s0, s1, P):
                h_rows[b0] = sbuf([P, H], BF16, "h_rows_%d" % b0, buffer)
                dst = h_rows[b0][:].rearrange("s (u p v) -> s u p v", u=2, v=2)
                src = a_banks[b0][:].rearrange("s (p u v) -> s u p v", u=2, v=2)
                if engine is vector:
                    vector.tensor_scalar_max(dst, src, 0.0)
                else:
                    scalar.activation(dst, src, RELU)

        def turn_h(s0, s1):
            turned = psum.tile([P, 2, s1 - s0], F32, name="turned_%d" % s0, tag="bank")
            for b0 in range(s0, s1, P):
                pairs = h_rows[b0][:].bitcast(F32)
                for u in range(2):
                    nc.tensor.transpose(turned[:, u, b0 - s0 : b0 - s0 + P], pairs[:, u * P : (u + 1) * P], identity[:])
            h_turned[s0] = turned

        def group_h(engine, s0, s1, into=None):
            t0, t1 = into or (s0, s1)
            if t0 not in h_grouped:
                h_grouped[t0] = sbuf([P, (t1 - t0) * PACK], BF16, "h_grouped_%d" % t0)
            grouped = h_grouped[t0][:, (s0 - t0) * PACK : (s1 - t0) * PACK]
            copy(engine, grouped.bitcast(F32).rearrange("p (s u) -> p s u", u=2), h_turned[s0][:].rearrange("p u s -> p s u"))

        def quantize_h(s0, s1):
            h_codes = sbuf([P, s1 - s0], U32, "h_codes_%d" % s0)
            h_plane = sbuf([P, s1 - s0], U8, "h_plane_%d" % s0)
            vector.quantize_mx(out=h_codes[:].bitcast(FP8X4), scales=h_plane[:], in_=h_grouped[s0][:])
            for b0 in range(s0, s1, P):
                h_operand[b0] = (h_codes[:, b0 - s0 :], h_plane[:, b0 - s0 :])

        def second_layer(b, *cuts):
            y_bank = psum.tile([P, cuts[-1] - cuts[0]], F32, name="y_bank_%d_%d" % (b, cuts[0]), tag="bank")
            for s0, s1 in zip(cuts, cuts[1:]):
                e = s0 // C
                nc.tensor.matmul_mx(
                    out=y_bank[:, s0 - cuts[0] : s1 - cuts[0]],
                    lhsT=w2_codes[:, e, 2 * b * P : 2 * (b + 1) * P].bitcast(FP4X4),
                    lhsT_scale=w2_plane[:, e, b * P : (b + 1) * P],
                    rhs=h_operand[s0][0][:, 0 : s1 - s0].bitcast(FP8X4),
                    rhs_scale=h_operand[s0][1][:, 0 : s1 - s0],
                    start=True,
                    stop=True,
                )
            y_banks[b, cuts[0]] = y_bank

        def keep_y(engine, b, s0, s1):
            copy(engine, y_half[b][:, s0:s1], y_banks[b, s0][:])

        def fetch_first(b, t0, t1):
            first_results[b, t0] = sbuf([P, t1 - t0], F32, "first_result_%d_%d" % (b, t0))
            offsets = first_slots[:, t0 // LIST_COLUMN : t1 // LIST_COLUMN]
            scalar.activation(first_results[b, t0][:], y_half[b][:].indirect(offsets), COPY)

        def add_second(b, total, base, t0, t1):
            offsets = second_slots[:, t0 // LIST_COLUMN : t1 // LIST_COLUMN]
            vector.tensor_tensor(total[:, t0 - base : t1 - base], y_half[b][:].indirect(offsets), first_results[b, t0][:], ADD)

        gather_x(vector, 0, FIRST_SPLIT, S, planes=[0], buffer="first_unit")
        spread_gates()
        gather_x(vector, 0, FIRST_SPLIT, S, planes=[1, 2, 3])
        for d in range(PACK):
            gather_x(scalar, 0, 0, 4 * P, planes=[d])
            gather_x(scalar, 0, 4 * P, FIRST_SPLIT, planes=[d], buffer="scalar_unit")
        first_pass_rest = sbuf([P, S - 4 * P, PACK], BF16, "x_grouped_first_rest")
        x_grouped[0, 4 * P] = first_pass_rest[:, 0 : 4 * P, :]
        x_grouped[0, 8 * P] = first_pass_rest[:, 4 * P : 6 * P, :]
        x_grouped[0, FIRST_SPLIT] = first_pass_rest[:, FIRST_SPLIT - 4 * P : 6 * P, :]
        multiply_on_gpsimd(0, FIRST_SPLIT, S)
        gather_x(vector, 1, 0, SECOND_SPLIT, buffer="second_unit")
        gather_x(scalar, 1, SECOND_SPLIT, 8 * P)
        open_grouped("wide_out", (0, 0, P))
        multiply_on_gpsimd(0, 0, P)
        open_grouped("pool_out", (1, 0, 4 * P))
        multiply_on_gpsimd(1, 0, POOL_SPLIT)
        open_grouped("first_unit", (1, 4 * P, 6 * P), (0, P, 4 * P))
        multiply_on_vector(0, P, 4 * P, unit=0)
        multiply_on_vector(1, 4 * P, SECOND_SPLIT, unit=0)
        multiply_on_vector(1, POOL_SPLIT, 4 * P, unit=0, part=0)
        gather_x(scalar, 2, 0, 4 * P)
        multiply_on_vector(0, 4 * P, FIRST_SPLIT)
        multiply_on_vector(1, SECOND_SPLIT, 6 * P, part=4 * P)
        gather_x(scalar, 2, 4 * P, 8 * P, buffer="scalar_unit")
        early_planes = sbuf([P, 14 * P], U8, "early_planes", "second_unit")
        quantize_x(0, 0, P, early_planes[:, 0:P])
        quantize_x(0, P, 4 * P, early_planes[:, P : 4 * P])
        first_layer([0], 0, 4 * P)
        quantize_x(0, 4 * P, 8 * P, early_planes[:, 4 * P : 8 * P])
        quantize_x(1, 0, 4 * P, early_planes[:, 8 * P : 12 * P])
        first_layer([1], 0, 4 * P)
        first_layer([0], 4 * P, 6 * P)

        open_grouped("pool_out", (1, 6 * P, 7 * P))
        multiply_on_gpsimd(1, 6 * P, 7 * P, unit=SECOND_SPLIT)
        open_grouped("wide_out", (2, 0, 4 * P))
        multiply_on_vector(2, 0, 4 * P)
        quantize_x(1, 4 * P, 6 * P, early_planes[:, 12 * P : 14 * P])
        quantize_x(2, 0, 4 * P)
        first_layer([2], 0, 4 * P)
        quantize_x(1, 6 * P, 7 * P)

        open_grouped("pool_out", (1, 7 * P, 8 * P))
        multiply_on_gpsimd(1, 7 * P, 8 * P, unit=SECOND_SPLIT)
        gather_x(vector, 2, 8 * P, 9 * P, buffer="first_unit")
        multiply_on_gpsimd(2, 8 * P, 9 * P)
        relu_rows(scalar, 0, P, buffer="first_rows")
        relu_rows(scalar, P, 2 * P)
        turn_h(0, 2 * P)
        first_layer([1], 4 * P, 6 * P)
        first_layer([0, 1], 6 * P, 7 * P)
        first_layer([0], 7 * P, 8 * P)
        relu_rows(scalar, 2 * P, 4 * P)
        gather_x(scalar, 1, 8 * P, S, buffer="first_rows")
        open_grouped("wide_out", (2, 4 * P, 8 * P))
        multiply_on_vector(2, 4 * P, 8 * P)
        quantize_x(1, 7 * P, 8 * P)
        first_layer([1], 7 * P, 8 * P)
        quantize_x(2, 8 * P, 9 * P)
        quantize_x(2, 4 * P, 8 * P)
        first_layer([2], 4 * P, 8 * P)

        gather_x(vector, 2, 9 * P, S, gated=True, buffer="scalar_unit")
        late_plane = sbuf([P, C], U8, "late_plane", "wide_out")
        quantize_x(0, 8 * P, S, late_plane[:])
        turn_h(2 * P, 4 * P)
        first_layer([0, 2], 8 * P, 9 * P)
        first_layer([0], 9 * P, S)
        round_gated(2, 9 * P, S)
        multiply_on_vector(1, 8 * P, S)
        relu_rows(scalar, 4 * P, 6 * P)
        quantize_x(2, 9 * P, S)
        turn_h(4 * P, 6 * P)
        first_layer([2], 9 * P, S)
        relu_rows(scalar, 6 * P, 8 * P)
        quantize_x(1, 8 * P, S)
        first_layer([1], 9 * P, S)
        first_layer([1], 8 * P, 9 * P)
        turn_h(6 * P, 8 * P)

        group_h(scalar, 0, C)
        group_h(scalar, C, 2 * C)
        group_h(vector, 2 * C, 3 * C)
        quantize_h(0, C)
        relu_rows(scalar, 9 * P, S)
        relu_rows(vector, 8 * P, 9 * P)
        turn_h(9 * P, S)
        turn_h(8 * P, 9 * P)
        group_h(scalar, 3 * C, 4 * C)
        quantize_h(C, 2 * C)
        second_layer(0, 0, C, 2 * C)
        group_h(scalar, 9 * P, S, (4 * C, S))
        group_h(scalar, 8 * P, 9 * P, (4 * C, S))
        quantize_h(2 * C, 3 * C)
        second_layer(1, 0, C, 2 * C)
        quantize_h(3 * C, 4 * C)
        second_layer(0, 2 * C, 3 * C, 4 * C)
        quantize_h(4 * C, S)
        keep_y(scalar, 0, 0, 2 * C)
        second_layer(0, 8 * P, 9 * P)
        second_layer(0, 9 * P, S)
        second_layer(1, 2 * C, 3 * C, 4 * C)
        second_layer(1, 4 * C, S)
        keep_y(vector, 0, 2 * C, 4 * C)
        keep_y(scalar, 1, 0, 2 * C)
        keep_y(vector, 0, 8 * P, 9 * P)
        keep_y(scalar, 0, 9 * P, S)
        keep_y(vector, 1, 2 * C, 4 * C)
        keep_y(vector, 1, 4 * C, S)

        pieces = list(zip(RESULT_CUTS, RESULT_CUTS[1:]))
        for b in range(N // P):
            for t0, t1 in pieces:
                fetch_first(b, t0, t1)
        last = len(pieces) - 1
        for b, first, end in ((0, 0, last + 1), (1, 0, last), (1, last, last + 1)):
            base, stop = pieces[first][0], pieces[end - 1][1]
            total = sbuf([P, T - base], F32, "total_%d_%d" % (b, base))
            for t0, t1 in pieces[first:end]:
                add_second(b, total, base, t0, t1)
            nc.sync.dma_start(out[b * P : (b + 1) * P, base:stop], total[:, 0 : stop - base])
